import numpy as np, ml_dtypes
CORES = [8,9,10,11,12,13]
N = 6
BF = ml_dtypes.bfloat16
def gentries(a):
    return np.ascontiguousarray(a.reshape(8, 16, -1).transpose(0, 2, 1)).reshape(8, -1)
def gtable(e):
    e = np.asarray(e); return np.ascontiguousarray(e.reshape(8, -1, 16).transpose(0, 2, 1)).reshape(128, -1).astype(np.int32)
VA, G, OB, W, CAP, S = 1024, 512, 2560, 4096, 256, 272
E0, M, RO = 3, 13, 5
WA, NIL = VA + G, W - 1
H = NIL - OB
KC = 6
def within(rng, ke, k):
    o = np.argsort(ke, kind="stable"); cnt = np.bincount(ke, minlength=KC); lo = np.add.accumulate(cnt) - cnt
    i = lo[k] + (rng.random(k.shape) * np.maximum(cnt[k], 1)).astype(np.int64)
    return o[np.minimum(i, ke.size - 1)]
def feat(rng, cen, k, a):
    v = np.swapaxes(cen[np.arange(8)[None, :, None], k], 2, 3)
    return v + rng.integers(-a, a + 1, v.shape)
def parts(rng, bd=None):
    if bd is None: bd = np.argsort(rng.random((N, 8, VA)), axis=-1)[..., :G]
    cen = rng.integers(-90, 91, (8, KC, 16)); ka = rng.integers(0, KC, (N, 8, VA)); kb = rng.integers(0, KC, (N, 8, OB))
    kx = np.concatenate([ka, np.take_along_axis(np.roll(ka, 1, axis=0), np.roll(bd, 1, axis=0), 2)], axis=2)
    eo = np.argsort(kx[:, :, None, :] + 1.5 * rng.random((N, 8, 16, WA)), axis=-1); ao = np.argsort(ka[:, :, None, :] + 1.5 * rng.random((N, 8, 16, VA)), axis=-1)
    nba = np.empty((N, 8, 16, VA), np.int64); np.put_along_axis(nba, ao, eo[..., np.arange(VA) * WA // VA], -1)
    ky = np.concatenate([kb, np.roll(kb, -1, axis=0)[..., :H]], axis=2); nbb = np.empty((N, 8, 16, OB), np.int64); f0 = np.empty((N, 8, 16, S), np.int64)
    dens = rng.choice(np.array([0.3, 0.5, 0.8]), (N, 8))
    for r in range(N):
        for g in range(8):
            k = np.where(rng.random((16, OB)) < 0.75, kb[r, g], rng.integers(0, KC, (16, OB)))
            nbb[r, g] = np.where(rng.random((16, OB)) < 0.04, NIL, within(rng, ky[r, g], k))
            keep = (rng.random((16, S)) < dens[r, g]) & (rng.random((1, S)) > 0.1)
            f0[r, g] = np.where(keep, within(rng, ky[r, g], np.broadcast_to(ka[r, g, :S], (16, S))), NIL)
    return dict(cen=cen, ka=ka, kb=kb, bd=bd, nba=nba, nbb=nbb, f0=f0, xa=feat(rng, cen, ka, 3), xb=feat(rng, cen, kb, 3))
def pack(d):
    t = lambda v, w: np.ascontiguousarray(np.reshape(v, (N, 128, w)))
    return {"xa": t(d["xa"], VA).astype(np.float32).astype(BF), "xb": t(d["xb"], OB).astype(np.float32).astype(BF), "nba": t(d["nba"], VA).astype(np.int32),
            "nbb": t(d["nbb"], OB).astype(np.int32), "f0": t(d["f0"], S).astype(np.int32), "bd": np.stack([gtable(a) for a in d["bd"]])}
def put(row, c, v):
    o = np.setdiff1d(np.arange(row.size), c); hit = o[np.isin(row[o], v)]
    row[hit] = np.setdiff1d(row[c], v)[:hit.size]; row[c] = v
def short(rng, d, r, g):
    z1, z2, x = S, S + 1, VA - 1; P = np.array([S // 4, S // 2, 3 * S // 4, VA - 4, VA - 3, VA - 2])
    T = rng.permutation(np.setdiff1d(np.arange(S), P[:3])); D1, D2 = int(T[0]), int(T[1]); T = T[2:]
    f = d["f0"][r, g]; f[:] = rng.integers(0, NIL, f.shape); f[:, P[:3]] = NIL; f[:15, D1] = NIL; f[:15, D2] = NIL
    m = np.concatenate([P[:3], np.arange(S + 2, VA)])
    for p in range(16):
        c, v = [z1, z2], [D1, D2]
        if p == 0: c, v = [z1, z2, x], [x, z1, int(T[0])]
        elif p == 1: v = [z2, D2]
        elif p == 2: c, v = [z1, z2, x], [D1, D2, z1]
        elif p < 9: c, v = [z1, z2, int(P[p - 3])], [D1, D2, z2]
        elif p < 15:
            i = m[(p - 9) * T.size:(p - 8) * T.size]; c, v = np.concatenate([c, i]), np.concatenate([v, T[:i.size]])
        else: v = [z1, z2]
        put(d["nba"][r, g, p], np.array(c, np.int64), np.array(v, np.int64))
def lone(rng, d, r, g, z0, L):
    c, u, w = OB - 1, VA - 1, S
    f = d["f0"][r, g]; nb = d["nba"][r, g]; v = rng.integers(0, NIL - 1, S)
    f[:] = NIL; f[rng.integers(0, 16, S), np.arange(S)] = v + (v >= c); f[:, 64 + rng.permutation(S - 64)[:z0]] = NIL
    f[:, 0] = NIL; f[0, 0] = NIL - 1; f[1:3, 1] = c
    cells = [0, u, w] if L == 0 else [u, u - 1] + [S + i for i in range(L)]
    d["xa"][r, g][:, cells] = 40; d["xb"][r, g][:, c] = 40; d["nbb"][r, g][:, c] = c
    for p in range(16):
        if L == 0:
            to = {u: p}
            if p == 1: to[w] = u
            if p == 2: to[0] = 1
            if p == 3: to[0] = w
        else:
            to = {u: 1 if p == 1 else S, u - 1: S if p == 1 else (1 if p == 2 else p)}
            for i in range(1, L + 1): to[S + i - 1] = u if p == 4 + i else (S + i if p == 3 and i < L else 16 * i + p)
        k = sorted(to); put(nb[p], np.array(k, np.int64), np.array([to[i] for i in k], np.int64))
def quiet(rng, d, r):
    for g in range(8):
        o = rng.permutation(min(S, CAP)); x, y = int(o[0]), int(o[1]); z = int(rng.integers(2 * CAP + 1, VA)); c = int(rng.integers(0, OB))
        d["f0"][r, g] = NIL; d["f0"][r, g][:, y] = c
        for p in range(16):
            d["nba"][r, g, p] = rng.permutation(VA)
            if p == 0: k, v = [x, y], [y, x]
            else: k, v = [x, z, y], [x, y, z]
            put(d["nba"][r, g, p], np.array(k, np.int64), np.array(v, np.int64))
        b = d["xb"][r, g][:, c]; d["xa"][r, g][:, x] = b + (E0 if g < 7 else E0 + 1); d["xa"][r, g][:, z] = b - (E0 + 1)
def setup_inputs(rng):
    return pack(parts(rng))
def setup_inputs_room(rng):
    d = parts(rng); d["xa"] = feat(rng, d["cen"], d["ka"], 1); d["xb"] = feat(rng, d["cen"], d["kb"], 1); z0 = (S - VA) % CAP
    d["xa"][:, ::2, M - 1:] = 127; d["xb"][:, ::2, M - 1:] = -127; d["xa"][:, 1::2, M:] = 127; d["xb"][:, 1::2, M:] = -127
    d["xa"][:, 1::4, :M] = rng.integers(-1, 2, (N, 2, M, VA)); d["xb"][:, 1::4, :M] = rng.integers(-1, 2, (N, 2, M, OB))
    for r in range(N):
        for g in (0, 4):
            z = z0 + (0, 1, -1)[(r + g // 2) % 3]; o = rng.permutation(S)
            d["f0"][r, g][:, o[:z]] = NIL; d["f0"][r, g, rng.integers(0, 16, S - z), o[z:]] = rng.integers(0, NIL, S - z)
        lone(rng, d, r, 2, z0, 0); lone(rng, d, r, 6, z0, RO - (VA - S + z0) // CAP)
        for g in (1, 5): short(rng, d, r, g)
    return pack(d)
def setup_inputs_ties(rng):
    d = parts(rng); d["xb"] = feat(rng, d["cen"], d["kb"], 0); v = feat(rng, d["cen"], d["ka"], 0)
    d["xa"] = v + rng.choice(np.array([0, E0, E0 + 1, E0 + 2]), v.shape, p=[0.3, 0.55, 0.12, 0.03]) * rng.choice(np.array([-1, 1]), v.shape)
    d["f0"][:, ::2] = d["f0"][:, ::2, :1].copy(); d["nbb"][:, 1::2] = d["nbb"][:, 1::2, 5:6].copy(); d["nbb"][:, 0, 15] = np.arange(OB)
    quiet(rng, d, 0)
    return pack(d)
def setup_inputs_ends(rng):
    o = 1 + np.argsort(rng.random((N, 8, VA - 2)), axis=-1)[..., :G - 2]; z = np.zeros((N, 8, 1), np.int64)
    d = parts(rng, np.concatenate([z, o, z + VA - 1], axis=2)); ends = np.array([0, H - 1, H, OB - 1, OB, W - 2, NIL])
    d["cen"][::2] = d["cen"][::2, :1].copy(); d["cen"][4] = 125; d["cen"][6] = -125
    d["xa"] = feat(rng, d["cen"], d["ka"], 2); d["xb"] = feat(rng, d["cen"], d["kb"], 2)
    d["f0"] = np.where(rng.random(d["f0"].shape) < 0.5, rng.choice(ends, d["f0"].shape), d["f0"])
    e = d["nbb"][:, ::2]; d["nbb"][:, ::2] = np.where(rng.random(e.shape) < 0.5, rng.choice(ends, e.shape), e)
    d["nbb"][:, 5] = NIL; d["f0"][0, 7] = NIL; d["nba"][:, 2, 0] = np.arange(VA); d["nba"][:, 2, 1] = WA - 1 - np.arange(VA)
    return pack(d)
def setup_inputs_cross(rng):
    h = min(S, G) // 2; a = np.argsort(rng.random((N, 8, S)), axis=-1)[..., :h]; b = S + np.argsort(rng.random((N, 8, VA - S)), axis=-1)[..., :G - h]
    bd = np.concatenate([a, b], axis=2); bd = np.take_along_axis(bd, np.argsort(rng.random(bd.shape), axis=-1), 2); d = parts(rng, bd)
    noise = np.full((1, 8, 1, 1), 3); noise[:, :2] = 1; d["xa"] = feat(rng, d["cen"], d["ka"], noise); d["xb"] = feat(rng, d["cen"], d["kb"], noise)
    for r in range(N):
        for g in range(8):
            far = OB + within(rng, d["kb"][(r + 1) % N, g, :H], np.broadcast_to(d["ka"][r, g, :S], (16, S))); f = d["f0"][r, g]
            d["f0"][r, g] = np.where((f != NIL) & (rng.random(f.shape) < 0.8), far, f)
    d["f0"][1::2, :4] = NIL; lo = np.arange(VA) < CAP
    for r in range(1, N, 2):
        for g in (0, 1):
            for p in range(16):
                row = d["nba"][r, g, p]; gh = row >= VA
                i = np.flatnonzero(gh & (lo == (g == 0))); j = np.flatnonzero(~gh & (lo == (g == 1))); k = min(i.size, j.size); i = i[:k]; j = j[:k]
                vi = row[i].copy(); row[i] = row[j]; row[j] = vi
    return pack(d)
def setup_inputs_spread(rng):
    d = parts(rng); cen = rng.integers(-127, 128, (8, KC, 16))
    for x, k, n in (("xa", d["ka"], VA), ("xb", d["kb"], OB)):
        v = np.clip(feat(rng, cen, k, rng.choice(np.array([0, 1, 2, 2, 3, 3, 5, 12]), (N, 8, 1, n))), -127, 127)
        v = np.where(rng.random((N, 8, 1, n)) < 0.125, rng.integers(-127, 128, v.shape), v)
        d[x] = v * (rng.random((N, 8, 1, n)) > 0.0625)
    d["nba"][:, :, 4:8] = np.argsort(rng.random((N, 8, 4, WA)), axis=-1)[..., :VA]
    d["nbb"] = np.where(rng.random(d["nbb"].shape) < 0.3, rng.integers(0, W, d["nbb"].shape), d["nbb"])
    return pack(d)
def check_inputs(d):
    bad = []
    for k, hi in (("nba", WA - 1), ("nbb", NIL), ("f0", NIL), ("bd", VA - 1)):
        if np.min(d[k]) < 0 or np.max(d[k]) > hi: bad.append("range of " + k)
    for k in ("xa", "xb"):
        v = d[k].astype(np.float32)
        if not np.all((v >= -127) & (v <= 127) & (np.rint(v) == v)): bad.append("whole numbers of " + k)
    s = np.sort(d["nba"], axis=2)
    if np.any(s[..., 1:] == s[..., :-1]): bad.append("repeated in a row of nba")
    s = np.sort(np.stack([gentries(a) for a in d["bd"]]), axis=2)
    if np.any(s[..., 1:] == s[..., :-1]): bad.append("repeated in bd")
    return bad
def reference(xa, xb, nba, nbb, f0, bd):
    A = xa.astype(np.float32).astype(np.int32).reshape(N, 8, 16, VA); own = xb.astype(np.float32).astype(np.int32).reshape(N, 8, 16, OB)
    na = nba.astype(np.int64).reshape(N, 8, 16, VA); no = nbb.astype(np.int64).reshape(N, 8, 16, OB); bl = np.stack([gentries(a) for a in bd]).astype(np.int64)
    B = np.zeros((N, 8, 16, W), np.int32); NB = np.full((N, 8, 16, W), NIL, np.int64)
    for r in range(N):
        q = (r + 1) % N; n = no[q, :, :, :H]
        B[r, :, :, :OB] = own[r]; B[r, :, :, OB:NIL] = own[q, :, :, :H]
        NB[r, :, :, :OB] = no[r]; NB[r, :, :, OB:NIL] = np.where(n < H, OB + n, NIL)
    F = np.full((N, 8, 16, VA), NIL, np.int64); F[..., :S] = f0.reshape(N, 8, 16, S)
    flag = np.ones((N, 8, VA), bool); e = [E0] * N; rows = np.arange(16)[:, None]
    for wave in range(RO):
        ext = []
        for r in range(N):
            q = (r - 1) % N; n = np.take_along_axis(F[q], bl[q][:, None, :], 2)
            ext.append(np.concatenate([F[r], np.where((n >= OB) & (n < NIL), n - OB, NIL)], axis=2))
        for r in range(N):
            good = 0
            for g in range(8):
                a = np.flatnonzero(flag[r, g] & np.all(F[r, g] == NIL, axis=0))[:CAP]
                x = A[r, g][:, a]; c = ext[r][g][rows, na[r, g][:, a]]; col = np.arange(a.size)
                new = np.full(c.shape, NIL, np.int64)
                for t in range(3):
                    near = (np.abs(B[r, g][:, c] - x[:, None, :]) <= e[r]).astype(np.int32)
                    v = (c != NIL) & (np.add.reduce(near, axis=0) >= M); new = np.where(v, c, new); some = np.any(v, axis=0)
                    if t == 0:
                        ok = some; b = np.where(ok, c[np.argmax(v, axis=0), col], NIL)
                    else:
                        b = np.where(some, c[15 - np.argmax(v[::-1], axis=0), col], b)
                    c = NB[r, g][:, b]
                s = a[ok]; b = b[ok]; F[r, g][:, s] = new[:, ok]
                A[r, g][:, s] = x[:, ok] + np.clip(B[r, g][:, b] - x[:, ok], -2, 2)
                flag[r, g, a] = False
                w = na[r, g][:, s].reshape(-1); flag[r, g, w[w < VA]] = True
                good += int(s.size)
            e[r] = E0 + (good & 1)
    return {"yf": F.reshape(N, 128, VA).astype(np.float32), "ya": A.reshape(N, 128, VA).astype(np.float32).astype(BF)}

@@ -1,0 +1,588 @@
+from concourse.mybir import AluOpType, AxisListType, ActivationFunctionType
+
+OP = AluOpType
+AF = ActivationFunctionType
+NOWN, NG, NB_, NS0, WAVES, H = 1024, 512, 2560, 34, 5, 1535
+DUMP, EW, GB = 1024, 1280, 1280
+EALL = GB + NG
+C0 = NS0 * 16
+MAG = 100663296.0
+WT = 32768.0
+GC, SC, LOOK = 0.0016, 0.0040, 0.05
+REM, WAKE, PEC = 4.0, 0.06, 0.00085
+ROUND_S = [(0, 0, 1), (0, 1, 1)]
+
+SIZE = {"float32": 4, "int32": 4, "bfloat16": 2, "float16": 2, "uint16": 2}
+SCRATCH = {}
+for _d, _l in (
+        ("bfloat16", "BT 4112 XA 1280 YA 1280 XR0 4096 XR1 4096 FLB 1024 FMB 1024 DGB 2048 NX 256 BG 1024 IB 128 INB 128"),
+        ("int32", "NBT 4104 NBX 1536 NAT 1280 NTMP 1024 F0 272 FI 272 FA 272 BD 32 IO 16 IO2 16 PI 1 PU 1 PQ 1 PV 1 FIN 256 FIA 256 "
+                  "BC 16 BI 16 PINT 1"),
+        ("uint16", "BDU 32 OFU 64 IDR 256 IXU 16 NAU 256 CU 256 BU 16 MO 256 ISU 16"),
+        ("float16", "SG 4096 DD_ 4096 NR 4096 DUMPR 256 ISN 272 BO 128 BON 128 BOB 128 I16 128 TRI 128 QF 128 QL 128 O16 128 SV 512 DG 2048 "
+                    "Z0 144 Z1 144 Z2 144 Z3 144 AV 64 IDF 256 V 256 SEL 256 SELC 256 OFFS 256 OT 256 PR16 1 DX 256 CL 256"),
+        ("float32", "E 1792 YF 1280 YT 1024 FL 1792 FM 1792 IDXW 2048 CELLV 1024 DEF 256 CA 64 MV 1280 GS 512 ONES 128 BOA 128 BOF 128 IF 128 "
+                    "UPF 128 S1F 128 S2F 128 TF 128 MK 16 PUF 1 PM 1 PN 1 IS 64 MC 8 NE 64 NT 64 T2 64 T3 64 XX 64 WTL 64 CS 65 U1 64 OF 64 "
+                    "INF 64 IXF 16 PH 256 CS0 256 FN 256 CS2 256 ACC 256 M 256 Y 256 B0 16 TS 16 TS2 16 PC 16 PR 1 NAF 256")):
+    _l = _l.split()
+    for _i in range(0, len(_l), 2):
+        SCRATCH[_l[_i]] = ("sbuf", [128, int(_l[_i + 1])], _d)
+PSUM = ("A0", "A1", "B0P", "B1P", "MP", "M5", "F6", "F7")
+for _n in PSUM:
+    SCRATCH[_n] = ("psum", [128, 512], "float32")
+
+LOADS = ("f0", "bd", "naA", "xaA", "xb", "nbA", "nbB", "naB", "xaB", "yaL", "oF", "oA")
+SEMAPHORES = (["cV", "cS", "cP", "cG", "bArr", "nArr", "bLoc", "nLoc", "crLoc"] + ["d_" + x for x in LOADS]
+              + ["gArr%d" % w for w in range(WAVES)] + ["gLoc%d" % w for w in range(WAVES)] + ["cred%d" % w for w in range(1, WAVES)])
+
+
+def rank_program(g, core, T, topo):
+    rank = T.rank_of(core)
+    if rank is None:
+        return
+    n = len(T.cores)
+    nxt, prv = T.cores[(rank + 1) % n], T.cores[(rank - 1) % n]
+    Q = {"V": g.vector, "S": g.scalar, "P": g.tensor, "G": g, "Y": g.sync}
+    cnt = {q: 0 for q in "VSPG"}
+    seen = {q: {} for q in Q}
+    know = {}
+    wr, rd = {}, {}
+    ops = []
+    loads = {}
+
+    def need(q, tok):
+        s, v = tok
+        if seen[q].get(s, 0) >= v:
+            return
+        Q[q].wait_ge(T.sem[s], v)
+        seen[q][s] = v
+        for s2, v2 in know.get(tok, {}).items():
+            if seen[q].get(s2, 0) < v2:
+                seen[q][s2] = v2
+
+    def conflicts(q, reads, writes, wr, rd, same_order):
+        out = []
+        for (nm, lo, hi) in reads:
+            ps = nm in PSUM
+            out += [(e[3], True) for e in wr.get(nm, ()) if ps or (e[0] < hi and lo < e[1])]
+            if ps:
+                out += [(e[3], e[2] != q) for e in rd.get(nm, ()) if same_order or e[2] != q]
+        for (nm, lo, hi) in writes:
+            ps = nm in PSUM
+            out += [(e[3], e[2] != q or not ps) for e in wr.get(nm, []) + rd.get(nm, [])
+                    if (ps or (e[0] < hi and lo < e[1])) and (same_order or e[2] != q or not ps)]
+        return out
+
+    def note(q, reads, writes, tok, wr, rd):
+        for (nm, lo, hi) in writes:
+            if nm in PSUM:
+                lo, hi = 0, 512
+            wr[nm] = [e for e in wr.get(nm, ()) if not (lo <= e[0] and e[1] <= hi)] + [(lo, hi, q, tok)]
+            rd[nm] = [e for e in rd.get(nm, ()) if not (lo <= e[0] and e[1] <= hi)]
+        for (nm, lo, hi) in reads:
+            if nm in PSUM:
+                lo, hi = 0, 512
+            rd[nm] = [e for e in rd.get(nm, ()) if not (e[2] == q and lo <= e[0] and e[1] <= hi)] + [(lo, hi, q, tok)]
+
+    def op(q, reads, writes, cost, lat, emit, after=()):
+        ops.append((q, reads, writes, cost, lat, emit, tuple(after)))
+        return len(ops) - 1
+
+    def waits(q, reads, writes, dma=False):
+        toks = {}
+        for tok, _ in conflicts(q, reads, writes, wr, rd, dma):
+            toks[tok[0]] = max(toks.get(tok[0], 0), tok[1])
+        for s in sorted(toks):
+            need(q, (s, toks[s]))
+
+    def run(q, reads, writes, cost, calls):
+        def emit():
+            waits(q, reads, writes)
+            for call in calls:
+                cnt[q] += 1
+                tok = ("c" + q, cnt[q])
+                know[tok] = dict(seen[q])
+                call().then_inc(T.sem["c" + q], 1)
+            note(q, reads, writes, tok, wr, rd)
+        return op(q, reads, writes, cost, 0.06, emit)
+
+    def issue():
+        m = len(ops)
+        w2, r2 = {}, {}
+        dep, succ = [], [[] for _ in range(m)]
+        for i, o in enumerate(ops):
+            d = {}
+            for j, strong in conflicts(o[0], o[1], o[2], w2, r2, True):
+                d[j] = d.get(j, False) or strong
+            for j in o[6]:
+                d[j] = True
+            dep.append(d)
+            for j in d:
+                succ[j].append(i)
+            note(o[0], o[1], o[2], i, w2, r2)
+        pri = [0.0] * m
+        for i in range(m - 1, -1, -1):
+            pri[i] = ops[i][3] + max([pri[j] + (ops[i][4] + WAKE if dep[j][i] else 0.0) for j in succ[i]] + [0.0])
+        left = [len(d) for d in dep]
+        ready = [0.0] * m
+        free, avail = {}, {}
+        for i, o in enumerate(ops):
+            free.setdefault(o[0], 0.0)
+            avail.setdefault(o[0], [])
+            if not left[i]:
+                avail[o[0]].append(i)
+        order = []
+        while len(order) < m:
+            t, q = min((max(free[q], min(ready[i] for i in a)), q) for q, a in avail.items() if a)
+            i = max((i for i in avail[q] if ready[i] <= t + LOOK), key=lambda i: (pri[i], -i))
+            t = max(t, ready[i])
+            avail[q].remove(i)
+            free[q] = t + ops[i][3]
+            order.append(i)
+            for j in succ[i]:
+                ready[j] = max(ready[j], t + ops[i][3] + (ops[i][4] + WAKE if dep[j][i] else 0.0))
+                left[j] -= 1
+                if not left[j]:
+                    avail[ops[j][0]].append(j)
+        for i in order:
+            ops[i][5]()
+
+    def R(nm, lo, hi, st=1):
+        return (T[nm][:, lo:hi:st] if st > 1 else T[nm][:, lo:hi], [(nm, lo, hi)])
+
+    def IND(nm, lo, hi, off, a, b):
+        return (T[nm][:, lo:hi].indirect(T[off][:, a:b]), [(nm, lo, hi)], [(off, a, b)])
+
+    def full(nm):
+        return R(nm, 0, SCRATCH[nm][1][1])
+
+    def hs(nm, h, k=128):
+        return R(nm, k * h, k * h + k)
+
+    def ind(x):
+        return len(x) > 2
+
+    def rds(*xs):
+        r = []
+        for x in xs:
+            if isinstance(x, tuple):
+                r += x[1] + (x[2] if ind(x) else [])
+        return r
+
+    def offs(out):
+        return out[2] if ind(out) else []
+
+    def ap(x):
+        return x[0] if isinstance(x, tuple) else x
+
+    def two(x):
+        return SIZE[SCRATCH[x[1][0][0]][2]] == 2
+
+    def width(x):
+        return x[0].shape[1]
+
+    def vcost(out, a, k, m):
+        if ind(out):
+            return 0.07 + m * SC
+        if ind(a):
+            return 0.07 + m * GC
+        return max(0.064, m * k * 0.001)
+
+    def cp(out, a):
+        m = width(a) if not ind(a) else width(out)
+        run("V", rds(a) + offs(out), out[1], vcost(out, a, 0.5 if two(out) and two(a) else 1.0, m),
+            [lambda: g.vector.tensor_copy(out[0], a[0])])
+
+    def tt(out, a, b, f):
+        k = 1.0 if a[1][0][0] in PSUM or b[1][0][0] in PSUM else 2.0
+        run("V", rds(a, b) + offs(out), out[1], vcost(out, a, k, width(b)), [lambda: g.vector.tensor_tensor(out[0], a[0], b[0], f)])
+
+    def ts(out, a, s1, op0, s2=None, op1=None):
+        c = vcost(out, a, 0.5 if two(out) and two(a) else 1.0, width(out))
+        if op1 is None:
+            run("V", rds(a, s1), out[1], c, [lambda: g.vector.tensor_scalar(out[0], a[0], ap(s1), None, op0)])
+        else:
+            run("V", rds(a, s1, s2), out[1], c, [lambda: g.vector.tensor_scalar(out[0], a[0], ap(s1), ap(s2), op0, op1)])
+
+    def ms(out, c):
+        return run("V", [], out[1], vcost(out, out, 0.5 if two(out) else 1.0, width(out)), [lambda: g.vector.memset(out[0], c)])
+
+    def act(out, a, func, **kw):
+        m = width(out) if ind(a) else width(a)
+        run("S", rds(a) + offs(out), out[1], 0.02 + vcost(out, a, 1.0, m), [lambda: g.scalar.activation(out[0], a[0], func, **kw)])
+
+    def mms(*group):
+        r, w, c, calls = [], [], 0.0, []
+        for (out, lhs, rhs, start, stop) in group:
+            r += [x for x in rds(lhs, rhs) if x not in r]
+            w += [x for x in out[1] if x not in w]
+            c += max(64, width(rhs)) * PEC
+            calls.append(lambda out=out, lhs=lhs, rhs=rhs, start=start, stop=stop: g.tensor.matmul(out[0], lhs[0], rhs[0], start, stop))
+        run("P", r, w, c, calls)
+
+    def aff(out, a, pattern, cmp, base, cm):
+        run("G", a[1], out[1], 0.4, [lambda: g.affine_select(out[0], a[0], pattern, cmp, 0.0, base, cm)])
+
+    def iota(out, pattern, base, cm):
+        kw = {} if SCRATCH[out[1][0][0]][2] == "int32" else {"allow_small_or_imprecise_dtypes": True}
+        run("G", [], out[1], 0.13 + 0.002 * width(out), [lambda: g.iota(out[0], pattern, base, cm, **kw)])
+
+    def load(q, sem, out, in_ap, after=(), fills=()):
+        nm, lo, hi = out[1][0]
+
+        def emit():
+            for k in after:
+                need(q, ("d_" + k, 16))
+            if fills:
+                waits(q, [], [(nm, 0, hi)], True)
+            tok = ("d_" + sem, 16)
+            know[tok] = dict(seen[q])
+            Q[q].dma_start(out[0], in_ap).then_inc(T.sem["d_" + sem], 16)
+            note("dma", [], out[1], tok, wr, rd)
+        loads[sem] = op(q, [], out[1], 0.1, 2.0 + (hi - lo) * SIZE[SCRATCH[nm][2]] * 128 / 150e3, emit, [loads[k] for k in after] + list(fills))
+
+    def store(q, sem, out_ap, a):
+        def emit():
+            waits(q, a[1], [], True)
+            Q[q].dma_start(out_ap, a[0]).then_inc(T.sem["d_" + sem], 16)
+        op(q, a[1], [], 0.1, 3.0, emit)
+
+    def send(dst, src, out, a, rsem, lsem, cred=None):
+        ne = len(topo.engines(core, dst))
+        ad = topo.addr(dst)
+
+        def emit():
+            waits("G", a[1], [])
+            if cred:
+                need("G", (cred, 1))
+            g.remote_dma(out_ap=out[0], in_ap=a[0], remote_sem=T.sem[rsem], local_sem=T.sem[lsem], pid=ad[1], routing_id=ad[0],
+                         dma_engine_mask=topo.mask(core, dst))
+            tok = (lsem, ne)
+            know[tok] = dict(seen["G"])
+            note("snd", a[1], [], tok, wr, rd)
+        i = op("G", a[1], [], 0.5, REM, emit)
+        op("R", [], out[1], 0.0, 0.0, lambda: note("rem", [], out[1], (rsem, len(topo.engines(src, core))), wr, rd), [i])
+
+    def credit(w):
+        ad = topo.addr(prv)
+
+        def emit():
+            waits("G", [], [("E", GB, EALL)])
+            g.remote_sem_update(T.sem["cred%d" % w], T.sem["crLoc"], ad[1], ad[0], 1 << topo.engines(core, prv)[0])
+        op("G", [], [("E", GB, EALL)], 0.3, 2.0, emit)
+
+    fb, fn = ms(R("BT", 0, 16), 512.0), ms(R("NBT", 0, 8), 4095)
+    load("Y", "f0", full("F0"), T.f0[:])
+    load("S", "bd", full("BD"), T.bd[:])
+    load("S", "xaA", R("XA", 0, C0), T.xa[:, 0:C0])
+    load("Y", "naA", R("NAT", 0, C0), T.nba[:, 0:C0])
+    load("Y", "xb", R("BT", 1, 1 + NB_), T.xb[:], (), [fb])
+    load("Y", "nbA", R("NBT", 1, 1 + H), T.nbb[:, 0:H], (), [fn])
+    load("Y", "nbB", R("NBT", 1 + H, 1 + NB_), T.nbb[:, H:NB_], ["xb"], [fn])
+    load("Y", "naB", R("NAT", C0, NOWN), T.nba[:, C0:NOWN])
+    load("Y", "xaB", R("XA", C0, NOWN), T.xa[:, C0:NOWN])
+    load("Y", "yaL", R("YA", 0, NOWN), T.xa[:])
+
+    def ghosts(w):
+        ts(full("GS"), IND("E", 0, NOWN, "BDU", 0, 32), -2560.0, OP.add, 0.0, OP.max)
+        send(nxt, prv, R("E", GB, EALL), full("GS"), "gArr%d" % w, "gLoc%d" % w, "cred%d" % w if w else None)
+
+    ms(full("ONES"), 1.0)
+    ms(R("E", 272, EW), 0.0)
+    ts(full("FI"), full("F0"), 1, OP.add)
+    ts(full("FA"), full("FI"), 4095, OP.bitwise_and)
+    cp(R("E", 0, 272), full("FA"))
+    cp(full("BDU"), full("BD"))
+    ts(full("ISN"), full("F0"), 4095, OP.is_equal)
+    ghosts(0)
+    send(prv, nxt, R("BT", 2561, 4096), R("BT", 1, 1 + H), "bArr", "bLoc")
+    iota(full("IO"), [[-1, 16]], 16, 1)
+    iota(full("PI"), [[0, 1]], 0, 1)
+    aff(full("BOA"), full("ONES"), [[-16, 8], [0, 16]], OP.is_ge, 0, 1)
+    aff(full("BOF"), full("BOA"), [[16, 8], [0, 16]], OP.is_ge, 15, -1)
+    aff(full("IF"), full("ONES"), [[-1, 128]], OP.is_equal, 0, 1)
+    aff(full("UPF"), full("BOF"), [[1, 128]], OP.is_gt, 0, -1)
+    iota(full("IS"), [[16, 64]], DUMP, 0)
+    iota(full("CELLV"), [[1, 1024]], 64, 0)
+    iota(full("DEF"), [[1, 256]], DUMP + 64, 0)
+    aff(full("S1F"), full("ONES"), [[1, 128]], OP.is_equal, -16, -1)
+    aff(full("S2F"), full("ONES"), [[1, 128]], OP.is_equal, 16, -1)
+    ts(full("IO2"), full("IO"), 15, OP.bitwise_and)
+    ts(full("PU"), full("PI"), 15, OP.bitwise_and)
+    ts(full("PQ"), full("PI"), 4, OP.logical_shift_right)
+    cp(full("PUF"), full("PU"))
+    ts(full("MK"), full("IO2"), 0, OP.is_equal)
+    ts(full("PV"), full("PQ"), 1, OP.bitwise_and)
+    cp(full("PM"), full("PV"))
+    ts(full("PN"), full("PM"), -1.0, OP.mult, 1.0, OP.add)
+    bo8 = (T["BOF"][:, 0:128:16], [("BOF", 0, 128)])
+    for z, v in (("Z1", 1.0), ("Z0", WT), ("Z2", 2048.0), ("Z3", 6144.0)):
+        ms(full(z), 0.0)
+        ts((T[z][:, 15:143:16], [(z, 0, 144)]), bo8, v, OP.mult)
+
+    def sel(z, p):
+        return R(z, 15 - p, 143 - p)
+
+    mms(*[(R("F7", 0, 17), sel("Z1", c), R("ISN", c, 272, 16), c == 0, c == 15) for c in range(16)])
+    cp(full("BO"), full("BOF"))
+    ts(full("TF"), full("IF"), -2047.0, OP.mult)
+    tt(full("TRI"), full("TF"), full("UPF"), OP.add)
+    ms(R("CS", 0, 1), 2047.0)
+    ts(full("CA"), full("IS"), full("PUF"), OP.add)
+    ms(full("AV"), 1.0)
+    ms(full("NE"), 0.0)
+    ms(full("WTL"), 1.0)
+    ts(R("AV", 0, 17), R("F7", 0, 17), 15.5, OP.is_gt)
+    ts(R("NE", 0, 17), R("F7", 0, 17), 15.5, OP.is_lt)
+
+    def front_a(w, ns):
+        mms((R("F6", 0, ns), full("TRI"), R("AV", 0, ns), True, True))
+        mms((R("F6", 64, 64 + ns), full("BO"), R("AV", 0, ns), True, True))
+        run("V", rds(R("ONES", 0, ns), R("F6", 64, 64 + ns)), [("CS", 1, 1 + ns)], 0.07,
+            [lambda: g.vector.tensor_tensor_scan(T["CS"][:, 1:1 + ns], T["ONES"][:, 0:ns], T["F6"][:, 64:64 + ns], 2047.0, OP.mult, OP.add)])
+        tt(R("U1", 0, ns), R("F6", 0, ns), R("CS", 0, ns), OP.add)
+        tt(R("OF", 0, ns), R("U1", 0, ns), R("CA", 0, ns), OP.min)
+        cp(R("OFU", 0, ns), R("OF", 0, ns))
+        act(R("IDXW", 0, 256), full("DEF"), AF.Copy)
+        act(IND("IDXW", 0, 2048, "OFU", 0, ns), R("CELLV", 0, 16 * ns), AF.Silu)
+        ts(R("INF", 0, ns), R("U1", 0, ns), 256.0, OP.is_lt)
+        tt(R("WTL", 0, ns), R("AV", 0, ns), R("INF", 0, ns), OP.subtract)
+
+    def front_b(w):
+        hi = C0 if w == 0 else EW
+        ts(full("IDF"), R("IDXW", 0, 256), -64.0, OP.add)
+        ts(full("IDR"), R("IDXW", 0, 256), -63.75, OP.add)
+        mms(*[(R("F7", 0, 16), R("DG", c * 128, c * 128 + 128), R("IDF", c, 256, 16), c == 0, c == 15) for c in range(16)])
+        for k in range(4):
+            act(R("XR%d" % (w % 2), 1024 * k, 1024 * k + 1024), IND("XA", 0, hi, "IDR", 64 * k, 64 * k + 64), AF.Identity)
+        ts(full("IXU"), R("F7", 0, 16), 0.25, OP.add)
+        cp(full("NAU"), IND("NAT", 0, hi, "IXU", 0, 16))
+        cp(full("IXF"), full("IXU"))
+        cp(full("NAF"), full("NAU"))
+
+    def remap(lo, hi):
+        ts(R("NTMP", lo, hi), R("NAT", lo, hi), 1024, OP.is_ge, 256, OP.mult)
+        tt(R("NAT", lo, hi), R("NAT", lo, hi), R("NTMP", lo, hi), OP.add)
+
+    front_a(0, NS0)
+    for c in range(16):
+        ts(R("DG", c * 128, c * 128 + 128), full("IF"), R("MK", c, c + 1), OP.mult)
+    remap(0, C0)
+    front_b(0)
+    ms(full("MC"), MAG + 8.0)
+    ms(R("BT", 4096, 4112), 512.0)
+    ms(R("NBT", 4096, 4104), 4095)
+    ts(full("BOB"), full("BOF"), -12.5 * WT / 16, OP.mult)
+    ms(full("O16"), 1.0)
+    tt(full("QF"), full("UPF"), full("IF"), OP.subtract)
+    tt(full("TF"), full("BOF"), full("UPF"), OP.subtract)
+    tt(full("TF"), full("TF"), full("IF"), OP.subtract)
+    tt(full("QL"), full("TF"), full("IF"), OP.subtract)
+    ts(R("NBX", 0, H), R("NBT", 1, 1 + H), 1535, OP.min, 2560, OP.add)
+    send(prv, nxt, R("NBT", 2561, 4096), R("NBX", 0, H), "nArr", "nLoc")
+    ts(full("BON"), full("BOF"), -4096.0, OP.mult)
+    cp(full("I16"), full("IF"))
+    ts(full("DUMPR"), full("DEF"), -64.0, OP.add)
+    ts(R("SV", 0, 128), full("IF"), full("PN"), OP.mult)
+    ts(R("SV", 128, 256), full("S1F"), full("PN"), OP.mult)
+    ts(R("SV", 256, 384), full("S2F"), full("PM"), OP.mult)
+    ts(R("SV", 384, 512), full("IF"), full("PM"), OP.mult)
+    cp(full("DGB"), full("DG"))
+    cp(full("IB"), full("IF"))
+    ts(full("INB"), full("IF"), -1.0, OP.mult)
+    for w in range(4):
+        ms(R("MV", 256 * w, 256 * w + 256), 4.0 * w + 4.0)
+    ms(R("MV", 1024, 1280), 100.0)
+    ms(full("FL"), 0.0)
+    ms(full("FM"), 0.0)
+    ms(R("NAT", NOWN, EW), DUMP)
+    ms(R("XA", NOWN, EW), 0.0)
+    ms(R("YA", NOWN, EW), 0.0)
+    remap(C0, NOWN)
+
+    def A(h):
+        return "A%d" % h
+
+    def B(h):
+        return "B%dP" % h
+
+    def seeds(h, q):
+        o = h * 128 + q * 64
+        out = R(A(h), 64 * q, 64 * q + 64)
+        ts(R("SG", o * 16, o * 16 + 1024), IND("E", 0, EALL, "NAU", o, o + 64), -2048.0, OP.add)
+        mms(*[(out, R("DG", p * 128, p * 128 + 128), R("SG", o * 16 + p, o * 16 + 1024, 16), p == 0, p == 15) for p in range(16)])
+
+    def seeds_end(h):
+        ts(hs("CU", h), R(A(h), 0, 128), 2048.0, OP.add)
+        act(hs("PH", h), R(A(h), 0, 128), AF.Identity)
+        act(hs("CS0", h), R(A(h), 0, 128), AF.Identity, bias=-4096.0)
+
+    def near(w, t, h, q):
+        o = h * 128 + q * 64
+        m = R("MC", w, w + 1)
+        xr = "XR%d" % (w % 2)
+        if (t, h, q) in ROUND_S:
+            act(full("BG"), IND("BT", 0, 4097, "CU", o, o + 64), AF.Identity)
+            for k, bank in enumerate(("M5", "F6")):
+                c = o * 16 + 512 * k
+                mms((R(bank, 0, 512), full("IB"), R("BG", 512 * k, 512 * k + 512), True, False),
+                    (R(bank, 0, 512), full("INB"), R(xr, c, c + 512), False, True))
+                ts(R("NR", c, c + 512), R(bank, 0, 512), m, OP.add, m, OP.is_equal)
+        else:
+            tt(R("DD_", o * 16, o * 16 + 1024), IND("BT", 0, 4097, "CU", o, o + 64), R(xr, o * 16, o * 16 + 1024), OP.subtract)
+            ts(R("NR", o * 16, o * 16 + 1024), R("DD_", o * 16, o * 16 + 1024), m, OP.add, m, OP.is_equal)
+        out = R(A(h), 64 * q, 64 * q + 64)
+        mms((out, full("BOB"), R("O16", 0, 64), True, False),
+            *[(out, sel("Z0", p), R("NR", o * 16 + p, o * 16 + 1024, 16), False, p == 15) for p in range(16)])
+
+    def seg1(w, t, h):
+        a = R(A(h), 0, 128)
+        ts(hs("V", h), a, 0.0, OP.is_gt)
+        mms((R(B(h), 0, 128), full("QF" if t == 0 else "QL"), hs("V", h), True, True))
+        if t == 0:
+            tt(hs("ACC", h), a, hs("CS0", h), OP.min)
+        elif t == 1:
+            tt(hs("M", h), a, hs("FN", h), OP.min)
+            tt(hs("ACC", h), hs("ACC", h), hs("M", h), OP.max)
+        else:
+            tt(hs("M", h), a, hs("CS2", h), OP.min)
+            tt(hs("FIN", h), hs("Y", h), hs("M", h), OP.max)
+            ts(hs("FIA", h), hs("FIN", h), 4095, OP.bitwise_and)
+            cp(IND("YF" if w == WAVES - 1 else "E", 0, EW, "IXU", 8 * h, 8 * h + 8), hs("FIA", h))
+
+    def seg2(w, t, h):
+        ts(hs("SEL", h), R(B(h), 0, 128), 0.0, OP.is_lt)
+        tt(hs("SELC", h), hs("SEL", h), hs("PH" if t == 0 else "FN", h), OP.mult)
+        out = R(B(h), 128, 136)
+        z = "Z2" if t == 0 else "Z3"
+        mms(*[(out, sel(z, c), R("SEL", 128 * h + c, 128 * h + 128, 16), c == 0, False) for c in range(16)],
+            *[(out, sel("Z1", c), R("SELC", 128 * h + c, 128 * h + 128, 16), False, c == 15) for c in range(16)])
+
+    def seg3(w, t, h):
+        x = R(B(h), 128, 136)
+        b = hs("BU", h, 8)
+        if t == 0:
+            cp(b, x)
+            cp(hs("B0", h, 8), x)
+        else:
+            tt(hs("BC", h, 8), x, hs("B0" if t == 1 else "BI", h, 8), OP.max)
+            ts(hs("BI", h, 8), hs("BC", h, 8), 4095, OP.bitwise_and)
+            cp(b, hs("BI", h, 8))
+        if t < 2:
+            ts(hs("FN", h), IND("NBT", 0, 4097, "BU", 8 * h, 8 * h + 8), -2047.0, OP.add)
+            ts(hs("CU", h), hs("FN", h), 2048.0, OP.add)
+        if t == 1:
+            last = w == WAVES - 1
+            ts(hs("CS2", h), hs("FN", h), 10240.0 - (1.0 if last else 0.0), OP.add)
+            ts(hs("Y", h), hs("ACC", h), 6144.0, OP.add, 0.0, OP.max)
+            if last:
+                ts(hs("Y", h), hs("Y", h), -1.0, OP.add)
+
+    def idxs(w):
+        ts(full("TS"), full("B0"), 0.0, OP.is_equal, 4096.0, OP.mult)
+        tt(full("TS"), full("TS"), R("CA", 0, 16), OP.min)
+        tt(full("TS2"), full("TS"), full("IXF"), OP.max)
+        cp(full("ISU"), full("TS2"))
+
+    def marks(w, h):
+        o = R("MP", 128 * h, 128 * h + 128)
+        mms((o, full("BON"), hs("SEL", h), True, False), (o, full("I16"), hs("DUMPR", h), False, True))
+        tt(hs("OFFS", h), o, hs("NAF", h), OP.max)
+        run("V", hs("OFFS", h)[1], hs("OT", h)[1], 0.07, [lambda: g.vector.transpose(hs("OT", h)[0], hs("OFFS", h)[0])])
+        grp = []
+        for v in range(2):
+            for b in range(4):
+                for k in range(2):
+                    z = (2 * v + k) * 128
+                    c = 128 * h + 32 * b + 16 * k
+                    grp.append((R("M5", 128 * h + 4 * v + b, 128 * h + 128, 8), R("SV", z, z + 128), R("OT", c, c + 16), k == 0, k == 1))
+        mms(*grp)
+        cp(hs("MO", h), R("M5", 128 * h, 128 * h + 128))
+        for p in range(16):
+            act(IND("FL" if p % 2 else "FM", 0, EALL, "MO", 128 * h + 8 * p, 128 * h + 8 * p + 8), R("MV", 256 * w, 256 * w + 128), AF.Silu)
+
+    def succeeded(w):
+        act(IND("FL", 0, EALL, "ISU", 0, 16), R("MV", 1024, 1280), AF.Silu)
+        act(full("FMB"), R("FM", 0, NOWN), AF.Copy)
+        act(full("FLB"), R("FL", 0, NOWN), AF.Copy)
+
+    def parity(w):
+        ts(full("PC"), full("B0"), 0.0, OP.is_gt)
+        run("V", rds(full("PC")), [("PR", 0, 1)], 0.07,
+            [lambda: g.vector.tensor_reduce(T["PR"][:, 0:1], T["PC"][:, 0:16], axis=AxisListType.X, op=OP.add)])
+        cp(full("PR16"), full("PR"))
+        mms((R("F7", 64, 65), full("O16"), full("PR16"), True, True))
+        cp(full("PINT"), R("F7", 64, 65))
+        ts(full("PINT"), full("PINT"), 1, OP.bitwise_and)
+        ts(R("MC", w + 1, w + 2), full("PINT"), -8.0, OP.mult, MAG + 8.0, OP.add)
+
+    def front_c(w):
+        for nm, k in (("FMB", 192), ("FLB", 128)):
+            mms(*[(R("F6", k, k + 64), R("DGB", c * 128, c * 128 + 128), R(nm, c, 1024, 16), c == 0, c == 15) for c in range(16)])
+        c = R("F6", 128, 192)
+        ts(full("T3"), R("F6", 192, 256), 4.0 * w + 2.0, OP.is_gt)
+        ts(full("T2"), c, 4.0 * w + 2.0, OP.is_gt)
+        ts(full("NT"), c, 60.0, OP.is_ge)
+        tt(full("XX"), full("WTL"), full("T3"), OP.max)
+        tt(full("XX"), full("XX"), full("T2"), OP.max)
+        tt(full("NE"), full("NE"), full("NT"), OP.max)
+        tt(full("AV"), full("XX"), full("NE"), OP.is_gt)
+        front_a(w + 1, 64)
+
+    def numbers(w, h):
+        x = R("XR%d" % (w % 2), 2048 * h, 2048 * h + 2048, 16)
+        tt(hs("DX", h), IND("BT", 0, 4097, "BU", 8 * h, 8 * h + 8), x, OP.subtract)
+        ts(hs("CL", h), hs("DX", h), -2.0, OP.max, 2.0, OP.min)
+        tt(hs("NX", h), hs("CL", h), x, OP.add)
+        cp(IND("YA", 0, EW, "ISU", 8 * h, 8 * h + 8), hs("NX", h))
+
+    for w in range(WAVES):
+        last = w == WAVES - 1
+        for h in range(2):
+            seeds(h, 0)
+            seeds(h, 1)
+            seeds_end(h)
+        if not last:
+            credit(w + 1)
+        else:
+            act(R("YF", 0, NOWN), R("E", 0, NOWN), AF.Identity, bias=-1.0)
+            act(full("YT"), R("E", 0, NOWN), AF.Identity, bias=4095.0, scale=-5000.0)
+            tt(R("YF", 0, NOWN), R("YF", 0, NOWN), full("YT"), OP.max)
+        for t in range(3):
+            for h in range(2):
+                near(w, t, h, 0)
+                near(w, t, h, 1)
+                seg1(w, t, h)
+                seg2(w, t, h)
+                if t == 0 and not last:
+                    marks(w, h)
+                seg3(w, t, h)
+            if t == 0:
+                idxs(w)
+                if not last:
+                    succeeded(w)
+                    parity(w)
+                    front_c(w)
+            if t == 2:
+                if not last:
+                    ghosts(w + 1)
+                else:
+                    store("Y", "oF", T.yf[:], R("YF", 0, NOWN))
+                numbers(w, 0)
+                numbers(w, 1)
+                if not last:
+                    front_b(w + 1)
+    store("Y", "oA", T.ya[:], R("YA", 0, NOWN))
+    issue()
+
+    for s in "VSPG":
+        g.wait_ge(T.sem["c" + s], cnt[s])
+    for x in LOADS:
+        g.wait_ge(T.sem["d_" + x], 16)
+    ne = len(topo.engines(core, nxt))
+    for w in range(WAVES):
+        g.wait_ge(T.sem["gArr%d" % w], ne)
+        g.wait_ge(T.sem["gLoc%d" % w], ne)
+    for s in ("bArr", "nArr", "bLoc", "nLoc"):
+        g.wait_ge(T.sem[s], len(topo.engines(core, prv)))
+    g.wait_ge(T.sem["crLoc"], WAVES - 1)

@@ -1,37 +1,49 @@
-from concourse.mybir import AluOpType, AxisListType, ActivationFunctionType
+from concourse.mybir import AluOpType, ActivationFunctionType
 
 OP = AluOpType
 AF = ActivationFunctionType
-NOWN, NG, NB_, NS0, WAVES, H = 1024, 512, 2560, 34, 5, 1535
-DUMP, EW, GB = 1024, 1280, 1280
-EALL = GB + NG
-C0 = NS0 * 16
+NOWN, NG, NB_, WAVES, H = 1024, 512, 2560, 5, 1535
+SP = 256
+EW = SP + NOWN
+EALL = EW + NG
+NS = (34, 49, 64, 64, 64)
+C0 = NS[0] * 16
 MAG = 100663296.0
+M32 = 402653184.0
 WT = 32768.0
-GC, SC, LOOK = 0.0016, 0.0040, 0.05
-REM, WAKE, PEC = 4.0, 0.06, 0.00085
-ROUND_S = [(0, 0, 1), (0, 1, 1)]
+NOFF = 783.5
+FW = 136
+CY, GC, SC, PEC = 0.00095, 1.56, 3.8, 0.0005
+LOOK, REM, WAKE = 0.05, 3.5, 0.06
+SEEDQ = ("SSVS", "SSVS", "SSVS", "SSVS", "SVSV")
+VPATH = (((0, 1), (1, 1), (2, 1)),) * 4 + (((0, 1), (1, 1), (2, 1), (0, 3), (1, 3), (2, 3)),)
+SIGNQ = "SSS"
+GHOSTQ = "S"
+XRQ = "G"
+PASSES = 8
+ORDER = []
 
 SIZE = {"float32": 4, "int32": 4, "bfloat16": 2, "float16": 2, "uint16": 2}
 SCRATCH = {}
 for _d, _l in (
-        ("bfloat16", "BT 4112 XA 1280 YA 1280 XR0 4096 XR1 4096 FLB 1024 FMB 1024 DGB 2048 NX 256 BG 1024 IB 128 INB 128"),
-        ("int32", "NBT 4104 NBX 1536 NAT 1280 NTMP 1024 F0 272 FI 272 FA 272 BD 32 IO 16 IO2 16 PI 1 PU 1 PQ 1 PV 1 FIN 256 FIA 256 "
-                  "BC 16 BI 16 PINT 1"),
-        ("uint16", "BDU 32 OFU 64 IDR 256 IXU 16 NAU 256 CU 256 BU 16 MO 256 ISU 16"),
-        ("float16", "SG 4096 DD_ 4096 NR 4096 DUMPR 256 ISN 272 BO 128 BON 128 BOB 128 I16 128 TRI 128 QF 128 QL 128 O16 128 SV 512 DG 2048 "
-                    "Z0 144 Z1 144 Z2 144 Z3 144 AV 64 IDF 256 V 256 SEL 256 SELC 256 OFFS 256 OT 256 PR16 1 DX 256 CL 256"),
-        ("float32", "E 1792 YF 1280 YT 1024 FL 1792 FM 1792 IDXW 2048 CELLV 1024 DEF 256 CA 64 MV 1280 GS 512 ONES 128 BOA 128 BOF 128 IF 128 "
-                    "UPF 128 S1F 128 S2F 128 TF 128 MK 16 PUF 1 PM 1 PN 1 IS 64 MC 8 NE 64 NT 64 T2 64 T3 64 XX 64 WTL 64 CS 65 U1 64 OF 64 "
-                    "INF 64 IXF 16 PH 256 CS0 256 FN 256 CS2 256 ACC 256 M 256 Y 256 B0 16 TS 16 TS2 16 PC 16 PR 1 NAF 256")):
+        ("bfloat16", "BT 4112 XA 1536 XR0 2048 XR1 2048 X0 256 X1 256 BG0 1024 BG1 1024 IB 128 INB 128 CL 256 HI 272"),
+        ("int32", "NBT 4104 NBX 1536 NAT 1280 F0 272 FI 272 FA 272 BD 32 IO 16 IO2 16 PI 1 PU 1 PQ 1 PV 1 FIN 256 FIA 256 "
+                  "K1 16 K2 16 K3 16 PINT 1"),
+        ("uint16", "BDU 32 IXU0 16 IXU1 16 SU 16 NAU 256 CU 256 BU0 16 BU1 16 BU2 16 ISU 16"),
+        ("float16", "SG 4096 DD_ 2048 NR 4096 ISN 272 BO 128 BOB 128 BOK 128 I16 128 TRI 128 QF 128 QL 128 O16 64 SV 512 DG 2048 "
+                    "Z0 144 Z1 144 ZU 144 AV 64 W1 64 N1 64 SGN 256 SEL 256 RR 256 PH 256 FN 256 DX 256 NF 256 CF 256 OH 256 S16 16 "
+                    "H0 272 LO 272 LF0 4352 LF1 4352 HF0 4352 HF1 4352 MS 1024"),
+        ("float32", "E 1792 YF 1280 GS 512 CELL 1280 JF 256 JT 16 JB 16 J2 16 ONES 128 BOA 128 BOF 128 IF 128 UPF 128 S1F 128 S2F 128 "
+                    "TF 128 TG 128 MK 16 PUF 1 PUW 1 PM 1 PN 1 THF 1 THL 1 MC 8 CS 65 U1 72 JUNK 1024 SA 16 IXF0 16 IXF1 16 "
+                    "CC 256 ACC 256 B0 16 TS 16 TS2 16 PC 16 PR 1")):
     _l = _l.split()
     for _i in range(0, len(_l), 2):
         SCRATCH[_l[_i]] = ("sbuf", [128, int(_l[_i + 1])], _d)
-PSUM = ("A0", "A1", "B0P", "B1P", "MP", "M5", "F6", "F7")
+PSUM = ("A0", "A1", "B0P", "B1P", "D0", "D1", "MKP", "F6")
 for _n in PSUM:
     SCRATCH[_n] = ("psum", [128, 512], "float32")
 
-LOADS = ("f0", "bd", "naA", "xaA", "xb", "nbA", "nbB", "naB", "xaB", "yaL", "oF", "oA")
+LOADS = ("f0", "bd", "naA", "xaA", "xbA", "xbB", "nbA", "nbB", "naB", "xaB", "oF", "oA")
 SEMAPHORES = (["cV", "cS", "cP", "cG", "bArr", "nArr", "bLoc", "nLoc", "crLoc"] + ["d_" + x for x in LOADS]
               + ["gArr%d" % w for w in range(WAVES)] + ["gLoc%d" % w for w in range(WAVES)] + ["cred%d" % w for w in range(1, WAVES)])
 
@@ -69,8 +81,8 @@ def rank_program(g, core, T, topo):
                 out += [(e[3], e[2] != q) for e in rd.get(nm, ()) if same_order or e[2] != q]
         for (nm, lo, hi) in writes:
             ps = nm in PSUM
-            out += [(e[3], e[2] != q or not ps) for e in wr.get(nm, []) + rd.get(nm, [])
-                    if (ps or (e[0] < hi and lo < e[1])) and (same_order or e[2] != q or not ps)]
+            out += [(e[3], e[2] != q or not ps or q != "P") for e in wr.get(nm, []) + rd.get(nm, [])
+                    if (ps or (e[0] < hi and lo < e[1])) and (same_order or e[2] != q or not ps or q != "P")]
         return out
 
     def note(q, reads, writes, tok, wr, rd):
@@ -110,7 +122,7 @@ def rank_program(g, core, T, topo):
         m = len(ops)
         w2, r2 = {}, {}
         dep, succ = [], [[] for _ in range(m)]
-        for i, o in enumerate(ops):
+        for i, o in enumerate(ops if not ORDER else ()):
             d = {}
             for j, strong in conflicts(o[0], o[1], o[2], w2, r2, True):
                 d[j] = d.get(j, False) or strong
@@ -120,35 +132,52 @@ def rank_program(g, core, T, topo):
             for j in d:
                 succ[j].append(i)
             note(o[0], o[1], o[2], i, w2, r2)
-        pri = [0.0] * m
-        for i in range(m - 1, -1, -1):
-            pri[i] = ops[i][3] + max([pri[j] + (ops[i][4] + WAKE if dep[j][i] else 0.0) for j in succ[i]] + [0.0])
-        left = [len(d) for d in dep]
-        ready = [0.0] * m
-        free, avail = {}, {}
-        for i, o in enumerate(ops):
-            free.setdefault(o[0], 0.0)
-            avail.setdefault(o[0], [])
-            if not left[i]:
-                avail[o[0]].append(i)
-        order = []
-        while len(order) < m:
-            t, q = min((max(free[q], min(ready[i] for i in a)), q) for q, a in avail.items() if a)
-            i = max((i for i in avail[q] if ready[i] <= t + LOOK), key=lambda i: (pri[i], -i))
-            t = max(t, ready[i])
-            avail[q].remove(i)
-            free[q] = t + ops[i][3]
-            order.append(i)
-            for j in succ[i]:
-                ready[j] = max(ready[j], t + ops[i][3] + (ops[i][4] + WAKE if dep[j][i] else 0.0))
-                left[j] -= 1
-                if not left[j]:
-                    avail[ops[j][0]].append(j)
-        for i in order:
+        fwd = [[(j, ops[i][4] + WAKE if dep[j][i] else 0.0) for j in succ[i]] for i in range(len(dep))]
+        bwd = [[(j, ops[j][4] + WAKE if dep[i][j] else 0.0) for j in dep[i]] for i in range(len(dep))]
+
+        def sweep(edges, pri):
+            left = [0] * m
+            for e in edges:
+                for j, _ in e:
+                    left[j] += 1
+            ready, end = [0.0] * m, [0.0] * m
+            free, avail = {}, {}
+            for i, o in enumerate(ops):
+                free.setdefault(o[0], 0.0)
+                avail.setdefault(o[0], [])
+                if not left[i]:
+                    avail[o[0]].append(i)
+            order = []
+            while len(order) < m:
+                t, q = min((max(free[q], min(ready[i] for i in a)), q) for q, a in avail.items() if a)
+                i = max((i for i in avail[q] if ready[i] <= t + LOOK), key=lambda i: (pri[i], -i))
+                avail[q].remove(i)
+                end[i] = free[q] = max(t, ready[i]) + ops[i][3]
+                order.append(i)
+                for j, lag in edges[i]:
+                    ready[j] = max(ready[j], end[i] + lag)
+                    left[j] -= 1
+                    if not left[j]:
+                        avail[ops[j][0]].append(j)
+            return order, end
+
+        if not ORDER:
+            pri = [0.0] * m
+            for i in range(m - 1, -1, -1):
+                pri[i] = ops[i][3] + max([pri[j] + lag for j, lag in fwd[i]] + [0.0])
+            best = None
+            for _ in range(PASSES):
+                order, end = sweep(fwd, pri)
+                if best is None or max(end) < best[0]:
+                    best = (max(end), order)
+                pri = sweep(bwd, end)[1]
+            ORDER.extend(best[1])
+        for i in ORDER:
             ops[i][5]()
 
-    def R(nm, lo, hi, st=1):
-        return (T[nm][:, lo:hi:st] if st > 1 else T[nm][:, lo:hi], [(nm, lo, hi)])
+    def R(nm, lo, hi, st=1, part=(0, 128)):
+        p = slice(part[0], part[1])
+        return (T[nm][p, lo:hi:st] if st > 1 else T[nm][p, lo:hi], [(nm, lo, hi)])
 
     def IND(nm, lo, hi, off, a, b):
         return (T[nm][:, lo:hi].indirect(T[off][:, a:b]), [(nm, lo, hi)], [(off, a, b)])
@@ -183,10 +212,10 @@ def rank_program(g, core, T, topo):
 
     def vcost(out, a, k, m):
         if ind(out):
-            return 0.07 + m * SC
+            return 0.05 + m * SC * CY
         if ind(a):
-            return 0.07 + m * GC
-        return max(0.064, m * k * 0.001)
+            return 0.05 + m * GC * CY
+        return max(64, m * k) * CY
 
     def cp(out, a):
         m = width(a) if not ind(a) else width(out)
@@ -207,25 +236,36 @@ def rank_program(g, core, T, topo):
     def ms(out, c):
         return run("V", [], out[1], vcost(out, out, 0.5 if two(out) else 1.0, width(out)), [lambda: g.vector.memset(out[0], c)])
 
-    def act(out, a, func, **kw):
+    def act(out, a, func=AF.Identity, bias=0.0, scale=1.0, acc=None):
         m = width(out) if ind(a) else width(a)
-        run("S", rds(a) + offs(out), out[1], 0.02 + vcost(out, a, 1.0, m), [lambda: g.scalar.activation(out[0], a[0], func, **kw)])
+        kw = {"accum_out": acc[0]} if acc else {}
+        run("S", rds(a, bias, scale) + offs(out), out[1] + (acc[1] if acc else []), (0.02 if acc or ind(a) else 0.0) + vcost(out, a, 1.0, m),
+            [lambda: g.scalar.activation(out[0], a[0], func, bias=ap(bias), scale=ap(scale), **kw)])
+
+    def add(q, out, a, c):
+        if q == "S":
+            act(out, a, bias=c)
+        else:
+            ts(out, a, c, OP.add)
 
     def mms(*group):
         r, w, c, calls = [], [], 0.0, []
         for (out, lhs, rhs, start, stop) in group:
             r += [x for x in rds(lhs, rhs) if x not in r]
             w += [x for x in out[1] if x not in w]
-            c += max(64, width(rhs)) * PEC
+            c += max(min(64, width(lhs)), width(rhs)) * PEC * (1 if two(lhs) else 4)
             calls.append(lambda out=out, lhs=lhs, rhs=rhs, start=start, stop=stop: g.tensor.matmul(out[0], lhs[0], rhs[0], start, stop))
         run("P", r, w, c, calls)
 
+    def summ(out, *pairs):
+        return [(out, l, r, i == 0, i == len(pairs) - 1) for i, (l, r) in enumerate(pairs)]
+
     def aff(out, a, pattern, cmp, base, cm):
-        run("G", a[1], out[1], 0.4, [lambda: g.affine_select(out[0], a[0], pattern, cmp, 0.0, base, cm)])
+        run("G", a[1], out[1], 0.17 + 2 * CY * width(out), [lambda: g.affine_select(out[0], a[0], pattern, cmp, 0.0, base, cm)])
 
     def iota(out, pattern, base, cm):
         kw = {} if SCRATCH[out[1][0][0]][2] == "int32" else {"allow_small_or_imprecise_dtypes": True}
-        run("G", [], out[1], 0.13 + 0.002 * width(out), [lambda: g.iota(out[0], pattern, base, cm, **kw)])
+        run("G", [], out[1], 0.13 + 2 * CY * width(out), [lambda: g.iota(out[0], pattern, base, cm, **kw)])
 
     def load(q, sem, out, in_ap, after=(), fills=()):
         nm, lo, hi = out[1][0]
@@ -239,7 +279,12 @@ def rank_program(g, core, T, topo):
             know[tok] = dict(seen[q])
             Q[q].dma_start(out[0], in_ap).then_inc(T.sem["d_" + sem], 16)
             note("dma", [], out[1], tok, wr, rd)
-        loads[sem] = op(q, [], out[1], 0.1, 2.0 + (hi - lo) * SIZE[SCRATCH[nm][2]] * 128 / 150e3, emit, [loads[k] for k in after] + list(fills))
+        queued[0] += (hi - lo) * SIZE[SCRATCH[nm][2]] * 128 / 200e3
+        prev = list(loads.values())[-1:] if q == "Y" else []
+        loads[sem] = op(q, [], out[1], 0.05, 1.8 + queued[0], emit, [loads[k] for k in after] + list(fills))
+        chain.append(loads[sem])
+
+    queued, chain = [0.0], []
 
     def store(q, sem, out_ap, a):
         def emit():
@@ -247,7 +292,7 @@ def rank_program(g, core, T, topo):
             Q[q].dma_start(out_ap, a[0]).then_inc(T.sem["d_" + sem], 16)
         op(q, a[1], [], 0.1, 3.0, emit)
 
-    def send(dst, src, out, a, rsem, lsem, cred=None):
+    def send(dst, src, out, a, rsem, lsem, cred=None, lat=REM):
         ne = len(topo.engines(core, dst))
         ad = topo.addr(dst)
 
@@ -260,51 +305,57 @@ def rank_program(g, core, T, topo):
             tok = (lsem, ne)
             know[tok] = dict(seen["G"])
             note("snd", a[1], [], tok, wr, rd)
-        i = op("G", a[1], [], 0.5, REM, emit)
+        i = op("G", a[1], [], 0.5, lat, emit)
         op("R", [], out[1], 0.0, 0.0, lambda: note("rem", [], out[1], (rsem, len(topo.engines(src, core))), wr, rd), [i])
 
     def credit(w):
         ad = topo.addr(prv)
 
         def emit():
-            waits("G", [], [("E", GB, EALL)])
+            waits("G", [], [("E", EW, EALL)])
             g.remote_sem_update(T.sem["cred%d" % w], T.sem["crLoc"], ad[1], ad[0], 1 << topo.engines(core, prv)[0])
-        op("G", [], [("E", GB, EALL)], 0.3, 2.0, emit)
+        op("G", [], [("E", EW, EALL)], 0.3, 2.0, emit)
 
     fb, fn = ms(R("BT", 0, 16), 512.0), ms(R("NBT", 0, 8), 4095)
     load("Y", "f0", full("F0"), T.f0[:])
     load("S", "bd", full("BD"), T.bd[:])
-    load("S", "xaA", R("XA", 0, C0), T.xa[:, 0:C0])
-    load("Y", "naA", R("NAT", 0, C0), T.nba[:, 0:C0])
-    load("Y", "xb", R("BT", 1, 1 + NB_), T.xb[:], (), [fb])
+    load("Y", "naA", R("NAT", SP, SP + C0), T.nba[:, 0:C0])
+    load("S", "xaA", R("XA", SP, SP + C0), T.xa[:, 0:C0])
+    load("Y", "xbA", R("BT", 1, 1 + H), T.xb[:, 0:H], (), [fb])
+    load("Y", "xbB", R("BT", 1 + H, 1 + NB_), T.xb[:, H:NB_], ["f0"])
     load("Y", "nbA", R("NBT", 1, 1 + H), T.nbb[:, 0:H], (), [fn])
-    load("Y", "nbB", R("NBT", 1 + H, 1 + NB_), T.nbb[:, H:NB_], ["xb"], [fn])
-    load("Y", "naB", R("NAT", C0, NOWN), T.nba[:, C0:NOWN])
-    load("Y", "xaB", R("XA", C0, NOWN), T.xa[:, C0:NOWN])
-    load("Y", "yaL", R("YA", 0, NOWN), T.xa[:])
+    load("Y", "nbB", R("NBT", 1 + H, 1 + NB_), T.nbb[:, H:NB_], ["xbA"])
+    load("Y", "naB", R("NAT", SP + C0, EW), T.nba[:, C0:NOWN], ["xbA"])
+    load("Y", "xaB", R("XA", SP + C0, EW), T.xa[:, C0:NOWN], ["xbA"])
 
     def ghosts(w):
-        ts(full("GS"), IND("E", 0, NOWN, "BDU", 0, 32), -2560.0, OP.add, 0.0, OP.max)
-        send(nxt, prv, R("E", GB, EALL), full("GS"), "gArr%d" % w, "gLoc%d" % w, "cred%d" % w if w else None)
+        src = IND("E", SP, EW, "BDU", 0, 32)
+        if GHOSTQ == "S":
+            act(full("GS"), src, AF.Relu, bias=-2560.0)
+        else:
+            ts(full("GS"), src, -2560.0, OP.add, 0.0, OP.max)
+        send(nxt, prv, R("E", EW, EALL), full("GS"), "gArr%d" % w, "gLoc%d" % w, "cred%d" % w if w else None, REM + (0 if w else 2))
 
     ms(full("ONES"), 1.0)
-    ms(R("E", 272, EW), 0.0)
+    ms(R("E", 0, SP), 0.0)
+    ms(R("E", SP + 272, EW), 0.0)
     ts(full("FI"), full("F0"), 1, OP.add)
     ts(full("FA"), full("FI"), 4095, OP.bitwise_and)
-    cp(R("E", 0, 272), full("FA"))
+    cp(R("E", SP, SP + 272), full("FA"))
     cp(full("BDU"), full("BD"))
     ts(full("ISN"), full("F0"), 4095, OP.is_equal)
     ghosts(0)
-    send(prv, nxt, R("BT", 2561, 4096), R("BT", 1, 1 + H), "bArr", "bLoc")
-    iota(full("IO"), [[-1, 16]], 16, 1)
+    send(prv, nxt, R("BT", 2561, 4096), R("BT", 1, 1 + H), "bArr", "bLoc", None, REM + 2)
     iota(full("PI"), [[0, 1]], 0, 1)
     aff(full("BOA"), full("ONES"), [[-16, 8], [0, 16]], OP.is_ge, 0, 1)
     aff(full("BOF"), full("BOA"), [[16, 8], [0, 16]], OP.is_ge, 15, -1)
     aff(full("IF"), full("ONES"), [[-1, 128]], OP.is_equal, 0, 1)
     aff(full("UPF"), full("BOF"), [[1, 128]], OP.is_gt, 0, -1)
-    iota(full("IS"), [[16, 64]], DUMP, 0)
-    iota(full("CELLV"), [[1, 1024]], 64, 0)
-    iota(full("DEF"), [[1, 256]], DUMP + 64, 0)
+    iota(full("IO"), [[-1, 16]], 16, 1)
+    iota(full("JT"), [[16, 16]], 0, 0)
+    iota(full("JF"), [[1, 256]], 0, 0)
+    iota(R("CELL", 0, SP + C0), [[1, SP + C0]], -SP, 0)
+    iota(R("CELL", SP + C0, EW), [[1, NOWN - C0]], C0, 0)
     aff(full("S1F"), full("ONES"), [[1, 128]], OP.is_equal, -16, -1)
     aff(full("S2F"), full("ONES"), [[1, 128]], OP.is_equal, 16, -1)
     ts(full("IO2"), full("IO"), 15, OP.bitwise_and)
@@ -315,90 +366,106 @@ def rank_program(g, core, T, topo):
     ts(full("PV"), full("PQ"), 1, OP.bitwise_and)
     cp(full("PM"), full("PV"))
     ts(full("PN"), full("PM"), -1.0, OP.mult, 1.0, OP.add)
+    ts(full("PUW"), full("PUF"), 1536.0, OP.add)
+    ts(full("THF"), full("PUF"), 2048.0, OP.mult, 2048.0, OP.add)
+    ts(full("THL"), full("PUF"), -2048.0, OP.mult, 32768.0, OP.add)
+    ts(full("JT"), full("JT"), full("PUF"), OP.add)
+    ts(full("JB"), full("JT"), 0.5 - 2047.0, OP.add)
+    ts(full("J2"), full("JT"), float(EW), OP.add)
     bo8 = (T["BOF"][:, 0:128:16], [("BOF", 0, 128)])
-    for z, v in (("Z1", 1.0), ("Z0", WT), ("Z2", 2048.0), ("Z3", 6144.0)):
+    for z, v in (("Z1", 1.0), ("Z0", WT), ("ZU", full("PUW"))):
         ms(full(z), 0.0)
         ts((T[z][:, 15:143:16], [(z, 0, 144)]), bo8, v, OP.mult)
 
     def sel(z, p):
         return R(z, 15 - p, 143 - p)
 
-    mms(*[(R("F7", 0, 17), sel("Z1", c), R("ISN", c, 272, 16), c == 0, c == 15) for c in range(16)])
-    cp(full("BO"), full("BOF"))
-    ts(full("TF"), full("IF"), -2047.0, OP.mult)
+    mms(*summ(R("F6", 0, 17), *[(sel("Z1", c), R("ISN", c, 272, 16)) for c in range(16)]))
+    act(full("BO"), full("BOF"))
+    act(full("I16"), full("IF"))
+    ts(full("TF"), full("IF"), 2047.0, OP.mult)
     tt(full("TRI"), full("TF"), full("UPF"), OP.add)
-    ms(R("CS", 0, 1), 2047.0)
-    ts(full("CA"), full("IS"), full("PUF"), OP.add)
+    ms(R("CS", 0, 1), -2047.0)
     ms(full("AV"), 1.0)
-    ms(full("NE"), 0.0)
-    ms(full("WTL"), 1.0)
-    ts(R("AV", 0, 17), R("F7", 0, 17), 15.5, OP.is_gt)
-    ts(R("NE", 0, 17), R("F7", 0, 17), 15.5, OP.is_lt)
+    ms(full("N1"), 0.0)
+    ms(full("W1"), 1.0)
+    ms(full("U1"), -5000.0)
+    ms(R("NAT", 0, SP), 0)
+    ms(R("XA", 0, SP), -512.0)
+    ts(R("AV", 0, 17), R("F6", 0, 17), 15.5, OP.is_gt)
+    ts(R("N1", 0, 17), R("F6", 0, 17), 15.5, OP.is_lt, -64.0, OP.mult)
 
-    def front_a(w, ns):
-        mms((R("F6", 0, ns), full("TRI"), R("AV", 0, ns), True, True))
-        mms((R("F6", 64, 64 + ns), full("BO"), R("AV", 0, ns), True, True))
-        run("V", rds(R("ONES", 0, ns), R("F6", 64, 64 + ns)), [("CS", 1, 1 + ns)], 0.07,
-            [lambda: g.vector.tensor_tensor_scan(T["CS"][:, 1:1 + ns], T["ONES"][:, 0:ns], T["F6"][:, 64:64 + ns], 2047.0, OP.mult, OP.add)])
-        tt(R("U1", 0, ns), R("F6", 0, ns), R("CS", 0, ns), OP.add)
-        tt(R("OF", 0, ns), R("U1", 0, ns), R("CA", 0, ns), OP.min)
-        cp(R("OFU", 0, ns), R("OF", 0, ns))
-        act(R("IDXW", 0, 256), full("DEF"), AF.Copy)
-        act(IND("IDXW", 0, 2048, "OFU", 0, ns), R("CELLV", 0, 16 * ns), AF.Silu)
-        ts(R("INF", 0, ns), R("U1", 0, ns), 256.0, OP.is_lt)
-        tt(R("WTL", 0, ns), R("AV", 0, ns), R("INF", 0, ns), OP.subtract)
+    def front(w):
+        ns, k = NS[w], w % 2
+        hi = SP + 16 * ns
+        mms((R("F6", 64, 64 + ns), full("TRI"), R("AV", 0, ns), True, True),
+            (R("F6", 128, 128 + ns), full("BO"), R("AV", 0, ns), True, True))
+        run("V", rds(R("ONES", 0, ns), R("F6", 128, 128 + ns)), [("CS", 1, 1 + ns)], 64 * CY,
+            [lambda: g.vector.tensor_tensor_scan(T["CS"][:, 1:1 + ns], T["ONES"][:, 0:ns], T["F6"][:, 128:128 + ns], -2047.0, OP.mult, OP.add)])
+        tt(R("U1", 0, ns), R("F6", 64, 64 + ns), R("CS", 0, ns), OP.add)
+        for t in range(16):
+            act(R("JUNK", 64 * t, 64 * t + ns), R("CS", 1, 1 + ns), AF.Sign, bias=R("JB", t, t + 1), scale=-1.0, acc=R("SA", t, t + 1))
+        ts(full("SU"), full("SA"), 0.5, OP.mult, 0.5 * ns, OP.add)
+        ts(full("S16"), full("SA"), 8.0, OP.mult, 8.0 * ns + SP - 1536.0, OP.add)
+        tt(full("OH"), IND("U1", 0, 72, "SU", 0, 16), full("JF"), OP.is_equal)
+        mms(*[(R("F6", 208, 224), sel("ZU", c), R("OH", c, 256, 16), c == 0, False) for c in range(16)],
+            (R("F6", 208, 224), full("I16"), full("S16"), False, True))
+        tt(full("IXF%d" % k), R("F6", 208, 224), full("JT"), OP.max)
+        cp(full("IXU%d" % k), full("IXF%d" % k))
+        ts(R("W1", 0, ns), R("U1", 0, ns), 255.5, OP.is_gt)
+        ts(full("NF"), IND("NAT", 0, hi, "IXU%d" % k, 0, 16), -NOFF, OP.add)
+        ts(full("NAU"), full("NF"), NOFF, OP.add)
+        act(full("X%d" % k), IND("XA", 0, hi, "IXU%d" % k, 0, 16))
+        for i, q in enumerate(sorted(set(q for _, q in VPATH[w]))):
+            for p in range(16):
+                out = (R("XR%d" % k, 1024 * i + p, 1024 * i + 1024, 16)[0], [("XR%d" % k, 1024 * i + 64 * p, 1024 * i + 64 * p + 64)])
+                a = R("X%d" % k, 64 * q, 64 * q + 64)
+                if XRQ == "G":
+                    aff(out, a, [[0, 64]], OP.is_ge, 0, 0)
+                else:
+                    cp(out, a)
+        if w < WAVES - 1:
+            act(full("CF"), IND("CELL", 0, hi, "IXU%d" % k, 0, 16), bias=-NOFF)
 
-    def front_b(w):
-        hi = C0 if w == 0 else EW
-        ts(full("IDF"), R("IDXW", 0, 256), -64.0, OP.add)
-        ts(full("IDR"), R("IDXW", 0, 256), -63.75, OP.add)
-        mms(*[(R("F7", 0, 16), R("DG", c * 128, c * 128 + 128), R("IDF", c, 256, 16), c == 0, c == 15) for c in range(16)])
-        for k in range(4):
-            act(R("XR%d" % (w % 2), 1024 * k, 1024 * k + 1024), IND("XA", 0, hi, "IDR", 64 * k, 64 * k + 64), AF.Identity)
-        ts(full("IXU"), R("F7", 0, 16), 0.25, OP.add)
-        cp(full("NAU"), IND("NAT", 0, hi, "IXU", 0, 16))
-        cp(full("IXF"), full("IXU"))
-        cp(full("NAF"), full("NAU"))
+    def turned(bank, c, h, masked):
+        for o, k, nm, st in ((0, 128, "NF", 1), (128, 8, "CF", 16)):
+            pairs = [(hs(nm, h), R("I16", 0, 128, st))] + ([(hs("SEL", h), R("BOK", 0, 128, st))] if masked else [])
+            yield from summ(R(bank, c + o, c + o + k), *pairs)
 
-    def remap(lo, hi):
-        ts(R("NTMP", lo, hi), R("NAT", lo, hi), 1024, OP.is_ge, 256, OP.mult)
-        tt(R("NAT", lo, hi), R("NAT", lo, hi), R("NTMP", lo, hi), OP.add)
+    def low(w, h):
+        t = R("F6", 240 + FW * h, 240 + FW * h + FW)
+        mms(*turned("F6", 240 + FW * h, h, False))
+        ts(hs("H0", h, FW), t, M32, OP.add, -M32, OP.add)
+        tt(hs("LO", h, FW), t, hs("H0", h, FW), OP.subtract)
+        for j in range(32):
+            ts(R("LF%d" % h, FW * j, FW * j + FW), hs("LO", h, FW), j - 15.5, OP.is_equal)
 
-    front_a(0, NS0)
+    front(0)
     for c in range(16):
-        ts(R("DG", c * 128, c * 128 + 128), full("IF"), R("MK", c, c + 1), OP.mult)
-    remap(0, C0)
-    front_b(0)
+        if c % 2:
+            ts(R("DG", c * 128, c * 128 + 128), full("I16"), R("MK", c, c + 1), OP.mult)
+        else:
+            act(R("DG", c * 128, c * 128 + 128), full("IF"), scale=R("MK", c, c + 1))
     ms(full("MC"), MAG + 8.0)
     ms(R("BT", 4096, 4112), 512.0)
     ms(R("NBT", 4096, 4104), 4095)
-    ts(full("BOB"), full("BOF"), -12.5 * WT / 16, OP.mult)
+    act(full("BOB"), full("BOF"), scale=-12.5 * WT / 16)
+    act(full("BOK"), full("BOF"), scale=4096.0)
     ms(full("O16"), 1.0)
-    tt(full("QF"), full("UPF"), full("IF"), OP.subtract)
-    tt(full("TF"), full("BOF"), full("UPF"), OP.subtract)
-    tt(full("TF"), full("TF"), full("IF"), OP.subtract)
-    tt(full("QL"), full("TF"), full("IF"), OP.subtract)
+    tt(full("TG"), full("IF"), full("UPF"), OP.subtract)
+    act(full("QF"), full("TG"), scale=2048.0)
+    tt(full("TF"), full("UPF"), full("BOF"), OP.subtract)
+    tt(full("TF"), full("TF"), full("IF"), OP.add)
+    tt(full("TF"), full("TF"), full("IF"), OP.add)
+    act(full("QL"), full("TF"), scale=2048.0)
     ts(R("NBX", 0, H), R("NBT", 1, 1 + H), 1535, OP.min, 2560, OP.add)
-    send(prv, nxt, R("NBT", 2561, 4096), R("NBX", 0, H), "nArr", "nLoc")
-    ts(full("BON"), full("BOF"), -4096.0, OP.mult)
-    cp(full("I16"), full("IF"))
-    ts(full("DUMPR"), full("DEF"), -64.0, OP.add)
-    ts(R("SV", 0, 128), full("IF"), full("PN"), OP.mult)
-    ts(R("SV", 128, 256), full("S1F"), full("PN"), OP.mult)
-    ts(R("SV", 256, 384), full("S2F"), full("PM"), OP.mult)
-    ts(R("SV", 384, 512), full("IF"), full("PM"), OP.mult)
-    cp(full("DGB"), full("DG"))
-    cp(full("IB"), full("IF"))
-    ts(full("INB"), full("IF"), -1.0, OP.mult)
-    for w in range(4):
-        ms(R("MV", 256 * w, 256 * w + 256), 4.0 * w + 4.0)
-    ms(R("MV", 1024, 1280), 100.0)
-    ms(full("FL"), 0.0)
-    ms(full("FM"), 0.0)
-    ms(R("NAT", NOWN, EW), DUMP)
-    ms(R("XA", NOWN, EW), 0.0)
-    ms(R("YA", NOWN, EW), 0.0)
-    remap(C0, NOWN)
+    send(prv, nxt, R("NBT", 2561, 4096), R("NBX", 0, H), "nArr", "nLoc", None, REM + 3)
+    act(R("SV", 0, 128), full("IF"), scale=full("PN"))
+    act(R("SV", 128, 256), full("S2F"), scale=full("PM"))
+    act(R("SV", 256, 384), full("S1F"), scale=full("PN"))
+    act(R("SV", 384, 512), full("IF"), scale=full("PM"))
+    act(full("IB"), full("IF"))
+    act(full("INB"), full("IF"), scale=-1.0)
 
     def A(h):
         return "A%d" % h
@@ -406,173 +473,189 @@ def rank_program(g, core, T, topo):
     def B(h):
         return "B%dP" % h
 
-    def seeds(h, q):
-        o = h * 128 + q * 64
-        out = R(A(h), 64 * q, 64 * q + 64)
-        ts(R("SG", o * 16, o * 16 + 1024), IND("E", 0, EALL, "NAU", o, o + 64), -2048.0, OP.add)
-        mms(*[(out, R("DG", p * 128, p * 128 + 128), R("SG", o * 16 + p, o * 16 + 1024, 16), p == 0, p == 15) for p in range(16)])
+    turn = [0, 0]
 
-    def seeds_end(h):
-        ts(hs("CU", h), R(A(h), 0, 128), 2048.0, OP.add)
-        act(hs("PH", h), R(A(h), 0, 128), AF.Identity)
-        act(hs("CS0", h), R(A(h), 0, 128), AF.Identity, bias=-4096.0)
+    def seeds(w, q):
+        h, o = q // 2, q * 64
+        out = R(A(h), 64 * (q % 2), 64 * (q % 2) + 64)
+        add(SEEDQ[w][q], R("SG", o * 16, o * 16 + 1024), IND("E", SP, EALL, "NAU", o, o + 64), -2048.0)
+        mms(*summ(out, *[(R("DG", p * 128, p * 128 + 128), R("SG", o * 16 + p, o * 16 + 1024, 16)) for p in range(16)]))
+        ts(R("CU", o, o + 64), out, 2048.0, OP.add)
 
-    def near(w, t, h, q):
-        o = h * 128 + q * 64
+    def seeds_end(w, h):
+        act(hs("PH", h), R(A(h), 0, 128))
+        act(hs("CC", h), hs("PH", h), bias=2047.0 if w == WAVES - 1 else 2048.0)
+
+    def near(w, t, q):
+        h, o = q // 2, q * 64
         m = R("MC", w, w + 1)
-        xr = "XR%d" % (w % 2)
-        if (t, h, q) in ROUND_S:
-            act(full("BG"), IND("BT", 0, 4097, "CU", o, o + 64), AF.Identity)
-            for k, bank in enumerate(("M5", "F6")):
-                c = o * 16 + 512 * k
-                mms((R(bank, 0, 512), full("IB"), R("BG", 512 * k, 512 * k + 512), True, False),
-                    (R(bank, 0, 512), full("INB"), R(xr, c, c + 512), False, True))
-                ts(R("NR", c, c + 512), R(bank, 0, 512), m, OP.add, m, OP.is_equal)
+        src = IND("BT", 0, 4097, "CU", o, o + 64)
+        if (t, q) in VPATH[w]:
+            i = sorted(set(q for _, q in VPATH[w])).index(q)
+            tt(R("DD_", 1024 * i, 1024 * i + 1024), src, R("XR%d" % (w % 2), 1024 * i, 1024 * i + 1024), OP.subtract)
+            ts(R("NR", o * 16, o * 16 + 1024), R("DD_", 1024 * i, 1024 * i + 1024), m, OP.add, m, OP.is_equal)
+            rows = [R("NR", o * 16 + p, o * 16 + 1024, 16) for p in range(16)]
         else:
-            tt(R("DD_", o * 16, o * 16 + 1024), IND("BT", 0, 4097, "CU", o, o + 64), R(xr, o * 16, o * 16 + 1024), OP.subtract)
-            ts(R("NR", o * 16, o * 16 + 1024), R("DD_", o * 16, o * 16 + 1024), m, OP.add, m, OP.is_equal)
-        out = R(A(h), 64 * q, 64 * q + 64)
-        mms((out, full("BOB"), R("O16", 0, 64), True, False),
-            *[(out, sel("Z0", p), R("NR", o * 16 + p, o * 16 + 1024, 16), False, p == 15) for p in range(16)])
+            bg = "BG%d" % turn[0]
+            turn[0] ^= 1
+            act(full(bg), src)
+            for k in range(2):
+                bank = "D%d" % turn[1]
+                turn[1] ^= 1
+                grp = []
+                for p in range(8 * k, 8 * k + 8):
+                    grp += summ(R(bank, 64 * (p % 8), 64 * (p % 8) + 64), (full("IB"), R(bg, p, 1024, 16)),
+                                (full("INB"), R("X%d" % (w % 2), o, o + 64)))
+                mms(*grp)
+                ts(R("NR", o * 16 + 512 * k, o * 16 + 512 * k + 512), R(bank, 0, 512), m, OP.add, m, OP.is_equal)
+            rows = [R("NR", o * 16 + 64 * p, o * 16 + 64 * p + 64) for p in range(16)]
+        out = R(A(h), 64 * (q % 2), 64 * (q % 2) + 64)
+        mms(*summ(out, (full("BOB"), full("O16")), *[(sel("Z0", p), rows[p]) for p in range(16)]))
 
-    def seg1(w, t, h):
+    def pick(w, t, h):
         a = R(A(h), 0, 128)
-        ts(hs("V", h), a, 0.0, OP.is_gt)
-        mms((R(B(h), 0, 128), full("QF" if t == 0 else "QL"), hs("V", h), True, True))
-        if t == 0:
-            tt(hs("ACC", h), a, hs("CS0", h), OP.min)
-        elif t == 1:
-            tt(hs("M", h), a, hs("FN", h), OP.min)
-            tt(hs("ACC", h), hs("ACC", h), hs("M", h), OP.max)
+        if SIGNQ[t] == "S":
+            act(hs("SGN", h), a, AF.Sign)
         else:
-            tt(hs("M", h), a, hs("CS2", h), OP.min)
-            tt(hs("FIN", h), hs("Y", h), hs("M", h), OP.max)
-            ts(hs("FIA", h), hs("FIN", h), 4095, OP.bitwise_and)
-            cp(IND("YF" if w == WAVES - 1 else "E", 0, EW, "IXU", 8 * h, 8 * h + 8), hs("FIA", h))
+            ts(hs("SGN", h), a, 1.0, OP.min, -1.0, OP.max)
+        mms(*summ(R(B(h), 0, 128), (full("QF" if t == 0 else "QL"), hs("SGN", h)), (full("I16"), hs("PH" if t == 0 else "FN", h))))
+        ts(hs("RR", h), R(B(h), 0, 128), full("THF" if t == 0 else "THL"), OP.subtract, -2048.0, OP.max)
 
-    def seg2(w, t, h):
-        ts(hs("SEL", h), R(B(h), 0, 128), 0.0, OP.is_lt)
-        tt(hs("SELC", h), hs("SEL", h), hs("PH" if t == 0 else "FN", h), OP.mult)
-        out = R(B(h), 128, 136)
-        z = "Z2" if t == 0 else "Z3"
-        mms(*[(out, sel(z, c), R("SEL", 128 * h + c, 128 * h + 128, 16), c == 0, False) for c in range(16)],
-            *[(out, sel("Z1", c), R("SELC", 128 * h + c, 128 * h + 128, 16), False, c == 15) for c in range(16)])
-
-    def seg3(w, t, h):
-        x = R(B(h), 128, 136)
-        b = hs("BU", h, 8)
+    def keep(w, t, h):
+        a, m = R(A(h), 0, 128), R(A(h), 128, 256)
+        last = w == WAVES - 1
         if t == 0:
-            cp(b, x)
-            cp(hs("B0", h, 8), x)
-        else:
-            tt(hs("BC", h, 8), x, hs("B0" if t == 1 else "BI", h, 8), OP.max)
-            ts(hs("BI", h, 8), hs("BC", h, 8), 4095, OP.bitwise_and)
-            cp(b, hs("BI", h, 8))
-        if t < 2:
-            ts(hs("FN", h), IND("NBT", 0, 4097, "BU", 8 * h, 8 * h + 8), -2047.0, OP.add)
-            ts(hs("CU", h), hs("FN", h), 2048.0, OP.add)
-        if t == 1:
-            last = w == WAVES - 1
-            ts(hs("CS2", h), hs("FN", h), 10240.0 - (1.0 if last else 0.0), OP.add)
-            ts(hs("Y", h), hs("ACC", h), 6144.0, OP.add, 0.0, OP.max)
+            tt(hs("ACC", h), a, hs("CC", h), OP.min)
             if last:
-                ts(hs("Y", h), hs("Y", h), -1.0, OP.add)
+                ts(hs("ACC", h), hs("ACC", h), -1.0, OP.max)
+            return
+        tt(m, a, hs("CC", h), OP.min)
+        if t == 1:
+            tt(hs("ACC", h), m, hs("ACC", h), OP.max)
+        else:
+            tt(hs("FIN", h), m, hs("ACC", h), OP.max)
+            ts(hs("FIA", h), hs("FIN", h), 4095, OP.bitwise_and)
+            cp(IND("YF" if last else "E", 0, EW, "IXU%d" % (w % 2), 8 * h, 8 * h + 8), hs("FIA", h))
 
-    def idxs(w):
-        ts(full("TS"), full("B0"), 0.0, OP.is_equal, 4096.0, OP.mult)
-        tt(full("TS"), full("TS"), R("CA", 0, 16), OP.min)
-        tt(full("TS2"), full("TS"), full("IXF"), OP.max)
-        cp(full("ISU"), full("TS2"))
+    def step(w, t, h):
+        x = R(B(h), 128, 136)
+        bu = "BU%d" % t
+        mms(*summ(x, *[(sel("Z1", c), R("RR", 128 * h + c, 128 * h + 128, 16)) for c in range(16)]))
+        ts(hs(bu, h, 8), x, 32768.0, OP.add)
+        ts(hs("FN", h), IND("NBT", 0, 4097, bu, 8 * h, 8 * h + 8), -2047.0, OP.add)
+        ts(hs("CU", h), hs("FN", h), 2048.0, OP.add)
+
+    def level(w, t, h):
+        act(hs("CC", h), hs("FN", h), bias=2048.0 + 4096.0 * (t + 1) - (1.0 if w == WAVES - 1 else 0.0))
 
     def marks(w, h):
-        o = R("MP", 128 * h, 128 * h + 128)
-        mms((o, full("BON"), hs("SEL", h), True, False), (o, full("I16"), hs("DUMPR", h), False, True))
-        tt(hs("OFFS", h), o, hs("NAF", h), OP.max)
-        run("V", hs("OFFS", h)[1], hs("OT", h)[1], 0.07, [lambda: g.vector.transpose(hs("OT", h)[0], hs("OFFS", h)[0])])
-        grp = []
-        for v in range(2):
-            for b in range(4):
-                for k in range(2):
-                    z = (2 * v + k) * 128
-                    c = 128 * h + 32 * b + 16 * k
-                    grp.append((R("M5", 128 * h + 4 * v + b, 128 * h + 128, 8), R("SV", z, z + 128), R("OT", c, c + 16), k == 0, k == 1))
-        mms(*grp)
-        cp(hs("MO", h), R("M5", 128 * h, 128 * h + 128))
-        for p in range(16):
-            act(IND("FL" if p % 2 else "FM", 0, EALL, "MO", 128 * h + 8 * p, 128 * h + 8 * p + 8), R("MV", 256 * w, 256 * w + 128), AF.Silu)
+        nh = (NS[w] + 1) // 2
+        ts(hs("SEL", h), hs("RR", h), -2047.5, OP.is_gt)
+        mms(*turned(B(h), 256, h, True))
+        act(hs("HI", h, FW), R(B(h), 256, 256 + FW), bias=2048.0)
+        for i in range(nh):
+            ts(R("HF%d" % h, FW * i, FW * i + FW), hs("HI", h, FW), 6144.0 + 32.0 * (i - 24), OP.is_equal)
+        for gr in range(8):
+            grp = []
+            for kind, cols in ((0, range(16 * gr, 16 * gr + 16)), (1, [128 + gr])):
+                c0 = 128 * kind + 64 * h + 32 * (gr % 2)
+                out = R("MKP", c0, c0 + nh, 1, (32 * (gr // 2), 32 * (gr // 2) + 32))
+                grp += summ(out, *[(R("LF%d" % h, c, 32 * FW, FW), R("HF%d" % h, c, nh * FW, FW)) for c in cols])
+            mms(*grp)
 
-    def succeeded(w):
-        act(IND("FL", 0, EALL, "ISU", 0, 16), R("MV", 1024, 1280), AF.Silu)
-        act(full("FMB"), R("FM", 0, NOWN), AF.Copy)
-        act(full("FLB"), R("FL", 0, NOWN), AF.Copy)
+    def flags(w):
+        nh = (NS[w] + 1) // 2
+        if nh == 32:
+            act(R("MS", 0, 128), R("MKP", 0, 128))
+            act(R("MS", 128, 256), R("MKP", 128, 256), scale=-32.0)
+        else:
+            for k in range(8):
+                act(R("MS", 32 * k, 32 * k + nh), R("MKP", 32 * k, 32 * k + nh), scale=-32.0 if k >= 4 else 1.0)
+        grp = []
+        for a1 in range(2):
+            pairs = [(full("I16"), R("W1", a1, 2 * nh, 2)), (full("I16"), R("N1", a1, 2 * nh, 2))]
+            pairs += [(hs("SV", 2 * (k % 2) + a1), R("MS", 32 * k, 32 * k + nh)) for k in range(8)]
+            grp += summ(R("F6", a1, 2 * nh, 2), *pairs)
+        if nh < 32:
+            grp += summ(R("F6", 2 * nh, 64), (full("I16"), R("W1", 2 * nh, 64)), (full("I16"), R("N1", 2 * nh, 64)))
+        mms(*grp)
+        ts(full("AV"), R("F6", 0, 64), 0.5, OP.is_gt)
+        ts(full("N1"), R("F6", 0, 64), -8.0, OP.is_lt, -64.0, OP.mult)
 
     def parity(w):
-        ts(full("PC"), full("B0"), 0.0, OP.is_gt)
-        run("V", rds(full("PC")), [("PR", 0, 1)], 0.07,
-            [lambda: g.vector.tensor_reduce(T["PR"][:, 0:1], T["PC"][:, 0:16], axis=AxisListType.X, op=OP.add)])
-        cp(full("PR16"), full("PR"))
-        mms((R("F7", 64, 65), full("O16"), full("PR16"), True, True))
-        cp(full("PINT"), R("F7", 64, 65))
+        act(full("PC"), full("B0"), AF.Sign, bias=-0.5, acc=full("PR"))
+        mms((R("MKP", 256, 257), full("ONES"), full("PR"), True, True))
+        ts(full("PINT"), R("MKP", 256, 257), 0.5, OP.mult, 1024.0, OP.add)
         ts(full("PINT"), full("PINT"), 1, OP.bitwise_and)
         ts(R("MC", w + 1, w + 2), full("PINT"), -8.0, OP.mult, MAG + 8.0, OP.add)
 
-    def front_c(w):
-        for nm, k in (("FMB", 192), ("FLB", 128)):
-            mms(*[(R("F6", k, k + 64), R("DGB", c * 128, c * 128 + 128), R(nm, c, 1024, 16), c == 0, c == 15) for c in range(16)])
-        c = R("F6", 128, 192)
-        ts(full("T3"), R("F6", 192, 256), 4.0 * w + 2.0, OP.is_gt)
-        ts(full("T2"), c, 4.0 * w + 2.0, OP.is_gt)
-        ts(full("NT"), c, 60.0, OP.is_ge)
-        tt(full("XX"), full("WTL"), full("T3"), OP.max)
-        tt(full("XX"), full("XX"), full("T2"), OP.max)
-        tt(full("NE"), full("NE"), full("NT"), OP.max)
-        tt(full("AV"), full("XX"), full("NE"), OP.is_gt)
-        front_a(w + 1, 64)
+    def idxs(w):
+        cp(full("B0"), full("BU0"))
+        ts(full("TS"), full("B0"), 0.0, OP.is_equal, 4096.0, OP.mult)
+        tt(full("TS"), full("TS"), full("IXF%d" % (w % 2)), OP.max)
+        tt(full("TS2"), full("TS"), full("J2"), OP.min)
+        cp(full("ISU"), full("TS2"))
 
-    def numbers(w, h):
-        x = R("XR%d" % (w % 2), 2048 * h, 2048 * h + 2048, 16)
-        tt(hs("DX", h), IND("BT", 0, 4097, "BU", 8 * h, 8 * h + 8), x, OP.subtract)
-        ts(hs("CL", h), hs("DX", h), -2.0, OP.max, 2.0, OP.min)
-        tt(hs("NX", h), hs("CL", h), x, OP.add)
-        cp(IND("YA", 0, EW, "ISU", 8 * h, 8 * h + 8), hs("NX", h))
+    def newer(out, key, old):
+        tt(full("K2"), key, old, OP.max)
+        ts(out, full("K2"), 4095, OP.bitwise_and)
+
+    def numbers(w):
+        x = R("B1P", 136, 152)
+        mms(*summ(x, *[(sel("Z1", c), R("RR", c, 256, 16)) for c in range(16)]))
+        ts(full("K1"), x, 32768.0, OP.add, 4097.0, OP.mult)
+        newer(full("K1"), full("K1"), full("K3"))
+        cp(full("BU2"), full("K1"))
+        xs = full("X%d" % (w % 2))
+        tt(full("DX"), IND("BT", 0, 4097, "BU2", 0, 16), xs, OP.subtract)
+        ts(full("CL"), full("DX"), -2.0, OP.max, 2.0, OP.min)
+        tt(IND("XA", 0, 1536, "ISU", 0, 16), full("CL"), xs, OP.add)
 
     for w in range(WAVES):
         last = w == WAVES - 1
+        if last:
+            for k in range(2):
+                e, y = R("E", SP + 512 * k, SP + 512 * k + 512), R("YF", SP + 512 * k, SP + 512 * k + 512)
+                act(y, e, bias=-1.0)
+                act(R("D%d" % k, 0, 512), e, bias=4095.0, scale=-5000.0)
+                tt(y, R("D%d" % k, 0, 512), y, OP.max)
         for h in range(2):
-            seeds(h, 0)
-            seeds(h, 1)
-            seeds_end(h)
+            seeds(w, 2 * h)
+            seeds(w, 2 * h + 1)
+            seeds_end(w, h)
         if not last:
             credit(w + 1)
-        else:
-            act(R("YF", 0, NOWN), R("E", 0, NOWN), AF.Identity, bias=-1.0)
-            act(full("YT"), R("E", 0, NOWN), AF.Identity, bias=4095.0, scale=-5000.0)
-            tt(R("YF", 0, NOWN), R("YF", 0, NOWN), full("YT"), OP.max)
+            low(w, 0)
+            low(w, 1)
         for t in range(3):
             for h in range(2):
-                near(w, t, h, 0)
-                near(w, t, h, 1)
-                seg1(w, t, h)
-                seg2(w, t, h)
+                near(w, t, 2 * h)
+                near(w, t, 2 * h + 1)
+                if t == 2:
+                    keep(w, t, h)
+                pick(w, t, h)
+                if t < 2:
+                    step(w, t, h)
+                    keep(w, t, h)
+                    level(w, t, h)
                 if t == 0 and not last:
                     marks(w, h)
-                seg3(w, t, h)
             if t == 0:
                 idxs(w)
                 if not last:
-                    succeeded(w)
                     parity(w)
-                    front_c(w)
+                    flags(w)
+                    front(w + 1)
+            if t == 1:
+                ts(full("K1"), full("BU1"), 4097.0, OP.mult)
+                newer(full("K3"), full("K1"), full("B0"))
             if t == 2:
                 if not last:
                     ghosts(w + 1)
                 else:
-                    store("Y", "oF", T.yf[:], R("YF", 0, NOWN))
-                numbers(w, 0)
-                numbers(w, 1)
-                if not last:
-                    front_b(w + 1)
-    store("Y", "oA", T.ya[:], R("YA", 0, NOWN))
+                    store("Y", "oF", T.yf[:], R("YF", SP, EW))
+                numbers(w)
+    store("Y", "oA", T.ya[:], R("XA", SP, EW))
     issue()
 
     for s in "VSPG":

@@ -13,38 +13,49 @@ M32 = 402653184.0
 WT = 32768.0
 NOFF = 783.5
 FW = 136
-CY, GC, SC, PEC = 0.00095, 1.56, 3.8, 0.0005
-LOOK, REM, WAKE = 0.05, 3.5, 0.06
-SEEDQ = ("SSVS", "SSVS", "SSVS", "SSVS", "SVSV")
-VPATH = (((0, 1), (1, 1), (2, 1)),) * 4 + (((0, 1), (1, 1), (2, 1), (0, 3), (1, 3), (2, 3)),)
+CY, GC, SC = 0.00092, 1.56, 3.8
+PEC = 0.00052
+LOOK = 0.05
+REM = 3.5
+WAKE = 0.1
+SEEDQ = ("VSVS", "VSVS", "VSVS", "VSVS", "SVSV")
+VPATH = (((0, 1), (1, 1), (2, 1), (2, 3)),) * 4 + (((0, 1), (1, 1), (2, 1), (0, 3), (1, 3), (2, 3)),)
 SIGNQ = "SSS"
 GHOSTQ = "S"
-XRQ = "G"
-PASSES = 8
+DPATH = ((),) * 5
+XRUNS = (((1,), (3,)),) * 5
+ACCL = 3.5
+SCAN = True
+PUTS = ((0, 2), (2, 3), (3, 4))
+LOWS = (31, 31, 31, 31)
+LEAD = {}
+EARLY = 0.0
+NOISE = 1.0
+PASSES = 30
 ORDER = []
 
 SIZE = {"float32": 4, "int32": 4, "bfloat16": 2, "float16": 2, "uint16": 2}
 SCRATCH = {}
 for _d, _l in (
-        ("bfloat16", "BT 4112 XA 1536 XR0 2048 XR1 2048 X0 256 X1 256 BG0 1024 BG1 1024 IB 128 INB 128 CL 256 HI 272"),
-        ("int32", "NBT 4104 NBX 1536 NAT 1280 F0 272 FI 272 FA 272 BD 32 IO 16 IO2 16 PI 1 PU 1 PQ 1 PV 1 FIN 256 FIA 256 "
+        ("bfloat16", "BT 4112 XA 1536 XR0 4096 XR1 4096 X0 256 X1 256 XN 256 BH 4096 BG0 1024 BG1 1024 IB 128 INB 128 CL 256 HI 272"),
+        ("int32", "NBT 4104 NBX 1536 NAT 1280 F0 272 FI 272 FA 272 BD 32 IO 16 PI 1 PU 1 PQ 1 FIN 256 FIA 256 "
                   "K1 16 K2 16 K3 16 PINT 1"),
         ("uint16", "BDU 32 IXU0 16 IXU1 16 SU 16 NAU 256 CU 256 BU0 16 BU1 16 BU2 16 ISU 16"),
         ("float16", "SG 4096 DD_ 2048 NR 4096 ISN 272 BO 128 BOB 128 BOK 128 I16 128 TRI 128 QF 128 QL 128 O16 64 SV 512 DG 2048 "
-                    "Z0 144 Z1 144 ZU 144 AV 64 W1 64 N1 64 SGN 256 SEL 256 RR 256 PH 256 FN 256 DX 256 NF 256 CF 256 OH 256 S16 16 "
+                    "Z0 144 Z1 144 ZU 144 AV 64 W1 64 N1 64 SGN 256 SEL 256 RR 256 NM 64 LM 128 FN 256 DX 256 NF 256 CF 256 OH 256 S16 16 "
                     "H0 272 LO 272 LF0 4352 LF1 4352 HF0 4352 HF1 4352 MS 1024"),
         ("float32", "E 1792 YF 1280 GS 512 CELL 1280 JF 256 JT 16 JB 16 J2 16 ONES 128 BOA 128 BOF 128 IF 128 UPF 128 S1F 128 S2F 128 "
                     "TF 128 TG 128 MK 16 PUF 1 PUW 1 PM 1 PN 1 THF 1 THL 1 MC 8 CS 65 U1 72 JUNK 1024 SA 16 IXF0 16 IXF1 16 "
-                    "CC 256 ACC 256 B0 16 TS 16 TS2 16 PC 16 PR 1")):
+                    "CC 256 ACC 256 SCN 256 RST 64 B0 16 TS 16 TS2 16 PC 16 PR 1")):
     _l = _l.split()
     for _i in range(0, len(_l), 2):
         SCRATCH[_l[_i]] = ("sbuf", [128, int(_l[_i + 1])], _d)
-PSUM = ("A0", "A1", "B0P", "B1P", "D0", "D1", "MKP", "F6")
+PSUM = ("A0", "A1", "A2", "A3", "D0", "D1", "MKP", "F6")
 for _n in PSUM:
     SCRATCH[_n] = ("psum", [128, 512], "float32")
 
 LOADS = ("f0", "bd", "naA", "xaA", "xbA", "xbB", "nbA", "nbB", "naB", "xaB", "oF", "oA")
-SEMAPHORES = (["cV", "cS", "cP", "cG", "bArr", "nArr", "bLoc", "nLoc", "crLoc"] + ["d_" + x for x in LOADS]
+SEMAPHORES = (["cV", "cS", "cP", "cG", "bArr", "nArr", "bLoc", "nLoc", "crLoc", "acc0", "acc1", "acc2", "acc3"] + ["d_" + x for x in LOADS]
               + ["gArr%d" % w for w in range(WAVES)] + ["gLoc%d" % w for w in range(WAVES)] + ["cred%d" % w for w in range(1, WAVES)])
 
 
@@ -60,6 +71,7 @@ def rank_program(g, core, T, topo):
     know = {}
     wr, rd = {}, {}
     ops = []
+    early = {}
     loads = {}
 
     def need(q, tok):
@@ -97,7 +109,8 @@ def rank_program(g, core, T, topo):
             rd[nm] = [e for e in rd.get(nm, ()) if not (e[2] == q and lo <= e[0] and e[1] <= hi)] + [(lo, hi, q, tok)]
 
     def op(q, reads, writes, cost, lat, emit, after=()):
-        ops.append((q, reads, writes, cost, lat, emit, tuple(after)))
+        lead = LEAD.get(writes[0][0].rstrip("0123") if writes else "", 0.0)
+        ops.append((q, reads, writes, cost, lat, emit, tuple(after), lead))
         return len(ops) - 1
 
     def waits(q, reads, writes, dma=False):
@@ -128,14 +141,18 @@ def rank_program(g, core, T, topo):
                 d[j] = d.get(j, False) or strong
             for j in o[6]:
                 d[j] = True
+            for j, k in same:
+                if k == i:
+                    d[j] = d.get(j, False)
             dep.append(d)
             for j in d:
                 succ[j].append(i)
             note(o[0], o[1], o[2], i, w2, r2)
         fwd = [[(j, ops[i][4] + WAKE if dep[j][i] else 0.0) for j in succ[i]] for i in range(len(dep))]
-        bwd = [[(j, ops[j][4] + WAKE if dep[i][j] else 0.0) for j in dep[i]] for i in range(len(dep))]
+        bwd = [[(j, (ops[j][4] + WAKE if dep[i][j] else 0.0) + early.get(j, 0.0)) for j in dep[i]] for i in range(len(dep))]
 
-        def sweep(edges, pri):
+        def sweep(edges, pri, sign):
+            pri = [p + sign * o[7] for p, o in zip(pri, ops)]
             left = [0] * m
             for e in edges:
                 for j, _ in e:
@@ -164,13 +181,17 @@ def rank_program(g, core, T, topo):
         if not ORDER:
             pri = [0.0] * m
             for i in range(m - 1, -1, -1):
-                pri[i] = ops[i][3] + max([pri[j] + lag for j, lag in fwd[i]] + [0.0])
-            best = None
-            for _ in range(PASSES):
-                order, end = sweep(fwd, pri)
+                pri[i] = ops[i][3] + max([pri[j] + lag for j, lag in fwd[i]] + [0.0]) + early.get(i, 0.0)
+            best, x = None, 1
+            for k in range(PASSES):
+                order, end = sweep(fwd, pri, 1.0)
                 if best is None or max(end) < best[0]:
-                    best = (max(end), order)
-                pri = sweep(bwd, end)[1]
+                    best = (max(end), order, end)
+                key = []
+                for e in best[2]:
+                    x = (x * 1103515245 + 12345) % 2147483648
+                    key.append(e + (NOISE * x / 2147483648 if k else 0.0))
+                pri = sweep(bwd, key, 0.0)[1]
             ORDER.extend(best[1])
         for i in ORDER:
             ops[i][5]()
@@ -267,24 +288,39 @@ def rank_program(g, core, T, topo):
         kw = {} if SCRATCH[out[1][0][0]][2] == "int32" else {"allow_small_or_imprecise_dtypes": True}
         run("G", [], out[1], 0.13 + 2 * CY * width(out), [lambda: g.iota(out[0], pattern, base, cm, **kw)])
 
-    def load(q, sem, out, in_ap, after=(), fills=()):
+    def load(q, sem, out, in_ap, lat, fills=(), written=(), sent=()):
         nm, lo, hi = out[1][0]
 
         def emit():
-            for k in after:
-                need(q, ("d_" + k, 16))
+            waits(q, list(written), list(sent), True)
             if fills:
                 waits(q, [], [(nm, 0, hi)], True)
             tok = ("d_" + sem, 16)
             know[tok] = dict(seen[q])
             Q[q].dma_start(out[0], in_ap).then_inc(T.sem["d_" + sem], 16)
             note("dma", [], out[1], tok, wr, rd)
-        queued[0] += (hi - lo) * SIZE[SCRATCH[nm][2]] * 128 / 200e3
-        prev = list(loads.values())[-1:] if q == "Y" else []
-        loads[sem] = op(q, [], out[1], 0.05, 1.8 + queued[0], emit, [loads[k] for k in after] + list(fills))
-        chain.append(loads[sem])
+        before = [loads[q]] if q in loads else []
+        loads[q] = op(q, list(written), out[1] + list(sent), 0.05, lat, emit, list(fills))
+        early[loads[q]] = 0.0
+        for j in before:
+            same.append((j, loads[q]))
 
-    queued, chain = [0.0], []
+    same = []
+
+    nacc = [0] * 4
+
+    def accum(q, out, a):
+        def emit():
+            waits("G", out[1] + a[1], out[1], True)
+            nacc[q] += 16
+            tok = ("acc%d" % q, nacc[q])
+            know[tok] = dict(seen["G"])
+            g.dma_start(out[0], a[0], accum_op=OP.add).then_inc(T.sem[tok[0]], 16)
+            note("dma", a[1], out[1], tok, wr, rd)
+        op("G", out[1] + a[1], out[1], 1.0, ACCL, emit)
+
+    def wide(w):
+        return [q for r in XRUNS[w] for q in r]
 
     def store(q, sem, out_ap, a):
         def emit():
@@ -317,16 +353,11 @@ def rank_program(g, core, T, topo):
         op("G", [], [("E", EW, EALL)], 0.3, 2.0, emit)
 
     fb, fn = ms(R("BT", 0, 16), 512.0), ms(R("NBT", 0, 8), 4095)
-    load("Y", "f0", full("F0"), T.f0[:])
-    load("S", "bd", full("BD"), T.bd[:])
-    load("Y", "naA", R("NAT", SP, SP + C0), T.nba[:, 0:C0])
-    load("S", "xaA", R("XA", SP, SP + C0), T.xa[:, 0:C0])
-    load("Y", "xbA", R("BT", 1, 1 + H), T.xb[:, 0:H], (), [fb])
-    load("Y", "xbB", R("BT", 1 + H, 1 + NB_), T.xb[:, H:NB_], ["f0"])
-    load("Y", "nbA", R("NBT", 1, 1 + H), T.nbb[:, 0:H], (), [fn])
-    load("Y", "nbB", R("NBT", 1 + H, 1 + NB_), T.nbb[:, H:NB_], ["xbA"])
-    load("Y", "naB", R("NAT", SP + C0, EW), T.nba[:, C0:NOWN], ["xbA"])
-    load("Y", "xaB", R("XA", SP + C0, EW), T.xa[:, C0:NOWN], ["xbA"])
+    load("Y", "f0", full("F0"), T.f0[:], 2.5)
+    load("S", "bd", full("BD"), T.bd[:], 2.5)
+    load("Y", "xbA", R("BT", 1, 1 + H), T.xb[:, 0:H], 4.5, [fb])
+    load("Y", "naA", R("NAT", SP, SP + C0), T.nba[:, 0:C0], 5.8)
+    load("Y", "xaA", R("XA", SP, SP + C0), T.xa[:, 0:C0], 6.4)
 
     def ghosts(w):
         src = IND("E", SP, EW, "BDU", 0, 32)
@@ -334,7 +365,7 @@ def rank_program(g, core, T, topo):
             act(full("GS"), src, AF.Relu, bias=-2560.0)
         else:
             ts(full("GS"), src, -2560.0, OP.add, 0.0, OP.max)
-        send(nxt, prv, R("E", EW, EALL), full("GS"), "gArr%d" % w, "gLoc%d" % w, "cred%d" % w if w else None, REM + (0 if w else 2))
+        send(nxt, prv, R("E", EW, EALL), full("GS"), "gArr%d" % w, "gLoc%d" % w, "cred%d" % w if w else None, REM + (0 if w else 1))
 
     ms(full("ONES"), 1.0)
     ms(R("E", 0, SP), 0.0)
@@ -345,7 +376,12 @@ def rank_program(g, core, T, topo):
     cp(full("BDU"), full("BD"))
     ts(full("ISN"), full("F0"), 4095, OP.is_equal)
     ghosts(0)
-    send(prv, nxt, R("BT", 2561, 4096), R("BT", 1, 1 + H), "bArr", "bLoc", None, REM + 2)
+    send(prv, nxt, R("BT", 2561, 4096), R("BT", 1, 1 + H), "bArr", "bLoc", None, REM + 1)
+    load("Y", "xbB", R("BT", 1 + H, 1 + NB_), T.xb[:, H:NB_], 3.1, written=full("GS")[1])
+    load("Y", "nbA", R("NBT", 1, 1 + H), T.nbb[:, 0:H], 5.8, [fn], sent=full("GS")[1])
+    load("Y", "nbB", R("NBT", 1 + H, 1 + NB_), T.nbb[:, H:NB_], 8.5)
+    load("Y", "naB", R("NAT", SP + C0, EW), T.nba[:, C0:NOWN], 6.0, written=R("NBT", 1 + H, 1 + NB_)[1])
+    load("Y", "xaB", R("XA", SP + C0, EW), T.xa[:, C0:NOWN], 6.5)
     iota(full("PI"), [[0, 1]], 0, 1)
     aff(full("BOA"), full("ONES"), [[-16, 8], [0, 16]], OP.is_ge, 0, 1)
     aff(full("BOF"), full("BOA"), [[16, 8], [0, 16]], OP.is_ge, 15, -1)
@@ -358,13 +394,12 @@ def rank_program(g, core, T, topo):
     iota(R("CELL", SP + C0, EW), [[1, NOWN - C0]], C0, 0)
     aff(full("S1F"), full("ONES"), [[1, 128]], OP.is_equal, -16, -1)
     aff(full("S2F"), full("ONES"), [[1, 128]], OP.is_equal, 16, -1)
-    ts(full("IO2"), full("IO"), 15, OP.bitwise_and)
+    ts(full("IO"), full("IO"), 15, OP.bitwise_and)
     ts(full("PU"), full("PI"), 15, OP.bitwise_and)
-    ts(full("PQ"), full("PI"), 4, OP.logical_shift_right)
+    ts(full("PQ"), full("PI"), 16, OP.bitwise_and)
     cp(full("PUF"), full("PU"))
-    ts(full("MK"), full("IO2"), 0, OP.is_equal)
-    ts(full("PV"), full("PQ"), 1, OP.bitwise_and)
-    cp(full("PM"), full("PV"))
+    ts(full("MK"), full("IO"), 0, OP.is_equal)
+    ts(full("PM"), full("PQ"), 0, OP.is_gt)
     ts(full("PN"), full("PM"), -1.0, OP.mult, 1.0, OP.add)
     ts(full("PUW"), full("PUF"), 1536.0, OP.add)
     ts(full("THF"), full("PUF"), 2048.0, OP.mult, 2048.0, OP.add)
@@ -415,15 +450,17 @@ def rank_program(g, core, T, topo):
         ts(R("W1", 0, ns), R("U1", 0, ns), 255.5, OP.is_gt)
         ts(full("NF"), IND("NAT", 0, hi, "IXU%d" % k, 0, 16), -NOFF, OP.add)
         ts(full("NAU"), full("NF"), NOFF, OP.add)
+        early[len(ops) - 1] = EARLY if w else 0.0
         act(full("X%d" % k), IND("XA", 0, hi, "IXU%d" % k, 0, 16))
-        for i, q in enumerate(sorted(set(q for _, q in VPATH[w]))):
+        act(full("XN"), full("X%d" % k), scale=-1.0)
+        i = 0
+        for run_ in XRUNS[w]:
+            m = len(run_)
             for p in range(16):
-                out = (R("XR%d" % k, 1024 * i + p, 1024 * i + 1024, 16)[0], [("XR%d" % k, 1024 * i + 64 * p, 1024 * i + 64 * p + 64)])
-                a = R("X%d" % k, 64 * q, 64 * q + 64)
-                if XRQ == "G":
-                    aff(out, a, [[0, 64]], OP.is_ge, 0, 0)
-                else:
-                    cp(out, a)
+                out = (R("XR%d" % k, 1024 * i + p, 1024 * (i + m), 16)[0],
+                       [("XR%d" % k, 1024 * j + 64 * p, 1024 * j + 64 * p + 64) for j in range(i, i + m)])
+                aff(out, R("XN", 64 * run_[0], 64 * (run_[0] + m)), [[0, 64 * m]], OP.is_ge, 0, 0)
+            i += m
         if w < WAVES - 1:
             act(full("CF"), IND("CELL", 0, hi, "IXU%d" % k, 0, 16), bias=-NOFF)
 
@@ -437,8 +474,12 @@ def rank_program(g, core, T, topo):
         mms(*turned("F6", 240 + FW * h, h, False))
         ts(hs("H0", h, FW), t, M32, OP.add, -M32, OP.add)
         tt(hs("LO", h, FW), t, hs("H0", h, FW), OP.subtract)
-        for j in range(32):
-            ts(R("LF%d" % h, FW * j, FW * j + FW), hs("LO", h, FW), j - 15.5, OP.is_equal)
+        for j in range(1, 32):
+            out = R("LF%d" % h, FW * j, FW * j + FW)
+            if j <= LOWS[w]:
+                act(out, hs("LO", h, FW), AF.Sigmoid, bias=-128.0 * (j - 16), scale=128.0)
+            else:
+                ts(out, hs("LO", h, FW), j - 16.0, OP.is_gt)
 
     front(0)
     for c in range(16):
@@ -452,6 +493,10 @@ def rank_program(g, core, T, topo):
     act(full("BOB"), full("BOF"), scale=-12.5 * WT / 16)
     act(full("BOK"), full("BOF"), scale=4096.0)
     ms(full("O16"), 1.0)
+    ms(full("RST"), 60000.0)
+    ms(R("RST", 0, 64, 16), -60000.0)
+    for k in range(4):
+        ts(hs("NM", k, 16), full("MK"), 32768.0, OP.mult, -32768.0, OP.add)
     tt(full("TG"), full("IF"), full("UPF"), OP.subtract)
     act(full("QF"), full("TG"), scale=2048.0)
     tt(full("TF"), full("UPF"), full("BOF"), OP.subtract)
@@ -459,41 +504,55 @@ def rank_program(g, core, T, topo):
     tt(full("TF"), full("TF"), full("IF"), OP.add)
     act(full("QL"), full("TF"), scale=2048.0)
     ts(R("NBX", 0, H), R("NBT", 1, 1 + H), 1535, OP.min, 2560, OP.add)
-    send(prv, nxt, R("NBT", 2561, 4096), R("NBX", 0, H), "nArr", "nLoc", None, REM + 3)
+    send(prv, nxt, R("NBT", 2561, 4096), R("NBX", 0, H), "nArr", "nLoc", None, REM + 1.5)
     act(R("SV", 0, 128), full("IF"), scale=full("PN"))
     act(R("SV", 128, 256), full("S2F"), scale=full("PM"))
     act(R("SV", 256, 384), full("S1F"), scale=full("PN"))
     act(R("SV", 384, 512), full("IF"), scale=full("PM"))
+    aff(full("BOA"), full("ONES"), [[0, 4], [1, 32]], OP.not_equal, 0, 0)
+    aff(full("BOA"), full("BOA"), [[1, 128]], OP.is_equal, -1, -1)
+    tt(full("LM"), full("IF"), full("BOA"), OP.subtract)
+    mms((R("D0", 0, 512), full("LM"), full("SV"), True, True))
+    act(full("SV"), R("D0", 0, 512))
+    for h in range(2):
+        ms(R("LF%d" % h, 0, FW), 1.0)
     act(full("IB"), full("IF"))
     act(full("INB"), full("IF"), scale=-1.0)
 
-    def A(h):
-        return "A%d" % h
+    def A(q, k):
+        return R("A%d" % q, 64 * k, 64 * k + 64)
 
-    def B(h):
-        return "B%dP" % h
+    def qs(nm, q):
+        return hs(nm, q, 64)
 
     turn = [0, 0]
 
     def seeds(w, q):
-        h, o = q // 2, q * 64
-        out = R(A(h), 64 * (q % 2), 64 * (q % 2) + 64)
+        o = q * 64
         add(SEEDQ[w][q], R("SG", o * 16, o * 16 + 1024), IND("E", SP, EALL, "NAU", o, o + 64), -2048.0)
-        mms(*summ(out, *[(R("DG", p * 128, p * 128 + 128), R("SG", o * 16 + p, o * 16 + 1024, 16)) for p in range(16)]))
-        ts(R("CU", o, o + 64), out, 2048.0, OP.add)
+        mms(*summ(A(q, 0), *[(R("DG", p * 128, p * 128 + 128), R("SG", o * 16 + p, o * 16 + 1024, 16)) for p in range(16)]))
+        ts(qs("CU", q), A(q, 0), 2048.0, OP.add)
 
-    def seeds_end(w, h):
-        act(hs("PH", h), R(A(h), 0, 128))
-        act(hs("CC", h), hs("PH", h), bias=2047.0 if w == WAVES - 1 else 2048.0)
+    def level(w, t, h):
+        ts(hs("FN", h), hs("CU", h), -2048.0, OP.add)
+        act(hs("CC", h), hs("FN", h), bias=2048.0 + 4096.0 * t - (1.0 if w == WAVES - 1 else 0.0))
 
     def near(w, t, q):
-        h, o = q // 2, q * 64
+        o = q * 64
         m = R("MC", w, w + 1)
         src = IND("BT", 0, 4097, "CU", o, o + 64)
         if (t, q) in VPATH[w]:
-            i = sorted(set(q for _, q in VPATH[w])).index(q)
-            tt(R("DD_", 1024 * i, 1024 * i + 1024), src, R("XR%d" % (w % 2), 1024 * i, 1024 * i + 1024), OP.subtract)
-            ts(R("NR", o * 16, o * 16 + 1024), R("DD_", 1024 * i, 1024 * i + 1024), m, OP.add, m, OP.is_equal)
+            i = wide(w).index(q)
+            d = R("DD_", 1024 * (q % 2), 1024 * (q % 2) + 1024)
+            tt(d, src, R("XR%d" % (w % 2), 1024 * i, 1024 * i + 1024), OP.add)
+            ts(R("NR", o * 16, o * 16 + 1024), d, m, OP.add, m, OP.is_equal)
+            rows = [R("NR", o * 16 + p, o * 16 + 1024, 16) for p in range(16)]
+        elif (t, q) in DPATH[w]:
+            i = wide(w).index(q)
+            d = R("BH", 1024 * q, 1024 * q + 1024)
+            act(d, src)
+            accum(q, d, R("XR%d" % (w % 2), 1024 * i, 1024 * i + 1024))
+            ts(R("NR", o * 16, o * 16 + 1024), d, m, OP.add, m, OP.is_equal)
             rows = [R("NR", o * 16 + p, o * 16 + 1024, 16) for p in range(16)]
         else:
             bg = "BG%d" % turn[0]
@@ -509,50 +568,48 @@ def rank_program(g, core, T, topo):
                 mms(*grp)
                 ts(R("NR", o * 16 + 512 * k, o * 16 + 512 * k + 512), R(bank, 0, 512), m, OP.add, m, OP.is_equal)
             rows = [R("NR", o * 16 + 64 * p, o * 16 + 64 * p + 64) for p in range(16)]
-        out = R(A(h), 64 * (q % 2), 64 * (q % 2) + 64)
-        mms(*summ(out, (full("BOB"), full("O16")), *[(sel("Z0", p), rows[p]) for p in range(16)]))
+        mms(*summ(A(q, 0), (full("BOB"), full("O16")), *[(sel("Z0", p), rows[p]) for p in range(16)]))
 
-    def pick(w, t, h):
-        a = R(A(h), 0, 128)
+    def pick(w, t, q):
         if SIGNQ[t] == "S":
-            act(hs("SGN", h), a, AF.Sign)
+            act(qs("SGN", q), A(q, 0), AF.Sign)
         else:
-            ts(hs("SGN", h), a, 1.0, OP.min, -1.0, OP.max)
-        mms(*summ(R(B(h), 0, 128), (full("QF" if t == 0 else "QL"), hs("SGN", h)), (full("I16"), hs("PH" if t == 0 else "FN", h))))
-        ts(hs("RR", h), R(B(h), 0, 128), full("THF" if t == 0 else "THL"), OP.subtract, -2048.0, OP.max)
+            ts(qs("SGN", q), A(q, 0), 1.0, OP.min, -1.0, OP.max)
+        mms(*summ(A(q, 1), (full("QF" if t == 0 else "QL"), qs("SGN", q)), (full("I16"), qs("FN", q))))
+        ts(qs("RR", q), A(q, 1), full("THF" if t == 0 else "THL"), OP.subtract, -2048.0, OP.max)
 
-    def keep(w, t, h):
-        a, m = R(A(h), 0, 128), R(A(h), 128, 256)
+    def keep(w, t, q):
         last = w == WAVES - 1
-        if t == 0:
-            tt(hs("ACC", h), a, hs("CC", h), OP.min)
-            if last:
-                ts(hs("ACC", h), hs("ACC", h), -1.0, OP.max)
-            return
-        tt(m, a, hs("CC", h), OP.min)
-        if t == 1:
-            tt(hs("ACC", h), m, hs("ACC", h), OP.max)
-        else:
-            tt(hs("FIN", h), m, hs("ACC", h), OP.max)
-            ts(hs("FIA", h), hs("FIN", h), 4095, OP.bitwise_and)
-            cp(IND("YF" if last else "E", 0, EW, "IXU%d" % (w % 2), 8 * h, 8 * h + 8), hs("FIA", h))
+        tt(A(q, 2) if t else qs("ACC", q), A(q, 0), qs("CC", q), OP.min)
+        if t == 0 and last:
+            ts(qs("ACC", q), qs("ACC", q), -1.0, OP.max)
+        if t:
+            tt(qs("FIN" if t == 2 else "ACC", q), A(q, 2), qs("ACC", q), OP.max)
 
-    def step(w, t, h):
-        x = R(B(h), 128, 136)
+    def put(w, lo, hi):
+        ts(R("FIA", 64 * lo, 64 * hi), R("FIN", 64 * lo, 64 * hi), 4095, OP.bitwise_and)
+        cp(IND("YF" if w == WAVES - 1 else "E", 0, EW, "IXU%d" % (w % 2), 4 * lo, 4 * hi), R("FIA", 64 * lo, 64 * hi))
+
+    def step(w, t, q):
         bu = "BU%d" % t
-        mms(*summ(x, *[(sel("Z1", c), R("RR", 128 * h + c, 128 * h + 128, 16)) for c in range(16)]))
-        ts(hs(bu, h, 8), x, 32768.0, OP.add)
-        ts(hs("FN", h), IND("NBT", 0, 4097, bu, 8 * h, 8 * h + 8), -2047.0, OP.add)
-        ts(hs("CU", h), hs("FN", h), 2048.0, OP.add)
-
-    def level(w, t, h):
-        act(hs("CC", h), hs("FN", h), bias=2048.0 + 4096.0 * (t + 1) - (1.0 if w == WAVES - 1 else 0.0))
+        if SCAN:
+            mms(*summ(A(q, 3), (full("BO"), qs("RR", q)), (full("I16"), full("NM"))))
+            y, o = A(q, 3), qs("SCN", q)
+            run("V", rds(y, full("RST")), o[1], 64 * CY,
+                [lambda: g.vector.tensor_tensor_scan(o[0], T["RST"][:, 0:64], y[0], 0.0, OP.min, OP.max)])
+            x = R("SCN", 64 * q + 15, 64 * q + 64, 16)
+        else:
+            x = R("A%d" % q, 192, 196)
+            mms(*summ(x, *[(sel("Z1", c), R("RR", 64 * q + c, 64 * q + 64, 16)) for c in range(16)]))
+        ts(hs(bu, q, 4), x, 32768.0, OP.add)
+        ts(qs("CU", q), IND("NBT", 0, 4097, bu, 4 * q, 4 * q + 4), 1.0, OP.add)
 
     def marks(w, h):
         nh = (NS[w] + 1) // 2
         ts(hs("SEL", h), hs("RR", h), -2047.5, OP.is_gt)
-        mms(*turned(B(h), 256, h, True))
-        act(hs("HI", h, FW), R(B(h), 256, 256 + FW), bias=2048.0)
+        bank = "A%d" % (2 * h + 1)
+        mms(*turned(bank, 256, h, True))
+        act(hs("HI", h, FW), R(bank, 256, 256 + FW), bias=2048.0)
         for i in range(nh):
             ts(R("HF%d" % h, FW * i, FW * i + FW), hs("HI", h, FW), 6144.0 + 32.0 * (i - 24), OP.is_equal)
         for gr in range(8):
@@ -601,7 +658,7 @@ def rank_program(g, core, T, topo):
         ts(out, full("K2"), 4095, OP.bitwise_and)
 
     def numbers(w):
-        x = R("B1P", 136, 152)
+        x = R("A3", 192, 208)
         mms(*summ(x, *[(sel("Z1", c), R("RR", c, 256, 16)) for c in range(16)]))
         ts(full("K1"), x, 32768.0, OP.add, 4097.0, OP.mult)
         newer(full("K1"), full("K1"), full("K3"))
@@ -622,24 +679,28 @@ def rank_program(g, core, T, topo):
         for h in range(2):
             seeds(w, 2 * h)
             seeds(w, 2 * h + 1)
-            seeds_end(w, h)
+            level(w, 0, h)
         if not last:
             credit(w + 1)
             low(w, 0)
             low(w, 1)
         for t in range(3):
             for h in range(2):
-                near(w, t, 2 * h)
-                near(w, t, 2 * h + 1)
-                if t == 2:
-                    keep(w, t, h)
-                pick(w, t, h)
-                if t < 2:
-                    step(w, t, h)
-                    keep(w, t, h)
-                    level(w, t, h)
+                for q in (2 * h, 2 * h + 1):
+                    near(w, t, q)
+                    if t == 2:
+                        keep(w, t, q)
+                        for lo, hi in PUTS:
+                            if hi == q + 1:
+                                put(w, lo, hi)
+                    pick(w, t, q)
+                    if t < 2:
+                        step(w, t, q)
+                        keep(w, t, q)
                 if t == 0 and not last:
                     marks(w, h)
+                if t < 2:
+                    level(w, t + 1, h)
             if t == 0:
                 idxs(w)
                 if not last:
@@ -662,6 +723,9 @@ def rank_program(g, core, T, topo):
         g.wait_ge(T.sem["c" + s], cnt[s])
     for x in LOADS:
         g.wait_ge(T.sem["d_" + x], 16)
+    for q in range(4):
+        if nacc[q]:
+            g.wait_ge(T.sem["acc%d" % q], nacc[q])
     ne = len(topo.engines(core, nxt))
     for w in range(WAVES):
         g.wait_ge(T.sem["gArr%d" % w], ne)

@@ -1,4 +1,5 @@
-from concourse.mybir import AluOpType, ActivationFunctionType
+import numpy as np
+from concourse.mybir import AluOpType, AxisListType, ActivationFunctionType
 
 OP = AluOpType
 AF = ActivationFunctionType
@@ -13,34 +14,52 @@ M32 = 402653184.0
 WT = 32768.0
 NOFF = 783.5
 FW = 136
-CY, GC, SC = 0.00092, 1.56, 3.8
-PEC = 0.00052
-LOOK = 0.05
+CY, GC, SC = np.array([0.00095, 0.00112, 0.00087]), np.array([1.5, 2.0, 1.15]), np.array([3.8, 2.5, 5.0])
+PEC = CY / 2
+WAKES = (0.14, 0.1, 0.2)
+WEIGHT = (1.0, 1.2, 1.0)
+LOOK = 0.1
+FIT = 0.05
 REM = 3.5
-WAKE = 0.1
+WAKE = 0.14
 SEEDQ = ("VSVS", "VSVS", "VSVS", "VSVS", "SVSV")
-VPATH = (((0, 1), (1, 1), (2, 1), (2, 3)),) * 4 + (((0, 1), (1, 1), (2, 1), (0, 3), (1, 3), (2, 3)),)
-SIGNQ = "SSS"
-GHOSTQ = "S"
-DPATH = ((),) * 5
-XRUNS = (((1,), (3,)),) * 5
-ACCL = 3.5
+VPATH = (((0, 1), (1, 1), (2, 1), (2, 3)),) * 4 + (((0, 1), (1, 1), (2, 1)),)
+SIGNQ = ("VSS",) * 4 + ("VVV",)
+LEVELQ = ("SSS",) * 4 + ("SVV",)
+PIECES = 1
+VPIECES = 1
+SPIECES = 1
+GHOSTQ = "SV"
+XRV = (8, 8, 8, 8, 4)
+XRS = (8, 8, 8, 8, 8)
+U16Q = "SSVVVV"
+STEPQ = "VVVV"
+LOWQ = "V"
+JUNKV = 6
+SPLIT = True
+NUMS = ((0, 4),)
 SCAN = True
 PUTS = ((0, 2), (2, 3), (3, 4))
-LOWS = (31, 31, 31, 31)
-LEAD = {}
+LOWS = (24, 24, 24, 24)
+LEAD = {k: 2.0 for k in ("RR", "SCN", "BU", "CU", "SGN", "A", "HF", "F6", "SEL", "HI")}
+TAIL = ((),) * 5
 EARLY = 0.0
-NOISE = 1.0
-PASSES = 30
+NOISE = 0.5
+SEED = 1
+SHIFT = 2.0
+SHARE = 0.2
+SPAN = 6.0
+MOVES = 400
+PASSES = 12
 ORDER = []
 
 SIZE = {"float32": 4, "int32": 4, "bfloat16": 2, "float16": 2, "uint16": 2}
 SCRATCH = {}
 for _d, _l in (
-        ("bfloat16", "BT 4112 XA 1536 XR0 4096 XR1 4096 X0 256 X1 256 XN 256 BH 4096 BG0 1024 BG1 1024 IB 128 INB 128 CL 256 HI 272"),
+        ("bfloat16", "BT 4112 XA 1536 XR0 4096 XR1 4096 X0 256 X1 256 BG 4096 IB 128 INB 128 CL 256 HI 272 H1 272"),
         ("int32", "NBT 4104 NBX 1536 NAT 1280 F0 272 FI 272 FA 272 BD 32 IO 16 PI 1 PU 1 PQ 1 FIN 256 FIA 256 "
                   "K1 16 K2 16 K3 16 PINT 1"),
-        ("uint16", "BDU 32 IXU0 16 IXU1 16 SU 16 NAU 256 CU 256 BU0 16 BU1 16 BU2 16 ISU 16"),
+        ("uint16", "BDU 32 IXU0 16 IXU1 16 IXG 16 SU 16 NAU 256 CU 256 BU0 16 BU1 16 BU2 16 ISU 16"),
         ("float16", "SG 4096 DD_ 2048 NR 4096 ISN 272 BO 128 BOB 128 BOK 128 I16 128 TRI 128 QF 128 QL 128 O16 64 SV 512 DG 2048 "
                     "Z0 144 Z1 144 ZU 144 AV 64 W1 64 N1 64 SGN 256 SEL 256 RR 256 NM 64 LM 128 FN 256 DX 256 NF 256 CF 256 OH 256 S16 16 "
                     "H0 272 LO 272 LF0 4352 LF1 4352 HF0 4352 HF1 4352 MS 1024"),
@@ -50,12 +69,12 @@ for _d, _l in (
     _l = _l.split()
     for _i in range(0, len(_l), 2):
         SCRATCH[_l[_i]] = ("sbuf", [128, int(_l[_i + 1])], _d)
-PSUM = ("A0", "A1", "A2", "A3", "D0", "D1", "MKP", "F6")
+PSUM = ("A0", "A1", "A2", "A3", "D0", "D1", "D2", "F6")
 for _n in PSUM:
     SCRATCH[_n] = ("psum", [128, 512], "float32")
 
 LOADS = ("f0", "bd", "naA", "xaA", "xbA", "xbB", "nbA", "nbB", "naB", "xaB", "oF", "oA")
-SEMAPHORES = (["cV", "cS", "cP", "cG", "bArr", "nArr", "bLoc", "nLoc", "crLoc", "acc0", "acc1", "acc2", "acc3"] + ["d_" + x for x in LOADS]
+SEMAPHORES = (["cV", "cS", "cP", "cG", "bArr", "nArr", "bLoc", "nLoc", "crLoc"] + ["d_" + x for x in LOADS]
               + ["gArr%d" % w for w in range(WAVES)] + ["gLoc%d" % w for w in range(WAVES)] + ["cred%d" % w for w in range(1, WAVES)])
 
 
@@ -86,31 +105,33 @@ def rank_program(g, core, T, topo):
 
     def conflicts(q, reads, writes, wr, rd, same_order):
         out = []
-        for (nm, lo, hi) in reads:
-            ps = nm in PSUM
-            out += [(e[3], True) for e in wr.get(nm, ()) if ps or (e[0] < hi and lo < e[1])]
-            if ps:
-                out += [(e[3], e[2] != q) for e in rd.get(nm, ()) if same_order or e[2] != q]
-        for (nm, lo, hi) in writes:
-            ps = nm in PSUM
-            out += [(e[3], e[2] != q or not ps or q != "P") for e in wr.get(nm, []) + rd.get(nm, [])
-                    if (ps or (e[0] < hi and lo < e[1])) and (same_order or e[2] != q or not ps or q != "P")]
+        for acc, olds in ((reads, (wr,)), (writes, (wr, rd))):
+            for (nm, lo, hi) in acc:
+                if nm not in PSUM:
+                    out += [(e[3], True) for d in olds for e in d.get(nm, ()) if e[0] < hi and lo < e[1]]
+                    continue
+                out += [(e[3], True) for d in (wr, rd) for e in d.get(nm, ()) if e[2] != q]
+                if q != "P":
+                    out += [(e[3], True) for d in olds for e in d.get(nm, ()) if e[2] == q and e[0] < hi and lo < e[1]]
+                if same_order:
+                    out += [(e[3], False) for d in (wr, rd) for e in d.get(nm, ()) if e[2] == q]
         return out
 
     def note(q, reads, writes, tok, wr, rd):
-        for (nm, lo, hi) in writes:
+        for (nm, lo, hi) in reads + writes:
             if nm in PSUM:
-                lo, hi = 0, 512
+                wr[nm] = [e for e in wr.get(nm, ()) if e[2] == q]
+                rd[nm] = [e for e in rd.get(nm, ()) if e[2] == q]
+        for (nm, lo, hi) in writes:
             wr[nm] = [e for e in wr.get(nm, ()) if not (lo <= e[0] and e[1] <= hi)] + [(lo, hi, q, tok)]
             rd[nm] = [e for e in rd.get(nm, ()) if not (lo <= e[0] and e[1] <= hi)]
         for (nm, lo, hi) in reads:
-            if nm in PSUM:
-                lo, hi = 0, 512
             rd[nm] = [e for e in rd.get(nm, ()) if not (e[2] == q and lo <= e[0] and e[1] <= hi)] + [(lo, hi, q, tok)]
 
     def op(q, reads, writes, cost, lat, emit, after=()):
         lead = LEAD.get(writes[0][0].rstrip("0123") if writes else "", 0.0)
-        ops.append((q, reads, writes, cost, lat, emit, tuple(after), lead))
+        cost = [float(c) for c in cost + 0.0 * CY]
+        ops.append((q, reads, writes, cost[0], lat, emit, tuple(after), lead, cost))
         return len(ops) - 1
 
     def waits(q, reads, writes, dma=False):
@@ -133,7 +154,9 @@ def rank_program(g, core, T, topo):
 
     def issue():
         m = len(ops)
-        w2, r2 = {}, {}
+        w2, r2, before = {}, {}, {}
+        for j, k in same:
+            before.setdefault(k, []).append(j)
         dep, succ = [], [[] for _ in range(m)]
         for i, o in enumerate(ops if not ORDER else ()):
             d = {}
@@ -141,9 +164,8 @@ def rank_program(g, core, T, topo):
                 d[j] = d.get(j, False) or strong
             for j in o[6]:
                 d[j] = True
-            for j, k in same:
-                if k == i:
-                    d[j] = d.get(j, False)
+            for j in before.get(i, ()):
+                d[j] = d.get(j, False)
             dep.append(d)
             for j in d:
                 succ[j].append(i)
@@ -168,6 +190,10 @@ def rank_program(g, core, T, topo):
             while len(order) < m:
                 t, q = min((max(free[q], min(ready[i] for i in a)), q) for q, a in avail.items() if a)
                 i = max((i for i in avail[q] if ready[i] <= t + LOOK), key=lambda i: (pri[i], -i))
+                if ready[i] > t:
+                    fit = [j for j in avail[q] if max(t, ready[j]) + ops[j][3] <= ready[i] + FIT]
+                    if fit:
+                        i = max(fit, key=lambda i: (pri[i], -i))
                 avail[q].remove(i)
                 end[i] = free[q] = max(t, ready[i]) + ops[i][3]
                 order.append(i)
@@ -182,16 +208,43 @@ def rank_program(g, core, T, topo):
             pri = [0.0] * m
             for i in range(m - 1, -1, -1):
                 pri[i] = ops[i][3] + max([pri[j] + lag for j, lag in fwd[i]] + [0.0]) + early.get(i, 0.0)
-            best, x = None, 1
+            def span(order, k):
+                end, free = [0.0] * m, {}
+                for i in order:
+                    t = free.get(ops[i][0], 0.0)
+                    for j, strong in dep[i].items():
+                        t = max(t, end[j] + (ops[j][4] + WAKES[k] if strong else 0.0))
+                    end[i] = free[ops[i][0]] = t + ops[i][8][k]
+                return max(end)
+
+            best, x = None, SEED
             for k in range(PASSES):
                 order, end = sweep(fwd, pri, 1.0)
-                if best is None or max(end) < best[0]:
-                    best = (max(end), order, end)
-                key = []
+                score = sum(c * span(order, k) for k, c in enumerate(WEIGHT))
+                if best is None or score < best[0]:
+                    best = (score, order, end)
+                key, shift = [], {}
                 for e in best[2]:
                     x = (x * 1103515245 + 12345) % 2147483648
                     key.append(e + (NOISE * x / 2147483648 if k else 0.0))
                 pri = sweep(bwd, key, 0.0)[1]
+            for k in range(MOVES):
+                x = (x * 1103515245 + 12345) % 2147483648
+                t0, shift, pri = (max(best[2]) + SPAN) * x / 2147483648 - SPAN, {}, []
+                for i, o in enumerate(ops):
+                    t = best[2][i] - o[3]
+                    if t0 <= t < t0 + SPAN:
+                        kind = (o[0], o[2][0][0] if o[2] else "")
+                        if kind not in shift:
+                            x = (x * 1103515245 + 12345) % 2147483648
+                            u = x / 2147483648
+                            shift[kind] = SHIFT * (2 * u / SHARE - 1) if u < SHARE else 0.0
+                        t += shift[kind]
+                    pri.append(-t)
+                order, end = sweep(fwd, pri, 0.0)
+                score = sum(c * span(order, k) for k, c in enumerate(WEIGHT))
+                if score <= best[0]:
+                    best = (score, order, end)
             ORDER.extend(best[1])
         for i in ORDER:
             ops[i][5]()
@@ -269,6 +322,12 @@ def rank_program(g, core, T, topo):
         else:
             ts(out, a, c, OP.add)
 
+    def over(q, out, a, c):
+        if q == "S":
+            act(out, a, AF.Sigmoid, bias=-128.0 * c, scale=128.0)
+        else:
+            ts(out, a, c, OP.is_gt)
+
     def mms(*group):
         r, w, c, calls = [], [], 0.0, []
         for (out, lhs, rhs, start, stop) in group:
@@ -307,20 +366,12 @@ def rank_program(g, core, T, topo):
 
     same = []
 
-    nacc = [0] * 4
-
-    def accum(q, out, a):
-        def emit():
-            waits("G", out[1] + a[1], out[1], True)
-            nacc[q] += 16
-            tok = ("acc%d" % q, nacc[q])
-            know[tok] = dict(seen["G"])
-            g.dma_start(out[0], a[0], accum_op=OP.add).then_inc(T.sem[tok[0]], 16)
-            note("dma", a[1], out[1], tok, wr, rd)
-        op("G", out[1] + a[1], out[1], 1.0, ACCL, emit)
-
     def wide(w):
-        return [q for r in XRUNS[w] for q in r]
+        r = []
+        for _, q in sorted(VPATH[w]):
+            if q not in r:
+                r.append(q)
+        return r
 
     def store(q, sem, out_ap, a):
         def emit():
@@ -360,15 +411,16 @@ def rank_program(g, core, T, topo):
     load("Y", "xaA", R("XA", SP, SP + C0), T.xa[:, 0:C0], 6.4)
 
     def ghosts(w):
-        src = IND("E", SP, EW, "BDU", 0, 32)
-        if GHOSTQ == "S":
-            act(full("GS"), src, AF.Relu, bias=-2560.0)
-        else:
-            ts(full("GS"), src, -2560.0, OP.add, 0.0, OP.max)
+        k = 32 // len(GHOSTQ)
+        for i, q in enumerate(GHOSTQ):
+            out, src = hs("GS", i, 16 * k), IND("E", SP, EW, "BDU", k * i, k * i + k)
+            if q == "S":
+                act(out, src, AF.Relu, bias=-2560.0)
+            else:
+                ts(out, src, -2560.0, OP.add, 0.0, OP.max)
         send(nxt, prv, R("E", EW, EALL), full("GS"), "gArr%d" % w, "gLoc%d" % w, "cred%d" % w if w else None, REM + (0 if w else 1))
 
     ms(full("ONES"), 1.0)
-    ms(R("E", 0, SP), 0.0)
     ms(R("E", SP + 272, EW), 0.0)
     ts(full("FI"), full("F0"), 1, OP.add)
     ts(full("FA"), full("FI"), 4095, OP.bitwise_and)
@@ -390,8 +442,6 @@ def rank_program(g, core, T, topo):
     iota(full("IO"), [[-1, 16]], 16, 1)
     iota(full("JT"), [[16, 16]], 0, 0)
     iota(full("JF"), [[1, 256]], 0, 0)
-    iota(R("CELL", 0, SP + C0), [[1, SP + C0]], -SP, 0)
-    iota(R("CELL", SP + C0, EW), [[1, NOWN - C0]], C0, 0)
     aff(full("S1F"), full("ONES"), [[1, 128]], OP.is_equal, -16, -1)
     aff(full("S2F"), full("ONES"), [[1, 128]], OP.is_equal, 16, -1)
     ts(full("IO"), full("IO"), 15, OP.bitwise_and)
@@ -427,6 +477,8 @@ def rank_program(g, core, T, topo):
     ms(full("U1"), -5000.0)
     ms(R("NAT", 0, SP), 0)
     ms(R("XA", 0, SP), -512.0)
+    for lo in range(0, EW, 320):
+        iota(R("CELL", lo, lo + 320), [[1, 320]], lo - SP, 0)
     ts(R("AV", 0, 17), R("F6", 0, 17), 15.5, OP.is_gt)
     ts(R("N1", 0, 17), R("F6", 0, 17), 15.5, OP.is_lt, -64.0, OP.mult)
 
@@ -439,47 +491,70 @@ def rank_program(g, core, T, topo):
             [lambda: g.vector.tensor_tensor_scan(T["CS"][:, 1:1 + ns], T["ONES"][:, 0:ns], T["F6"][:, 128:128 + ns], -2047.0, OP.mult, OP.add)])
         tt(R("U1", 0, ns), R("F6", 64, 64 + ns), R("CS", 0, ns), OP.add)
         for t in range(16):
-            act(R("JUNK", 64 * t, 64 * t + ns), R("CS", 1, 1 + ns), AF.Sign, bias=R("JB", t, t + 1), scale=-1.0, acc=R("SA", t, t + 1))
-        ts(full("SU"), full("SA"), 0.5, OP.mult, 0.5 * ns, OP.add)
-        ts(full("S16"), full("SA"), 8.0, OP.mult, 8.0 * ns + SP - 1536.0, OP.add)
+            junk, cs, sa = R("JUNK", 64 * t, 64 * t + ns), R("CS", 1, 1 + ns), R("SA", t, t + 1)
+            if t < 16 - JUNKV:
+                act(junk, cs, AF.Sign, bias=R("JB", t, t + 1), scale=-1.0, acc=sa)
+            else:
+                ts(junk, cs, R("JB", t, t + 1), OP.is_lt, 0.5, OP.subtract)
+                run("V", junk[1], sa[1], 64 * CY,
+                    [lambda junk=junk, sa=sa: g.vector.tensor_reduce(sa[0], junk[0], axis=AxisListType.X, op=OP.add)])
+        for lo, hi_, f in ((0, 16 - JUNKV, 0.5), (16 - JUNKV, 16, 1.0)):
+            if lo < hi_:
+                ts(R("SU", lo, hi_), R("SA", lo, hi_), f, OP.mult, 0.5 * ns, OP.add)
+        ts(full("S16"), full("SU"), 16.0, OP.mult, SP - 1536.0, OP.add)
         tt(full("OH"), IND("U1", 0, 72, "SU", 0, 16), full("JF"), OP.is_equal)
-        mms(*[(R("F6", 208, 224), sel("ZU", c), R("OH", c, 256, 16), c == 0, False) for c in range(16)],
-            (R("F6", 208, 224), full("I16"), full("S16"), False, True))
-        tt(full("IXF%d" % k), R("F6", 208, 224), full("JT"), OP.max)
+        ix = R("F6", 208, 224)
+        mms(*summ(ix, (full("I16"), full("S16")), *[(sel("ZU", c), R("OH", c, 256, 16)) for c in range(16)]))
+        cp(full("IXG"), ix)
+        tt(full("IXF%d" % k), ix, full("JT"), OP.max)
         cp(full("IXU%d" % k), full("IXF%d" % k))
-        ts(R("W1", 0, ns), R("U1", 0, ns), 255.5, OP.is_gt)
-        ts(full("NF"), IND("NAT", 0, hi, "IXU%d" % k, 0, 16), -NOFF, OP.add)
-        ts(full("NAU"), full("NF"), NOFF, OP.add)
+        over(STEPQ[2], R("W1", 0, ns), R("U1", 0, ns), 255.5)
+        add(U16Q[3], full("NAU"), IND("NAT", 0, hi, "IXG", 0, 16), 0.0)
         early[len(ops) - 1] = EARLY if w else 0.0
-        act(full("X%d" % k), IND("XA", 0, hi, "IXU%d" % k, 0, 16))
-        act(full("XN"), full("X%d" % k), scale=-1.0)
-        i = 0
-        for run_ in XRUNS[w]:
-            m = len(run_)
+        act(full("X%d" % k), IND("XA", 0, hi, "IXG", 0, 16))
+        for i, q in enumerate(wide(w)):
             for p in range(16):
-                out = (R("XR%d" % k, 1024 * i + p, 1024 * (i + m), 16)[0],
-                       [("XR%d" % k, 1024 * j + 64 * p, 1024 * j + 64 * p + 64) for j in range(i, i + m)])
-                aff(out, R("XN", 64 * run_[0], 64 * (run_[0] + m)), [[0, 64 * m]], OP.is_ge, 0, 0)
-            i += m
+                out = (R("XR%d" % k, 1024 * i + p, 1024 * i + 1024, 16)[0], [("XR%d" % k, 1024 * i + 64 * p, 1024 * i + 64 * p + 64)])
+                a = R("X%d" % k, 64 * q, 64 * q + 64)
+                if i == 0 and p < XRV[w]:
+                    cp(out, a)
+                elif i == 0 and p < XRV[w] + XRS[w]:
+                    act(out, a)
+                else:
+                    aff(out, a, [[0, 64]], OP.is_ge, 0, 0)
         if w < WAVES - 1:
-            act(full("CF"), IND("CELL", 0, hi, "IXU%d" % k, 0, 16), bias=-NOFF)
+            ts(full("NF"), full("NAU"), -NOFF, OP.add)
+            act(full("CF"), IND("CELL", 0, hi, "IXG", 0, 16), bias=-NOFF)
 
     def turned(bank, c, h, masked):
         for o, k, nm, st in ((0, 128, "NF", 1), (128, 8, "CF", 16)):
             pairs = [(hs(nm, h), R("I16", 0, 128, st))] + ([(hs("SEL", h), R("BOK", 0, 128, st))] if masked else [])
             yield from summ(R(bank, c + o, c + o + k), *pairs)
 
-    def low(w, h):
-        t = R("F6", 240 + FW * h, 240 + FW * h + FW)
-        mms(*turned("F6", 240 + FW * h, h, False))
-        ts(hs("H0", h, FW), t, M32, OP.add, -M32, OP.add)
-        tt(hs("LO", h, FW), t, hs("H0", h, FW), OP.subtract)
-        for j in range(1, 32):
-            out = R("LF%d" % h, FW * j, FW * j + FW)
-            if j <= LOWS[w]:
-                act(out, hs("LO", h, FW), AF.Sigmoid, bias=-128.0 * (j - 16), scale=128.0)
-            else:
-                ts(out, hs("LO", h, FW), j - 16.0, OP.is_gt)
+    turn = [0, 0]
+
+    def dbank():
+        turn[1] = (turn[1] + 1) % 3
+        return "D%d" % turn[1]
+
+    def low(w):
+        bank = dbank()
+        t = R(bank, 0, 2 * FW)
+        mms(*turned(bank, 0, 0, False), *turned(bank, FW, 1, False))
+        if LOWQ == "S":
+            act(full("H1"), t, bias=6144.0)
+            grp = []
+            for h in range(2):
+                for (out, l, r, _, _), (a, b) in zip(turned(bank, FW * h, h, False), ((0, 128), (128, FW))):
+                    grp += summ(out, (l, r), (full("INB"), R("H1", FW * h + a, FW * h + b)))
+            mms(*grp)
+            act(full("LO"), t, bias=6144.0)
+        else:
+            ts(full("H0"), t, M32, OP.add, -M32, OP.add)
+            tt(full("LO"), t, full("H0"), OP.subtract)
+        for h in range(2):
+            for j in range(1, 32):
+                over("S" if j <= LOWS[w] else "V", R("LF%d" % h, FW * j, FW * j + FW), hs("LO", h, FW), j - 16.0)
 
     front(0)
     for c in range(16):
@@ -525,17 +600,21 @@ def rank_program(g, core, T, topo):
     def qs(nm, q):
         return hs(nm, q, 64)
 
-    turn = [0, 0]
-
     def seeds(w, q):
         o = q * 64
-        add(SEEDQ[w][q], R("SG", o * 16, o * 16 + 1024), IND("E", SP, EALL, "NAU", o, o + 64), -2048.0)
+        k = 64 // SPIECES
+        for c in range(o, o + 64, k):
+            add(SEEDQ[w][q], R("SG", c * 16, (c + k) * 16), IND("E", SP, EALL, "NAU", c, c + k), -2048.0)
         mms(*summ(A(q, 0), *[(R("DG", p * 128, p * 128 + 128), R("SG", o * 16 + p, o * 16 + 1024, 16)) for p in range(16)]))
-        ts(qs("CU", q), A(q, 0), 2048.0, OP.add)
+        add(U16Q[2], qs("CU", q), A(q, 0), 2048.0)
 
     def level(w, t, h):
-        ts(hs("FN", h), hs("CU", h), -2048.0, OP.add)
-        act(hs("CC", h), hs("FN", h), bias=2048.0 + 4096.0 * t - (1.0 if w == WAVES - 1 else 0.0))
+        add(U16Q[4], hs("FN", h), hs("CU", h), -2048.0)
+        c = 4096.0 * t - (1.0 if w == WAVES - 1 else 0.0)
+        if LEVELQ[w][t] == "S":
+            act(hs("CC", h), hs("FN", h), bias=2048.0 + c) if U16Q[4] == "V" else act(hs("CC", h), hs("CU", h), bias=c)
+        else:
+            ts(hs("CC", h), hs("CU", h), c, OP.add)
 
     def near(w, t, q):
         o = q * 64
@@ -544,34 +623,34 @@ def rank_program(g, core, T, topo):
         if (t, q) in VPATH[w]:
             i = wide(w).index(q)
             d = R("DD_", 1024 * (q % 2), 1024 * (q % 2) + 1024)
-            tt(d, src, R("XR%d" % (w % 2), 1024 * i, 1024 * i + 1024), OP.add)
-            ts(R("NR", o * 16, o * 16 + 1024), d, m, OP.add, m, OP.is_equal)
-            rows = [R("NR", o * 16 + p, o * 16 + 1024, 16) for p in range(16)]
-        elif (t, q) in DPATH[w]:
-            i = wide(w).index(q)
-            d = R("BH", 1024 * q, 1024 * q + 1024)
-            act(d, src)
-            accum(q, d, R("XR%d" % (w % 2), 1024 * i, 1024 * i + 1024))
+            k = 64 // VPIECES
+            for c in range(0, 64, k):
+                tt(R("DD_", 1024 * (q % 2) + 16 * c, 1024 * (q % 2) + 16 * (c + k)), IND("BT", 0, 4097, "CU", o + c, o + c + k),
+                   R("XR%d" % (w % 2), 1024 * i + 16 * c, 1024 * i + 16 * (c + k)), OP.subtract)
             ts(R("NR", o * 16, o * 16 + 1024), d, m, OP.add, m, OP.is_equal)
             rows = [R("NR", o * 16 + p, o * 16 + 1024, 16) for p in range(16)]
         else:
-            bg = "BG%d" % turn[0]
-            turn[0] ^= 1
-            act(full(bg), src)
+            k = 64 // PIECES
+            for c in range(o, o + 64, k):
+                act(R("BG", c * 16, (c + k) * 16), IND("BT", 0, 4097, "CU", c, c + k))
             for k in range(2):
-                bank = "D%d" % turn[1]
-                turn[1] ^= 1
+                bank = dbank()
                 grp = []
                 for p in range(8 * k, 8 * k + 8):
-                    grp += summ(R(bank, 64 * (p % 8), 64 * (p % 8) + 64), (full("IB"), R(bg, p, 1024, 16)),
+                    grp += summ(R(bank, 64 * (p % 8), 64 * (p % 8) + 64), (full("IB"), R("BG", o * 16 + p, o * 16 + 1024, 16)),
                                 (full("INB"), R("X%d" % (w % 2), o, o + 64)))
                 mms(*grp)
                 ts(R("NR", o * 16 + 512 * k, o * 16 + 512 * k + 512), R(bank, 0, 512), m, OP.add, m, OP.is_equal)
             rows = [R("NR", o * 16 + 64 * p, o * 16 + 64 * p + 64) for p in range(16)]
-        mms(*summ(A(q, 0), (full("BOB"), full("O16")), *[(sel("Z0", p), rows[p]) for p in range(16)]))
+        count = summ(A(q, 0), (full("BOB"), full("O16")), *[(sel("Z0", p), rows[p]) for p in range(16)])
+        if SPLIT and (t, q) not in VPATH[w]:
+            mms(*count[:9])
+            mms(*count[9:])
+        else:
+            mms(*count)
 
     def pick(w, t, q):
-        if SIGNQ[t] == "S":
+        if SIGNQ[w][t] == "S":
             act(qs("SGN", q), A(q, 0), AF.Sign)
         else:
             ts(qs("SGN", q), A(q, 0), 1.0, OP.min, -1.0, OP.max)
@@ -601,12 +680,12 @@ def rank_program(g, core, T, topo):
         else:
             x = R("A%d" % q, 192, 196)
             mms(*summ(x, *[(sel("Z1", c), R("RR", 64 * q + c, 64 * q + 64, 16)) for c in range(16)]))
-        ts(hs(bu, q, 4), x, 32768.0, OP.add)
-        ts(qs("CU", q), IND("NBT", 0, 4097, bu, 4 * q, 4 * q + 4), 1.0, OP.add)
+        add(U16Q[0], hs(bu, q, 4), x, 32768.0)
+        add(U16Q[1], qs("CU", q), IND("NBT", 0, 4097, bu, 4 * q, 4 * q + 4), 1.0)
 
     def marks(w, h):
         nh = (NS[w] + 1) // 2
-        ts(hs("SEL", h), hs("RR", h), -2047.5, OP.is_gt)
+        over(STEPQ[0], hs("SEL", h), hs("RR", h), -2047.5)
         bank = "A%d" % (2 * h + 1)
         mms(*turned(bank, 256, h, True))
         act(hs("HI", h, FW), R(bank, 256, 256 + FW), bias=2048.0)
@@ -615,19 +694,19 @@ def rank_program(g, core, T, topo):
         for gr in range(8):
             grp = []
             for kind, cols in ((0, range(16 * gr, 16 * gr + 16)), (1, [128 + gr])):
-                c0 = 128 * kind + 64 * h + 32 * (gr % 2)
-                out = R("MKP", c0, c0 + nh, 1, (32 * (gr // 2), 32 * (gr // 2) + 32))
+                c0 = 256 + 128 * kind + 64 * h + 32 * (gr % 2)
+                out = R("F6", c0, c0 + nh, 1, (32 * (gr // 2), 32 * (gr // 2) + 32))
                 grp += summ(out, *[(R("LF%d" % h, c, 32 * FW, FW), R("HF%d" % h, c, nh * FW, FW)) for c in cols])
             mms(*grp)
 
     def flags(w):
         nh = (NS[w] + 1) // 2
         if nh == 32:
-            act(R("MS", 0, 128), R("MKP", 0, 128))
-            act(R("MS", 128, 256), R("MKP", 128, 256), scale=-32.0)
+            act(R("MS", 0, 128), R("F6", 256, 384))
+            act(R("MS", 128, 256), R("F6", 384, 512), scale=-32.0)
         else:
             for k in range(8):
-                act(R("MS", 32 * k, 32 * k + nh), R("MKP", 32 * k, 32 * k + nh), scale=-32.0 if k >= 4 else 1.0)
+                act(R("MS", 32 * k, 32 * k + nh), R("F6", 256 + 32 * k, 256 + 32 * k + nh), scale=-32.0 if k >= 4 else 1.0)
         grp = []
         for a1 in range(2):
             pairs = [(full("I16"), R("W1", a1, 2 * nh, 2)), (full("I16"), R("N1", a1, 2 * nh, 2))]
@@ -636,37 +715,41 @@ def rank_program(g, core, T, topo):
         if nh < 32:
             grp += summ(R("F6", 2 * nh, 64), (full("I16"), R("W1", 2 * nh, 64)), (full("I16"), R("N1", 2 * nh, 64)))
         mms(*grp)
-        ts(full("AV"), R("F6", 0, 64), 0.5, OP.is_gt)
+        over(STEPQ[1], full("AV"), R("F6", 0, 64), 0.5)
         ts(full("N1"), R("F6", 0, 64), -8.0, OP.is_lt, -64.0, OP.mult)
 
     def parity(w):
         act(full("PC"), full("B0"), AF.Sign, bias=-0.5, acc=full("PR"))
-        mms((R("MKP", 256, 257), full("ONES"), full("PR"), True, True))
-        ts(full("PINT"), R("MKP", 256, 257), 0.5, OP.mult, 1024.0, OP.add)
+        mms((R("A0", 256, 257), full("ONES"), full("PR"), True, True))
+        ts(full("PINT"), R("A0", 256, 257), 0.5, OP.mult, 1024.0, OP.add)
         ts(full("PINT"), full("PINT"), 1, OP.bitwise_and)
         ts(R("MC", w + 1, w + 2), full("PINT"), -8.0, OP.mult, MAG + 8.0, OP.add)
 
     def idxs(w):
-        cp(full("B0"), full("BU0"))
-        ts(full("TS"), full("B0"), 0.0, OP.is_equal, 4096.0, OP.mult)
+        add(U16Q[5], full("B0"), full("BU0"), 0.0)
+        if STEPQ[3] == "S":
+            act(full("TS"), full("B0"), AF.Relu, bias=4096.0, scale=-4096.0)
+        else:
+            ts(full("TS"), full("B0"), 0.0, OP.is_equal, 4096.0, OP.mult)
         tt(full("TS"), full("TS"), full("IXF%d" % (w % 2)), OP.max)
         tt(full("TS2"), full("TS"), full("J2"), OP.min)
         cp(full("ISU"), full("TS2"))
 
-    def newer(out, key, old):
-        tt(full("K2"), key, old, OP.max)
-        ts(out, full("K2"), 4095, OP.bitwise_and)
+    def newer(out, key, old, lo, hi):
+        tt(R("K2", lo, hi), R(key, lo, hi), R(old, lo, hi), OP.max)
+        ts(R(out, lo, hi), R("K2", lo, hi), 4095, OP.bitwise_and)
 
-    def numbers(w):
-        x = R("A3", 192, 208)
-        mms(*summ(x, *[(sel("Z1", c), R("RR", c, 256, 16)) for c in range(16)]))
-        ts(full("K1"), x, 32768.0, OP.add, 4097.0, OP.mult)
-        newer(full("K1"), full("K1"), full("K3"))
-        cp(full("BU2"), full("K1"))
-        xs = full("X%d" % (w % 2))
-        tt(full("DX"), IND("BT", 0, 4097, "BU2", 0, 16), xs, OP.subtract)
-        ts(full("CL"), full("DX"), -2.0, OP.max, 2.0, OP.min)
-        tt(IND("XA", 0, 1536, "ISU", 0, 16), full("CL"), xs, OP.add)
+    def numbers(w, lo, hi):
+        a, b = 4 * lo, 4 * hi
+        x = R("A%d" % (hi - 1), 192, 192 + b - a)
+        mms(*summ(x, *[(sel("Z1", c), R("RR", 16 * a + c, 16 * b, 16)) for c in range(16)]))
+        ts(R("K1", a, b), x, 32768.0, OP.add, 4097.0, OP.mult)
+        newer("K1", "K1", "K3", a, b)
+        cp(R("BU2", a, b), R("K1", a, b))
+        xs, dx, cl = R("X%d" % (w % 2), 16 * a, 16 * b), R("DX", 16 * a, 16 * b), R("CL", 16 * a, 16 * b)
+        tt(dx, IND("BT", 0, 4097, "BU2", a, b), xs, OP.subtract)
+        ts(cl, dx, -2.0, OP.max, 2.0, OP.min)
+        tt(IND("XA", 0, 1536, "ISU", a, b), cl, xs, OP.add)
 
     for w in range(WAVES):
         last = w == WAVES - 1
@@ -674,16 +757,21 @@ def rank_program(g, core, T, topo):
             for k in range(2):
                 e, y = R("E", SP + 512 * k, SP + 512 * k + 512), R("YF", SP + 512 * k, SP + 512 * k + 512)
                 act(y, e, bias=-1.0)
-                act(R("D%d" % k, 0, 512), e, bias=4095.0, scale=-5000.0)
-                tt(y, R("D%d" % k, 0, 512), y, OP.max)
+                d = R(dbank(), 0, 512)
+                act(d, e, bias=4095.0, scale=-5000.0)
+                tt(y, d, y, OP.max)
+        a = len(ops)
+        if not last:
+            low(w)
+        b = len(ops)
         for h in range(2):
             seeds(w, 2 * h)
             seeds(w, 2 * h + 1)
             level(w, 0, h)
+        steps = [j for j in range(a, b) if ops[j][2][0][0] in TAIL[w]]
+        same.extend((j, k) for k in range(b, len(ops)) if ops[k][2][0][0] == "SG" for j in steps if ops[j][0] == ops[k][0])
         if not last:
             credit(w + 1)
-            low(w, 0)
-            low(w, 1)
         for t in range(3):
             for h in range(2):
                 for q in (2 * h, 2 * h + 1):
@@ -694,6 +782,10 @@ def rank_program(g, core, T, topo):
                             if hi == q + 1:
                                 put(w, lo, hi)
                     pick(w, t, q)
+                    if t == 2 and last:
+                        for lo, hi in NUMS:
+                            if hi == q + 1:
+                                numbers(w, lo, hi)
                     if t < 2:
                         step(w, t, q)
                         keep(w, t, q)
@@ -704,18 +796,19 @@ def rank_program(g, core, T, topo):
             if t == 0:
                 idxs(w)
                 if not last:
-                    parity(w)
                     flags(w)
                     front(w + 1)
             if t == 1:
+                if not last:
+                    parity(w)
                 ts(full("K1"), full("BU1"), 4097.0, OP.mult)
-                newer(full("K3"), full("K1"), full("B0"))
+                newer("K3", "K1", "B0", 0, 16)
             if t == 2:
                 if not last:
                     ghosts(w + 1)
+                    numbers(w, 0, 4)
                 else:
                     store("Y", "oF", T.yf[:], R("YF", SP, EW))
-                numbers(w)
     store("Y", "oA", T.ya[:], R("XA", SP, EW))
     issue()
 
@@ -723,9 +816,6 @@ def rank_program(g, core, T, topo):
         g.wait_ge(T.sem["c" + s], cnt[s])
     for x in LOADS:
         g.wait_ge(T.sem["d_" + x], 16)
-    for q in range(4):
-        if nacc[q]:
-            g.wait_ge(T.sem["acc%d" % q], nacc[q])
     ne = len(topo.engines(core, nxt))
     for w in range(WAVES):
         g.wait_ge(T.sem["gArr%d" % w], ne)

import numpy as np
from concourse.mybir import AluOpType, AxisListType, ActivationFunctionType

OP = AluOpType
AF = ActivationFunctionType
NOWN, NG, NB_, WAVES, H = 1024, 512, 2560, 5, 1535
SP = 256
EW = SP + NOWN
EALL = EW + NG
NS = (34, 49, 64, 64, 64)
C0 = NS[0] * 16
MAG = 100663296.0
M32 = 402653184.0
WT = 32768.0
NOFF = 783.5
FW = 136
CY, GC, SC = np.array([0.00095, 0.00112, 0.00087]), np.array([1.5, 2.0, 1.15]), np.array([3.8, 2.5, 5.0])
PEC = CY / 2
WAKES = (0.14, 0.1, 0.2)
WEIGHT = (1.0, 1.2, 1.0)
LOOK = 0.1
FIT = 0.05
REM = 3.5
WAKE = 0.14
SEEDQ = ("VSVS", "VSVS", "VSVS", "VSVS", "SVSV")
VPATH = (((0, 1), (1, 1), (2, 1), (2, 3)),) * 4 + (((0, 1), (1, 1), (2, 1)),)
SIGNQ = ("VSS",) * 4 + ("VVV",)
LEVELQ = ("SSS",) * 4 + ("SVV",)
PIECES = 1
VPIECES = 1
SPIECES = 1
GHOSTQ = "SV"
XRV = (8, 8, 8, 8, 4)
XRS = (8, 8, 8, 8, 8)
U16Q = "SSVVVV"
STEPQ = "VVVV"
LOWQ = "V"
JUNKV = 6
SPLIT = True
NUMS = ((0, 4),)
SCAN = True
PUTS = ((0, 2), (2, 3), (3, 4))
LOWS = (24, 24, 24, 24)
LEAD = {k: 2.0 for k in ("RR", "SCN", "BU", "CU", "SGN", "A", "HF", "F6", "SEL", "HI")}
TAIL = ((),) * 5
EARLY = 0.0
NOISE = 0.5
SEED = 1
SHIFT = 2.0
SHARE = 0.2
SPAN = 6.0
MOVES = 400
PASSES = 12
ORDER = []

SIZE = {"float32": 4, "int32": 4, "bfloat16": 2, "float16": 2, "uint16": 2}
SCRATCH = {}
for _d, _l in (
        ("bfloat16", "BT 4112 XA 1536 XR0 4096 XR1 4096 X0 256 X1 256 BG 4096 IB 128 INB 128 CL 256 HI 272 H1 272"),
        ("int32", "NBT 4104 NBX 1536 NAT 1280 F0 272 FI 272 FA 272 BD 32 IO 16 PI 1 PU 1 PQ 1 FIN 256 FIA 256 "
                  "K1 16 K2 16 K3 16 PINT 1"),
        ("uint16", "BDU 32 IXU0 16 IXU1 16 IXG 16 SU 16 NAU 256 CU 256 BU0 16 BU1 16 BU2 16 ISU 16"),
        ("float16", "SG 4096 DD_ 2048 NR 4096 ISN 272 BO 128 BOB 128 BOK 128 I16 128 TRI 128 QF 128 QL 128 O16 64 SV 512 DG 2048 "
                    "Z0 144 Z1 144 ZU 144 AV 64 W1 64 N1 64 SGN 256 SEL 256 RR 256 NM 64 LM 128 FN 256 DX 256 NF 256 CF 256 OH 256 S16 16 "
                    "H0 272 LO 272 LF0 4352 LF1 4352 HF0 4352 HF1 4352 MS 1024"),
        ("float32", "E 1792 YF 1280 GS 512 CELL 1280 JF 256 JT 16 JB 16 J2 16 ONES 128 BOA 128 BOF 128 IF 128 UPF 128 S1F 128 S2F 128 "
                    "TF 128 TG 128 MK 16 PUF 1 PUW 1 PM 1 PN 1 THF 1 THL 1 MC 8 CS 65 U1 72 JUNK 1024 SA 16 IXF0 16 IXF1 16 "
                    "CC 256 ACC 256 SCN 256 RST 64 B0 16 TS 16 TS2 16 PC 16 PR 1")):
    _l = _l.split()
    for _i in range(0, len(_l), 2):
        SCRATCH[_l[_i]] = ("sbuf", [128, int(_l[_i + 1])], _d)
PSUM = ("A0", "A1", "A2", "A3", "D0", "D1", "D2", "F6")
for _n in PSUM:
    SCRATCH[_n] = ("psum", [128, 512], "float32")

LOADS = ("f0", "bd", "naA", "xaA", "xbA", "xbB", "nbA", "nbB", "naB", "xaB", "oF", "oA")
SEMAPHORES = (["cV", "cS", "cP", "cG", "bArr", "nArr", "bLoc", "nLoc", "crLoc"] + ["d_" + x for x in LOADS]
              + ["gArr%d" % w for w in range(WAVES)] + ["gLoc%d" % w for w in range(WAVES)] + ["cred%d" % w for w in range(1, WAVES)])


def rank_program(g, core, T, topo):
    rank = T.rank_of(core)
    if rank is None:
        return
    n = len(T.cores)
    nxt, prv = T.cores[(rank + 1) % n], T.cores[(rank - 1) % n]
    Q = {"V": g.vector, "S": g.scalar, "P": g.tensor, "G": g, "Y": g.sync}
    cnt = {q: 0 for q in "VSPG"}
    seen = {q: {} for q in Q}
    know = {}
    wr, rd = {}, {}
    ops = []
    early = {}
    loads = {}

    def need(q, tok):
        s, v = tok
        if seen[q].get(s, 0) >= v:
            return
        Q[q].wait_ge(T.sem[s], v)
        seen[q][s] = v
        for s2, v2 in know.get(tok, {}).items():
            if seen[q].get(s2, 0) < v2:
                seen[q][s2] = v2

    def conflicts(q, reads, writes, wr, rd, same_order):
        out = []
        for acc, olds in ((reads, (wr,)), (writes, (wr, rd))):
            for (nm, lo, hi) in acc:
                if nm not in PSUM:
                    out += [(e[3], True) for d in olds for e in d.get(nm, ()) if e[0] < hi and lo < e[1]]
                    continue
                out += [(e[3], True) for d in (wr, rd) for e in d.get(nm, ()) if e[2] != q]
                if q != "P":
                    out += [(e[3], True) for d in olds for e in d.get(nm, ()) if e[2] == q and e[0] < hi and lo < e[1]]
                if same_order:
                    out += [(e[3], False) for d in (wr, rd) for e in d.get(nm, ()) if e[2] == q]
        return out

    def note(q, reads, writes, tok, wr, rd):
        for (nm, lo, hi) in reads + writes:
            if nm in PSUM:
                wr[nm] = [e for e in wr.get(nm, ()) if e[2] == q]
                rd[nm] = [e for e in rd.get(nm, ()) if e[2] == q]
        for (nm, lo, hi) in writes:
            wr[nm] = [e for e in wr.get(nm, ()) if not (lo <= e[0] and e[1] <= hi)] + [(lo, hi, q, tok)]
            rd[nm] = [e for e in rd.get(nm, ()) if not (lo <= e[0] and e[1] <= hi)]
        for (nm, lo, hi) in reads:
            rd[nm] = [e for e in rd.get(nm, ()) if not (e[2] == q and lo <= e[0] and e[1] <= hi)] + [(lo, hi, q, tok)]

    def op(q, reads, writes, cost, lat, emit, after=()):
        lead = LEAD.get(writes[0][0].rstrip("0123") if writes else "", 0.0)
        cost = [float(c) for c in cost + 0.0 * CY]
        ops.append((q, reads, writes, cost[0], lat, emit, tuple(after), lead, cost))
        return len(ops) - 1

    def waits(q, reads, writes, dma=False):
        toks = {}
        for tok, _ in conflicts(q, reads, writes, wr, rd, dma):
            toks[tok[0]] = max(toks.get(tok[0], 0), tok[1])
        for s in sorted(toks):
            need(q, (s, toks[s]))

    def run(q, reads, writes, cost, calls):
        def emit():
            waits(q, reads, writes)
            for call in calls:
                cnt[q] += 1
                tok = ("c" + q, cnt[q])
                know[tok] = dict(seen[q])
                call().then_inc(T.sem["c" + q], 1)
            note(q, reads, writes, tok, wr, rd)
        return op(q, reads, writes, cost, 0.06, emit)

    def issue():
        m = len(ops)
        w2, r2, before = {}, {}, {}
        for j, k in same:
            before.setdefault(k, []).append(j)
        dep, succ = [], [[] for _ in range(m)]
        for i, o in enumerate(ops if not ORDER else ()):
            d = {}
            for j, strong in conflicts(o[0], o[1], o[2], w2, r2, True):
                d[j] = d.get(j, False) or strong
            for j in o[6]:
                d[j] = True
            for j in before.get(i, ()):
                d[j] = d.get(j, False)
            dep.append(d)
            for j in d:
                succ[j].append(i)
            note(o[0], o[1], o[2], i, w2, r2)
        fwd = [[(j, ops[i][4] + WAKE if dep[j][i] else 0.0) for j in succ[i]] for i in range(len(dep))]
        bwd = [[(j, (ops[j][4] + WAKE if dep[i][j] else 0.0) + early.get(j, 0.0)) for j in dep[i]] for i in range(len(dep))]

        def sweep(edges, pri, sign):
            pri = [p + sign * o[7] for p, o in zip(pri, ops)]
            left = [0] * m
            for e in edges:
                for j, _ in e:
                    left[j] += 1
            ready, end = [0.0] * m, [0.0] * m
            free, avail = {}, {}
            for i, o in enumerate(ops):
                free.setdefault(o[0], 0.0)
                avail.setdefault(o[0], [])
                if not left[i]:
                    avail[o[0]].append(i)
            order = []
            while len(order) < m:
                t, q = min((max(free[q], min(ready[i] for i in a)), q) for q, a in avail.items() if a)
                i = max((i for i in avail[q] if ready[i] <= t + LOOK), key=lambda i: (pri[i], -i))
                if ready[i] > t:
                    fit = [j for j in avail[q] if max(t, ready[j]) + ops[j][3] <= ready[i] + FIT]
                    if fit:
                        i = max(fit, key=lambda i: (pri[i], -i))
                avail[q].remove(i)
                end[i] = free[q] = max(t, ready[i]) + ops[i][3]
                order.append(i)
                for j, lag in edges[i]:
                    ready[j] = max(ready[j], end[i] + lag)
                    left[j] -= 1
                    if not left[j]:
                        avail[ops[j][0]].append(j)
            return order, end

        if not ORDER:
            pri = [0.0] * m
            for i in range(m - 1, -1, -1):
                pri[i] = ops[i][3] + max([pri[j] + lag for j, lag in fwd[i]] + [0.0]) + early.get(i, 0.0)
            def span(order, k):
                end, free = [0.0] * m, {}
                for i in order:
                    t = free.get(ops[i][0], 0.0)
                    for j, strong in dep[i].items():
                        t = max(t, end[j] + (ops[j][4] + WAKES[k] if strong else 0.0))
                    end[i] = free[ops[i][0]] = t + ops[i][8][k]
                return max(end)

            best, x = None, SEED
            for k in range(PASSES):
                order, end = sweep(fwd, pri, 1.0)
                score = sum(c * span(order, k) for k, c in enumerate(WEIGHT))
                if best is None or score < best[0]:
                    best = (score, order, end)
                key, shift = [], {}
                for e in best[2]:
                    x = (x * 1103515245 + 12345) % 2147483648
                    key.append(e + (NOISE * x / 2147483648 if k else 0.0))
                pri = sweep(bwd, key, 0.0)[1]
            for k in range(MOVES):
                x = (x * 1103515245 + 12345) % 2147483648
                t0, shift, pri = (max(best[2]) + SPAN) * x / 2147483648 - SPAN, {}, []
                for i, o in enumerate(ops):
                    t = best[2][i] - o[3]
                    if t0 <= t < t0 + SPAN:
                        kind = (o[0], o[2][0][0] if o[2] else "")
                        if kind not in shift:
                            x = (x * 1103515245 + 12345) % 2147483648
                            u = x / 2147483648
                            shift[kind] = SHIFT * (2 * u / SHARE - 1) if u < SHARE else 0.0
                        t += shift[kind]
                    pri.append(-t)
                order, end = sweep(fwd, pri, 0.0)
                score = sum(c * span(order, k) for k, c in enumerate(WEIGHT))
                if score <= best[0]:
                    best = (score, order, end)
            ORDER.extend(best[1])
        for i in ORDER:
            ops[i][5]()

    def R(nm, lo, hi, st=1, part=(0, 128)):
        p = slice(part[0], part[1])
        return (T[nm][p, lo:hi:st] if st > 1 else T[nm][p, lo:hi], [(nm, lo, hi)])

    def IND(nm, lo, hi, off, a, b):
        return (T[nm][:, lo:hi].indirect(T[off][:, a:b]), [(nm, lo, hi)], [(off, a, b)])

    def full(nm):
        return R(nm, 0, SCRATCH[nm][1][1])

    def hs(nm, h, k=128):
        return R(nm, k * h, k * h + k)

    def ind(x):
        return len(x) > 2

    def rds(*xs):
        r = []
        for x in xs:
            if isinstance(x, tuple):
                r += x[1] + (x[2] if ind(x) else [])
        return r

    def offs(out):
        return out[2] if ind(out) else []

    def ap(x):
        return x[0] if isinstance(x, tuple) else x

    def two(x):
        return SIZE[SCRATCH[x[1][0][0]][2]] == 2

    def width(x):
        return x[0].shape[1]

    def vcost(out, a, k, m):
        if ind(out):
            return 0.05 + m * SC * CY
        if ind(a):
            return 0.05 + m * GC * CY
        return max(64, m * k) * CY

    def cp(out, a):
        m = width(a) if not ind(a) else width(out)
        run("V", rds(a) + offs(out), out[1], vcost(out, a, 0.5 if two(out) and two(a) else 1.0, m),
            [lambda: g.vector.tensor_copy(out[0], a[0])])

    def tt(out, a, b, f):
        k = 1.0 if a[1][0][0] in PSUM or b[1][0][0] in PSUM else 2.0
        run("V", rds(a, b) + offs(out), out[1], vcost(out, a, k, width(b)), [lambda: g.vector.tensor_tensor(out[0], a[0], b[0], f)])

    def ts(out, a, s1, op0, s2=None, op1=None):
        c = vcost(out, a, 0.5 if two(out) and two(a) else 1.0, width(out))
        if op1 is None:
            run("V", rds(a, s1), out[1], c, [lambda: g.vector.tensor_scalar(out[0], a[0], ap(s1), None, op0)])
        else:
            run("V", rds(a, s1, s2), out[1], c, [lambda: g.vector.tensor_scalar(out[0], a[0], ap(s1), ap(s2), op0, op1)])

    def ms(out, c):
        return run("V", [], out[1], vcost(out, out, 0.5 if two(out) else 1.0, width(out)), [lambda: g.vector.memset(out[0], c)])

    def act(out, a, func=AF.Identity, bias=0.0, scale=1.0, acc=None):
        m = width(out) if ind(a) else width(a)
        kw = {"accum_out": acc[0]} if acc else {}
        run("S", rds(a, bias, scale) + offs(out), out[1] + (acc[1] if acc else []), (0.02 if acc or ind(a) else 0.0) + vcost(out, a, 1.0, m),
            [lambda: g.scalar.activation(out[0], a[0], func, bias=ap(bias), scale=ap(scale), **kw)])

    def add(q, out, a, c):
        if q == "S":
            act(out, a, bias=c)
        else:
            ts(out, a, c, OP.add)

    def over(q, out, a, c):
        if q == "S":
            act(out, a, AF.Sigmoid, bias=-128.0 * c, scale=128.0)
        else:
            ts(out, a, c, OP.is_gt)

    def mms(*group):
        r, w, c, calls = [], [], 0.0, []
        for (out, lhs, rhs, start, stop) in group:
            r += [x for x in rds(lhs, rhs) if x not in r]
            w += [x for x in out[1] if x not in w]
            c += max(min(64, width(lhs)), width(rhs)) * PEC * (1 if two(lhs) else 4)
            calls.append(lambda out=out, lhs=lhs, rhs=rhs, start=start, stop=stop: g.tensor.matmul(out[0], lhs[0], rhs[0], start, stop))
        run("P", r, w, c, calls)

    def summ(out, *pairs):
        return [(out, l, r, i == 0, i == len(pairs) - 1) for i, (l, r) in enumerate(pairs)]

    def aff(out, a, pattern, cmp, base, cm):
        run("G", a[1], out[1], 0.17 + 2 * CY * width(out), [lambda: g.affine_select(out[0], a[0], pattern, cmp, 0.0, base, cm)])

    def iota(out, pattern, base, cm):
        kw = {} if SCRATCH[out[1][0][0]][2] == "int32" else {"allow_small_or_imprecise_dtypes": True}
        run("G", [], out[1], 0.13 + 2 * CY * width(out), [lambda: g.iota(out[0], pattern, base, cm, **kw)])

    def load(q, sem, out, in_ap, lat, fills=(), written=(), sent=()):
        nm, lo, hi = out[1][0]

        def emit():
            waits(q, list(written), list(sent), True)
            if fills:
                waits(q, [], [(nm, 0, hi)], True)
            tok = ("d_" + sem, 16)
            know[tok] = dict(seen[q])
            Q[q].dma_start(out[0], in_ap).then_inc(T.sem["d_" + sem], 16)
            note("dma", [], out[1], tok, wr, rd)
        before = [loads[q]] if q in loads else []
        loads[q] = op(q, list(written), out[1] + list(sent), 0.05, lat, emit, list(fills))
        early[loads[q]] = 0.0
        for j in before:
            same.append((j, loads[q]))

    same = []

    def wide(w):
        r = []
        for _, q in sorted(VPATH[w]):
            if q not in r:
                r.append(q)
        return r

    def store(q, sem, out_ap, a):
        def emit():
            waits(q, a[1], [], True)
            Q[q].dma_start(out_ap, a[0]).then_inc(T.sem["d_" + sem], 16)
        op(q, a[1], [], 0.1, 3.0, emit)

    def send(dst, src, out, a, rsem, lsem, cred=None, lat=REM):
        ne = len(topo.engines(core, dst))
        ad = topo.addr(dst)

        def emit():
            waits("G", a[1], [])
            if cred:
                need("G", (cred, 1))
            g.remote_dma(out_ap=out[0], in_ap=a[0], remote_sem=T.sem[rsem], local_sem=T.sem[lsem], pid=ad[1], routing_id=ad[0],
                         dma_engine_mask=topo.mask(core, dst))
            tok = (lsem, ne)
            know[tok] = dict(seen["G"])
            note("snd", a[1], [], tok, wr, rd)
        i = op("G", a[1], [], 0.5, lat, emit)
        op("R", [], out[1], 0.0, 0.0, lambda: note("rem", [], out[1], (rsem, len(topo.engines(src, core))), wr, rd), [i])

    def credit(w):
        ad = topo.addr(prv)

        def emit():
            waits("G", [], [("E", EW, EALL)])
            g.remote_sem_update(T.sem["cred%d" % w], T.sem["crLoc"], ad[1], ad[0], 1 << topo.engines(core, prv)[0])
        op("G", [], [("E", EW, EALL)], 0.3, 2.0, emit)

    fb, fn = ms(R("BT", 0, 16), 512.0), ms(R("NBT", 0, 8), 4095)
    load("Y", "f0", full("F0"), T.f0[:], 2.5)
    load("S", "bd", full("BD"), T.bd[:], 2.5)
    load("Y", "xbA", R("BT", 1, 1 + H), T.xb[:, 0:H], 4.5, [fb])
    load("Y", "naA", R("NAT", SP, SP + C0), T.nba[:, 0:C0], 5.8)
    load("Y", "xaA", R("XA", SP, SP + C0), T.xa[:, 0:C0], 6.4)

    def ghosts(w):
        k = 32 // len(GHOSTQ)
        for i, q in enumerate(GHOSTQ):
            out, src = hs("GS", i, 16 * k), IND("E", SP, EW, "BDU", k * i, k * i + k)
            if q == "S":
                act(out, src, AF.Relu, bias=-2560.0)
            else:
                ts(out, src, -2560.0, OP.add, 0.0, OP.max)
        send(nxt, prv, R("E", EW, EALL), full("GS"), "gArr%d" % w, "gLoc%d" % w, "cred%d" % w if w else None, REM + (0 if w else 1))

    ms(full("ONES"), 1.0)
    ms(R("E", SP + 272, EW), 0.0)
    ts(full("FI"), full("F0"), 1, OP.add)
    ts(full("FA"), full("FI"), 4095, OP.bitwise_and)
    cp(R("E", SP, SP + 272), full("FA"))
    cp(full("BDU"), full("BD"))
    ts(full("ISN"), full("F0"), 4095, OP.is_equal)
    ghosts(0)
    send(prv, nxt, R("BT", 2561, 4096), R("BT", 1, 1 + H), "bArr", "bLoc", None, REM + 1)
    load("Y", "xbB", R("BT", 1 + H, 1 + NB_), T.xb[:, H:NB_], 3.1, written=full("GS")[1])
    load("Y", "nbA", R("NBT", 1, 1 + H), T.nbb[:, 0:H], 5.8, [fn], sent=full("GS")[1])
    load("Y", "nbB", R("NBT", 1 + H, 1 + NB_), T.nbb[:, H:NB_], 8.5)
    load("Y", "naB", R("NAT", SP + C0, EW), T.nba[:, C0:NOWN], 6.0, written=R("NBT", 1 + H, 1 + NB_)[1])
    load("Y", "xaB", R("XA", SP + C0, EW), T.xa[:, C0:NOWN], 6.5)
    iota(full("PI"), [[0, 1]], 0, 1)
    aff(full("BOA"), full("ONES"), [[-16, 8], [0, 16]], OP.is_ge, 0, 1)
    aff(full("BOF"), full("BOA"), [[16, 8], [0, 16]], OP.is_ge, 15, -1)
    aff(full("IF"), full("ONES"), [[-1, 128]], OP.is_equal, 0, 1)
    aff(full("UPF"), full("BOF"), [[1, 128]], OP.is_gt, 0, -1)
    iota(full("IO"), [[-1, 16]], 16, 1)
    iota(full("JT"), [[16, 16]], 0, 0)
    iota(full("JF"), [[1, 256]], 0, 0)
    aff(full("S1F"), full("ONES"), [[1, 128]], OP.is_equal, -16, -1)
    aff(full("S2F"), full("ONES"), [[1, 128]], OP.is_equal, 16, -1)
    ts(full("IO"), full("IO"), 15, OP.bitwise_and)
    ts(full("PU"), full("PI"), 15, OP.bitwise_and)
    ts(full("PQ"), full("PI"), 16, OP.bitwise_and)
    cp(full("PUF"), full("PU"))
    ts(full("MK"), full("IO"), 0, OP.is_equal)
    ts(full("PM"), full("PQ"), 0, OP.is_gt)
    ts(full("PN"), full("PM"), -1.0, OP.mult, 1.0, OP.add)
    ts(full("PUW"), full("PUF"), 1536.0, OP.add)
    ts(full("THF"), full("PUF"), 2048.0, OP.mult, 2048.0, OP.add)
    ts(full("THL"), full("PUF"), -2048.0, OP.mult, 32768.0, OP.add)
    ts(full("JT"), full("JT"), full("PUF"), OP.add)
    ts(full("JB"), full("JT"), 0.5 - 2047.0, OP.add)
    ts(full("J2"), full("JT"), float(EW), OP.add)
    bo8 = (T["BOF"][:, 0:128:16], [("BOF", 0, 128)])
    for z, v in (("Z1", 1.0), ("Z0", WT), ("ZU", full("PUW"))):
        ms(full(z), 0.0)
        ts((T[z][:, 15:143:16], [(z, 0, 144)]), bo8, v, OP.mult)

    def sel(z, p):
        return R(z, 15 - p, 143 - p)

    mms(*summ(R("F6", 0, 17), *[(sel("Z1", c), R("ISN", c, 272, 16)) for c in range(16)]))
    act(full("BO"), full("BOF"))
    act(full("I16"), full("IF"))
    ts(full("TF"), full("IF"), 2047.0, OP.mult)
    tt(full("TRI"), full("TF"), full("UPF"), OP.add)
    ms(R("CS", 0, 1), -2047.0)
    ms(full("AV"), 1.0)
    ms(full("N1"), 0.0)
    ms(full("W1"), 1.0)
    ms(full("U1"), -5000.0)
    ms(R("NAT", 0, SP), 0)
    ms(R("XA", 0, SP), -512.0)
    for lo in range(0, EW, 320):
        iota(R("CELL", lo, lo + 320), [[1, 320]], lo - SP, 0)
    ts(R("AV", 0, 17), R("F6", 0, 17), 15.5, OP.is_gt)
    ts(R("N1", 0, 17), R("F6", 0, 17), 15.5, OP.is_lt, -64.0, OP.mult)

    def front(w):
        ns, k = NS[w], w % 2
        hi = SP + 16 * ns
        mms((R("F6", 64, 64 + ns), full("TRI"), R("AV", 0, ns), True, True),
            (R("F6", 128, 128 + ns), full("BO"), R("AV", 0, ns), True, True))
        run("V", rds(R("ONES", 0, ns), R("F6", 128, 128 + ns)), [("CS", 1, 1 + ns)], 64 * CY,
            [lambda: g.vector.tensor_tensor_scan(T["CS"][:, 1:1 + ns], T["ONES"][:, 0:ns], T["F6"][:, 128:128 + ns], -2047.0, OP.mult, OP.add)])
        tt(R("U1", 0, ns), R("F6", 64, 64 + ns), R("CS", 0, ns), OP.add)
        for t in range(16):
            junk, cs, sa = R("JUNK", 64 * t, 64 * t + ns), R("CS", 1, 1 + ns), R("SA", t, t + 1)
            if t < 16 - JUNKV:
                act(junk, cs, AF.Sign, bias=R("JB", t, t + 1), scale=-1.0, acc=sa)
            else:
                ts(junk, cs, R("JB", t, t + 1), OP.is_lt, 0.5, OP.subtract)
                run("V", junk[1], sa[1], 64 * CY,
                    [lambda junk=junk, sa=sa: g.vector.tensor_reduce(sa[0], junk[0], axis=AxisListType.X, op=OP.add)])
        for lo, hi_, f in ((0, 16 - JUNKV, 0.5), (16 - JUNKV, 16, 1.0)):
            if lo < hi_:
                ts(R("SU", lo, hi_), R("SA", lo, hi_), f, OP.mult, 0.5 * ns, OP.add)
        ts(full("S16"), full("SU"), 16.0, OP.mult, SP - 1536.0, OP.add)
        tt(full("OH"), IND("U1", 0, 72, "SU", 0, 16), full("JF"), OP.is_equal)
        ix = R("F6", 208, 224)
        mms(*summ(ix, (full("I16"), full("S16")), *[(sel("ZU", c), R("OH", c, 256, 16)) for c in range(16)]))
        cp(full("IXG"), ix)
        tt(full("IXF%d" % k), ix, full("JT"), OP.max)
        cp(full("IXU%d" % k), full("IXF%d" % k))
        over(STEPQ[2], R("W1", 0, ns), R("U1", 0, ns), 255.5)
        add(U16Q[3], full("NAU"), IND("NAT", 0, hi, "IXG", 0, 16), 0.0)
        early[len(ops) - 1] = EARLY if w else 0.0
        act(full("X%d" % k), IND("XA", 0, hi, "IXG", 0, 16))
        for i, q in enumerate(wide(w)):
            for p in range(16):
                out = (R("XR%d" % k, 1024 * i + p, 1024 * i + 1024, 16)[0], [("XR%d" % k, 1024 * i + 64 * p, 1024 * i + 64 * p + 64)])
                a = R("X%d" % k, 64 * q, 64 * q + 64)
                if i == 0 and p < XRV[w]:
                    cp(out, a)
                elif i == 0 and p < XRV[w] + XRS[w]:
                    act(out, a)
                else:
                    aff(out, a, [[0, 64]], OP.is_ge, 0, 0)
        if w < WAVES - 1:
            ts(full("NF"), full("NAU"), -NOFF, OP.add)
            act(full("CF"), IND("CELL", 0, hi, "IXG", 0, 16), bias=-NOFF)

    def turned(bank, c, h, masked):
        for o, k, nm, st in ((0, 128, "NF", 1), (128, 8, "CF", 16)):
            pairs = [(hs(nm, h), R("I16", 0, 128, st))] + ([(hs("SEL", h), R("BOK", 0, 128, st))] if masked else [])
            yield from summ(R(bank, c + o, c + o + k), *pairs)

    turn = [0, 0]

    def dbank():
        turn[1] = (turn[1] + 1) % 3
        return "D%d" % turn[1]

    def low(w):
        bank = dbank()
        t = R(bank, 0, 2 * FW)
        mms(*turned(bank, 0, 0, False), *turned(bank, FW, 1, False))
        if LOWQ == "S":
            act(full("H1"), t, bias=6144.0)
            grp = []
            for h in range(2):
                for (out, l, r, _, _), (a, b) in zip(turned(bank, FW * h, h, False), ((0, 128), (128, FW))):
                    grp += summ(out, (l, r), (full("INB"), R("H1", FW * h + a, FW * h + b)))
            mms(*grp)
            act(full("LO"), t, bias=6144.0)
        else:
            ts(full("H0"), t, M32, OP.add, -M32, OP.add)
            tt(full("LO"), t, full("H0"), OP.subtract)
        for h in range(2):
            for j in range(1, 32):
                over("S" if j <= LOWS[w] else "V", R("LF%d" % h, FW * j, FW * j + FW), hs("LO", h, FW), j - 16.0)

    front(0)
    for c in range(16):
        if c % 2:
            ts(R("DG", c * 128, c * 128 + 128), full("I16"), R("MK", c, c + 1), OP.mult)
        else:
            act(R("DG", c * 128, c * 128 + 128), full("IF"), scale=R("MK", c, c + 1))
    ms(full("MC"), MAG + 8.0)
    ms(R("BT", 4096, 4112), 512.0)
    ms(R("NBT", 4096, 4104), 4095)
    act(full("BOB"), full("BOF"), scale=-12.5 * WT / 16)
    act(full("BOK"), full("BOF"), scale=4096.0)
    ms(full("O16"), 1.0)
    ms(full("RST"), 60000.0)
    ms(R("RST", 0, 64, 16), -60000.0)
    for k in range(4):
        ts(hs("NM", k, 16), full("MK"), 32768.0, OP.mult, -32768.0, OP.add)
    tt(full("TG"), full("IF"), full("UPF"), OP.subtract)
    act(full("QF"), full("TG"), scale=2048.0)
    tt(full("TF"), full("UPF"), full("BOF"), OP.subtract)
    tt(full("TF"), full("TF"), full("IF"), OP.add)
    tt(full("TF"), full("TF"), full("IF"), OP.add)
    act(full("QL"), full("TF"), scale=2048.0)
    ts(R("NBX", 0, H), R("NBT", 1, 1 + H), 1535, OP.min, 2560, OP.add)
    send(prv, nxt, R("NBT", 2561, 4096), R("NBX", 0, H), "nArr", "nLoc", None, REM + 1.5)
    act(R("SV", 0, 128), full("IF"), scale=full("PN"))
    act(R("SV", 128, 256), full("S2F"), scale=full("PM"))
    act(R("SV", 256, 384), full("S1F"), scale=full("PN"))
    act(R("SV", 384, 512), full("IF"), scale=full("PM"))
    aff(full("BOA"), full("ONES"), [[0, 4], [1, 32]], OP.not_equal, 0, 0)
    aff(full("BOA"), full("BOA"), [[1, 128]], OP.is_equal, -1, -1)
    tt(full("LM"), full("IF"), full("BOA"), OP.subtract)
    mms((R("D0", 0, 512), full("LM"), full("SV"), True, True))
    act(full("SV"), R("D0", 0, 512))
    for h in range(2):
        ms(R("LF%d" % h, 0, FW), 1.0)
    act(full("IB"), full("IF"))
    act(full("INB"), full("IF"), scale=-1.0)

    def A(q, k):
        return R("A%d" % q, 64 * k, 64 * k + 64)

    def qs(nm, q):
        return hs(nm, q, 64)

    def seeds(w, q):
        o = q * 64
        k = 64 // SPIECES
        for c in range(o, o + 64, k):
            add(SEEDQ[w][q], R("SG", c * 16, (c + k) * 16), IND("E", SP, EALL, "NAU", c, c + k), -2048.0)
        mms(*summ(A(q, 0), *[(R("DG", p * 128, p * 128 + 128), R("SG", o * 16 + p, o * 16 + 1024, 16)) for p in range(16)]))
        add(U16Q[2], qs("CU", q), A(q, 0), 2048.0)

    def level(w, t, h):
        add(U16Q[4], hs("FN", h), hs("CU", h), -2048.0)
        c = 4096.0 * t - (1.0 if w == WAVES - 1 else 0.0)
        if LEVELQ[w][t] == "S":
            act(hs("CC", h), hs("FN", h), bias=2048.0 + c) if U16Q[4] == "V" else act(hs("CC", h), hs("CU", h), bias=c)
        else:
            ts(hs("CC", h), hs("CU", h), c, OP.add)

    def near(w, t, q):
        o = q * 64
        m = R("MC", w, w + 1)
        src = IND("BT", 0, 4097, "CU", o, o + 64)
        if (t, q) in VPATH[w]:
            i = wide(w).index(q)
            d = R("DD_", 1024 * (q % 2), 1024 * (q % 2) + 1024)
            k = 64 // VPIECES
            for c in range(0, 64, k):
                tt(R("DD_", 1024 * (q % 2) + 16 * c, 1024 * (q % 2) + 16 * (c + k)), IND("BT", 0, 4097, "CU", o + c, o + c + k),
                   R("XR%d" % (w % 2), 1024 * i + 16 * c, 1024 * i + 16 * (c + k)), OP.subtract)
            ts(R("NR", o * 16, o * 16 + 1024), d, m, OP.add, m, OP.is_equal)
            rows = [R("NR", o * 16 + p, o * 16 + 1024, 16) for p in range(16)]
        else:
            k = 64 // PIECES
            for c in range(o, o + 64, k):
                act(R("BG", c * 16, (c + k) * 16), IND("BT", 0, 4097, "CU", c, c + k))
            for k in range(2):
                bank = dbank()
                grp = []
                for p in range(8 * k, 8 * k + 8):
                    grp += summ(R(bank, 64 * (p % 8), 64 * (p % 8) + 64), (full("IB"), R("BG", o * 16 + p, o * 16 + 1024, 16)),
                                (full("INB"), R("X%d" % (w % 2), o, o + 64)))
                mms(*grp)
                ts(R("NR", o * 16 + 512 * k, o * 16 + 512 * k + 512), R(bank, 0, 512), m, OP.add, m, OP.is_equal)
            rows = [R("NR", o * 16 + 64 * p, o * 16 + 64 * p + 64) for p in range(16)]
        count = summ(A(q, 0), (full("BOB"), full("O16")), *[(sel("Z0", p), rows[p]) for p in range(16)])
        if SPLIT and (t, q) not in VPATH[w]:
            mms(*count[:9])
            mms(*count[9:])
        else:
            mms(*count)

    def pick(w, t, q):
        if SIGNQ[w][t] == "S":
            act(qs("SGN", q), A(q, 0), AF.Sign)
        else:
            ts(qs("SGN", q), A(q, 0), 1.0, OP.min, -1.0, OP.max)
        mms(*summ(A(q, 1), (full("QF" if t == 0 else "QL"), qs("SGN", q)), (full("I16"), qs("FN", q))))
        ts(qs("RR", q), A(q, 1), full("THF" if t == 0 else "THL"), OP.subtract, -2048.0, OP.max)

    def keep(w, t, q):
        last = w == WAVES - 1
        tt(A(q, 2) if t else qs("ACC", q), A(q, 0), qs("CC", q), OP.min)
        if t == 0 and last:
            ts(qs("ACC", q), qs("ACC", q), -1.0, OP.max)
        if t:
            tt(qs("FIN" if t == 2 else "ACC", q), A(q, 2), qs("ACC", q), OP.max)

    def put(w, lo, hi):
        ts(R("FIA", 64 * lo, 64 * hi), R("FIN", 64 * lo, 64 * hi), 4095, OP.bitwise_and)
        cp(IND("YF" if w == WAVES - 1 else "E", 0, EW, "IXU%d" % (w % 2), 4 * lo, 4 * hi), R("FIA", 64 * lo, 64 * hi))

    def step(w, t, q):
        bu = "BU%d" % t
        if SCAN:
            mms(*summ(A(q, 3), (full("BO"), qs("RR", q)), (full("I16"), full("NM"))))
            y, o = A(q, 3), qs("SCN", q)
            run("V", rds(y, full("RST")), o[1], 64 * CY,
                [lambda: g.vector.tensor_tensor_scan(o[0], T["RST"][:, 0:64], y[0], 0.0, OP.min, OP.max)])
            x = R("SCN", 64 * q + 15, 64 * q + 64, 16)
        else:
            x = R("A%d" % q, 192, 196)
            mms(*summ(x, *[(sel("Z1", c), R("RR", 64 * q + c, 64 * q + 64, 16)) for c in range(16)]))
        add(U16Q[0], hs(bu, q, 4), x, 32768.0)
        add(U16Q[1], qs("CU", q), IND("NBT", 0, 4097, bu, 4 * q, 4 * q + 4), 1.0)

    def marks(w, h):
        nh = (NS[w] + 1) // 2
        over(STEPQ[0], hs("SEL", h), hs("RR", h), -2047.5)
        bank = "A%d" % (2 * h + 1)
        mms(*turned(bank, 256, h, True))
        act(hs("HI", h, FW), R(bank, 256, 256 + FW), bias=2048.0)
        for i in range(nh):
            ts(R("HF%d" % h, FW * i, FW * i + FW), hs("HI", h, FW), 6144.0 + 32.0 * (i - 24), OP.is_equal)
        for gr in range(8):
            grp = []
            for kind, cols in ((0, range(16 * gr, 16 * gr + 16)), (1, [128 + gr])):
                c0 = 256 + 128 * kind + 64 * h + 32 * (gr % 2)
                out = R("F6", c0, c0 + nh, 1, (32 * (gr // 2), 32 * (gr // 2) + 32))
                grp += summ(out, *[(R("LF%d" % h, c, 32 * FW, FW), R("HF%d" % h, c, nh * FW, FW)) for c in cols])
            mms(*grp)

    def flags(w):
        nh = (NS[w] + 1) // 2
        if nh == 32:
            act(R("MS", 0, 128), R("F6", 256, 384))
            act(R("MS", 128, 256), R("F6", 384, 512), scale=-32.0)
        else:
            for k in range(8):
                act(R("MS", 32 * k, 32 * k + nh), R("F6", 256 + 32 * k, 256 + 32 * k + nh), scale=-32.0 if k >= 4 else 1.0)
        grp = []
        for a1 in range(2):
            pairs = [(full("I16"), R("W1", a1, 2 * nh, 2)), (full("I16"), R("N1", a1, 2 * nh, 2))]
            pairs += [(hs("SV", 2 * (k % 2) + a1), R("MS", 32 * k, 32 * k + nh)) for k in range(8)]
            grp += summ(R("F6", a1, 2 * nh, 2), *pairs)
        if nh < 32:
            grp += summ(R("F6", 2 * nh, 64), (full("I16"), R("W1", 2 * nh, 64)), (full("I16"), R("N1", 2 * nh, 64)))
        mms(*grp)
        over(STEPQ[1], full("AV"), R("F6", 0, 64), 0.5)
        ts(full("N1"), R("F6", 0, 64), -8.0, OP.is_lt, -64.0, OP.mult)

    def parity(w):
        act(full("PC"), full("B0"), AF.Sign, bias=-0.5, acc=full("PR"))
        mms((R("A0", 256, 257), full("ONES"), full("PR"), True, True))
        ts(full("PINT"), R("A0", 256, 257), 0.5, OP.mult, 1024.0, OP.add)
        ts(full("PINT"), full("PINT"), 1, OP.bitwise_and)
        ts(R("MC", w + 1, w + 2), full("PINT"), -8.0, OP.mult, MAG + 8.0, OP.add)

    def idxs(w):
        add(U16Q[5], full("B0"), full("BU0"), 0.0)
        if STEPQ[3] == "S":
            act(full("TS"), full("B0"), AF.Relu, bias=4096.0, scale=-4096.0)
        else:
            ts(full("TS"), full("B0"), 0.0, OP.is_equal, 4096.0, OP.mult)
        tt(full("TS"), full("TS"), full("IXF%d" % (w % 2)), OP.max)
        tt(full("TS2"), full("TS"), full("J2"), OP.min)
        cp(full("ISU"), full("TS2"))

    def newer(out, key, old, lo, hi):
        tt(R("K2", lo, hi), R(key, lo, hi), R(old, lo, hi), OP.max)
        ts(R(out, lo, hi), R("K2", lo, hi), 4095, OP.bitwise_and)

    def numbers(w, lo, hi):
        a, b = 4 * lo, 4 * hi
        x = R("A%d" % (hi - 1), 192, 192 + b - a)
        mms(*summ(x, *[(sel("Z1", c), R("RR", 16 * a + c, 16 * b, 16)) for c in range(16)]))
        ts(R("K1", a, b), x, 32768.0, OP.add, 4097.0, OP.mult)
        newer("K1", "K1", "K3", a, b)
        cp(R("BU2", a, b), R("K1", a, b))
        xs, dx, cl = R("X%d" % (w % 2), 16 * a, 16 * b), R("DX", 16 * a, 16 * b), R("CL", 16 * a, 16 * b)
        tt(dx, IND("BT", 0, 4097, "BU2", a, b), xs, OP.subtract)
        ts(cl, dx, -2.0, OP.max, 2.0, OP.min)
        tt(IND("XA", 0, 1536, "ISU", a, b), cl, xs, OP.add)

    for w in range(WAVES):
        last = w == WAVES - 1
        if last:
            for k in range(2):
                e, y = R("E", SP + 512 * k, SP + 512 * k + 512), R("YF", SP + 512 * k, SP + 512 * k + 512)
                act(y, e, bias=-1.0)
                d = R(dbank(), 0, 512)
                act(d, e, bias=4095.0, scale=-5000.0)
                tt(y, d, y, OP.max)
        a = len(ops)
        if not last:
            low(w)
        b = len(ops)
        for h in range(2):
            seeds(w, 2 * h)
            seeds(w, 2 * h + 1)
            level(w, 0, h)
        steps = [j for j in range(a, b) if ops[j][2][0][0] in TAIL[w]]
        same.extend((j, k) for k in range(b, len(ops)) if ops[k][2][0][0] == "SG" for j in steps if ops[j][0] == ops[k][0])
        if not last:
            credit(w + 1)
        for t in range(3):
            for h in range(2):
                for q in (2 * h, 2 * h + 1):
                    near(w, t, q)
                    if t == 2:
                        keep(w, t, q)
                        for lo, hi in PUTS:
                            if hi == q + 1:
                                put(w, lo, hi)
                    pick(w, t, q)
                    if t == 2 and last:
                        for lo, hi in NUMS:
                            if hi == q + 1:
                                numbers(w, lo, hi)
                    if t < 2:
                        step(w, t, q)
                        keep(w, t, q)
                if t == 0 and not last:
                    marks(w, h)
                if t < 2:
                    level(w, t + 1, h)
            if t == 0:
                idxs(w)
                if not last:
                    flags(w)
                    front(w + 1)
            if t == 1:
                if not last:
                    parity(w)
                ts(full("K1"), full("BU1"), 4097.0, OP.mult)
                newer("K3", "K1", "B0", 0, 16)
            if t == 2:
                if not last:
                    ghosts(w + 1)
                    numbers(w, 0, 4)
                else:
                    store("Y", "oF", T.yf[:], R("YF", SP, EW))
    store("Y", "oA", T.ya[:], R("XA", SP, EW))
    issue()

    for s in "VSPG":
        g.wait_ge(T.sem["c" + s], cnt[s])
    for x in LOADS:
        g.wait_ge(T.sem["d_" + x], 16)
    ne = len(topo.engines(core, nxt))
    for w in range(WAVES):
        g.wait_ge(T.sem["gArr%d" % w], ne)
        g.wait_ge(T.sem["gLoc%d" % w], ne)
    for s in ("bArr", "nArr", "bLoc", "nLoc"):
        g.wait_ge(T.sem[s], len(topo.engines(core, prv)))
    g.wait_ge(T.sem["crLoc"], WAVES - 1)
